import numpy as np
import ml_dtypes


def mxq(x, axis, fmt="e4m3"):
    dtype, down = {"e4m3": (ml_dtypes.float8_e4m3fn, 7), "e5m2": (ml_dtypes.float8_e5m2, 14)}[fmt]
    v = np.moveaxis(np.asarray(x, np.float32).astype(ml_dtypes.bfloat16).astype(np.float64), axis, -1)
    blocks = v.reshape(v.shape[:-1] + (-1, 32))
    amax = np.abs(blocks).max(-1, keepdims=True)
    byte = np.maximum(np.where(amax > 0, np.frexp(amax)[1] - 1 + 127, 0) - down, 1)
    scale = np.exp2(byte - 127.0)
    codes = (blocks / scale).astype(np.float32).astype(dtype).astype(np.float64)
    return np.moveaxis((codes * scale).reshape(v.shape), -1, axis)


WIDE = False


def mx_kscale(k):
    if not WIDE:
        return np.ones(k)
    levels = np.array([10, -10, 5, -5, 0])
    if k % 512:
        return np.exp2(np.random.permutation(np.resize(levels, k // 32))).repeat(32)
    a = np.empty((k // 512, 16))
    for p in range(k // 512):
        a[p, :8] = np.random.permutation(np.resize(levels, 8))
        for g in range(8):
            far = levels[np.abs(levels - a[p, g]) >= 10]
            a[p, g + 8] = far[np.random.randint(len(far))]
    return np.exp2(a.ravel()).repeat(32)


def f64(x):
    return np.asarray(x).astype(np.float64)


def striped8(idx):
    return np.concatenate([x.reshape(-1, 16).T for x in idx]).astype(np.uint16)


def runs(offs, k):
    lists = np.stack([offs[16 * r : 16 * r + 16].T.reshape(-1) for r in range(8)]).astype(np.int64)
    return lists[np.arange(k) % 512 // 64]


def pack_weight(w):
    k, n = w.shape
    w = f64(np.asarray(w, np.float32).astype(ml_dtypes.bfloat16)).reshape(k // 32, 32, n)
    amax = np.abs(w).max(1)
    byte = np.clip(np.where(amax > 0, np.frexp(amax)[1] - 1 + 127 - 7, 1), 1, 254)
    scaled = (w * np.exp2(127.0 - byte)[:, None, :]).reshape(k, n).astype(np.float32)
    words = np.ascontiguousarray(scaled.reshape(k // 512, 128, 4, n).transpose(0, 1, 3, 2)).astype(ml_dtypes.float8_e4m3fn).view(np.uint8)
    return words, np.ascontiguousarray(byte.astype(np.uint8).reshape(k // 512, 16, n))


def unpack_weight(words, scales):
    g, p, n, _ = words.shape
    vals = np.ascontiguousarray(words).view(ml_dtypes.float8_e4m3fn).astype(np.float64) * np.repeat(np.exp2(scales.astype(np.float64) - 127.0), 8, axis=1)[..., None]
    return vals.transpose(0, 1, 3, 2).reshape(g * 512, n)


E2M1 = np.array([0.0, 0.5, 1.0, 1.5, 2.0, 3.0, 4.0, 6.0, -0.0, -0.5, -1.0, -1.5, -2.0, -3.0, -4.0, -6.0])


def pack_fp4(w):
    k, n = w.shape
    w = f64(np.asarray(w, np.float32).astype(ml_dtypes.bfloat16)).reshape(k // 32, 32, n)
    amax = np.abs(w).max(1)
    mant, ex = np.frexp(amax / 6.0)
    byte = np.clip(np.where(amax > 0, np.where(mant > 0.5, ex, ex - 1) + 127, 1), 1, 254)
    scaled = (w * np.exp2(127.0 - byte)[:, None, :]).reshape(k, n).astype(np.float32)
    c = np.ascontiguousarray(scaled.reshape(k // 512, 128, 4, n).transpose(0, 1, 3, 2)).astype(ml_dtypes.float4_e2m1fn).view(np.uint8) & 0xF
    words = (c[..., 0::2] | (c[..., 1::2] << 4)).reshape(k // 512, 128, 2 * n)
    return np.ascontiguousarray(words), np.ascontiguousarray(byte.astype(np.uint8).reshape(k // 512, 16, n))


def unpack_fp4(words, scales):
    g, _, n = scales.shape
    words = np.ascontiguousarray(words).reshape(g, 128, n, 2)
    nib = np.empty((g, 128, n, 4), np.uint8)
    nib[..., 0::2] = words & 0xF
    nib[..., 1::2] = words >> 4
    vals = E2M1[nib] * np.repeat(np.exp2(scales.astype(np.float64) - 127.0), 8, axis=1)[..., None]
    return vals.transpose(0, 1, 3, 2).reshape(g * 512, n)


def relu(v):
    return np.maximum(v, 0.0)


K, T, S, H, N = 512, 2048, 1024, 512, 256


def setup_inputs():
    n = np.random.standard_normal
    s = mx_kscale(K)[:, None]
    u = mx_kscale(H)
    packed_xT = pack_weight(n((K, T)) * s)
    packed_w2 = pack_fp4(n((H, N)) / np.sqrt(H) / u[:, None])
    return {
        "x_words": packed_xT[0],
        "x_scales": packed_xT[1],
        "w1": (n((K, H)) / np.sqrt(K) / s * u).astype(np.float32),
        "w2_words": packed_w2[0],
        "w2_scales": packed_w2[1],
        "pos": (0.5 * n((H, S)) * u[:, None]).astype(np.float32),
        "offs": striped8(np.random.randint(0, T, (8, S))),
    }


def reference(x_words, x_scales, w1, w2_words, w2_scales, pos, offs):
    xq = unpack_weight(x_words, x_scales)[np.arange(K)[:, None], runs(offs, K)]
    h = relu((mxq(f64(w1), 0, "e4m3").T @ xq) + f64(pos))
    return unpack_fp4(w2_words, w2_scales).T @ mxq(h, 0, "e4m3")

@@ -1,0 +1,186 @@
+from contextlib import ExitStack
+
+import concourse.mybir as mybir
+
+K, T, S, H, N = 512, 2048, 1024, 512, 256
+FLOPS = 2 * K * H * S + 2 * H * N * S
+
+F32 = mybir.dt.float32
+BF16 = mybir.dt.bfloat16
+I32 = mybir.dt.int32
+U32 = mybir.dt.uint32
+U16 = mybir.dt.uint16
+U8 = mybir.dt.uint8
+FP8X4 = mybir.dt.float8_e4m3fn_x4
+FP4X4 = mybir.dt.float4_e2m1fn_x4
+ADD = mybir.AluOpType.add
+MAX = mybir.AluOpType.max
+RELU = mybir.ActivationFunctionType.Relu
+
+P = 128
+PACK = 4
+BANK = 512
+PIECE = 256
+HALF = 512
+CHUNKS = ((0, 256), (256, 256), (512, 256), (768, 128), (896, 128))
+RELU_ON_VECTOR = (0, 0, 64, 64, 128)
+W1_ON_VECTOR = 84
+
+
+def tile_picked_phpq_relu_p_kernel(tc, x_words, x_scales, w1, w2_words, w2_scales, pos, offs, out):
+    nc = tc.nc
+    with ExitStack() as ctx:
+        keep = ctx.enter_context(tc.tile_pool(name="keep", bufs=1))
+        ring = ctx.enter_context(tc.tile_pool(name="ring", bufs=5))
+        psum_h = ctx.enter_context(tc.psum_pool(name="psum_h", bufs=6))
+        psum_o = ctx.enter_context(tc.psum_pool(name="psum_o", bufs=2))
+
+        offsets = keep.tile([P, S // 16], U16, name="offsets")
+        nc.sync.dma_start(offsets[:], offs)
+
+        scale_table = keep.tile([P, T], U8, name="scale_table", tag="early", align_bytes=64)
+        nc.gpsimd.memset(scale_table[:].bitcast(I32), 0)
+        w2_codes = keep.tile([P, 2 * N], U8, name="w2_codes", align_bytes=64)
+        nc.sync.dma_start(w2_codes[:].bitcast(I32), w2_words[0].bitcast(I32))
+        for e in range(2):
+            nc.sync.dma_start(scale_table[e:P:16, :].bitcast(I32), x_scales[0, e:16:2, :].bitcast(I32))
+
+        word_table = keep.tile([P, T], I32, name="word_table", align_bytes=64)
+        nc.sync.dma_start(word_table[:], x_words[0].rearrange("p n t -> p (n t)").bitcast(I32))
+        w1_raw = keep.tile([P, PACK, H], F32, name="w1_raw", align_bytes=64)
+        nc.sync.dma_start(w1_raw[:], w1.rearrange("(p j) c -> p j c", j=PACK))
+
+        w2_plane = keep.tile([P, N], U8, name="w2_plane", align_bytes=64)
+        nc.vector.memset(w2_plane[:].bitcast(I32), 0)
+        for q in range(4):
+            queue = nc.gpsimd if q < 3 else nc.sync
+            queue.dma_start(w2_plane[32 * q : 32 * q + 4, :].bitcast(I32), w2_scales[0, 4 * q : 4 * q + 4, :].bitcast(I32))
+
+        warm = keep.tile([P, 8], F32, name="warm")
+        nc.vector.memset(warm[:, 0:1], 0.0)
+        nc.scalar.activation(warm[:, 4:5], warm[:, 0:1], RELU)
+
+        pos_rows = pos.rearrange("(p t) s -> p t s", t=PACK)
+
+        x_planes = []
+        picked = []
+
+        def gather_scales(half):
+            columns = HALF // 16
+            tile = keep.tile([P, HALF], U8, name="picked%d" % half, align_bytes=64)
+            nc.vector.tensor_copy(tile[:], scale_table[:].indirect(offsets[:, half * columns : (half + 1) * columns]))
+            picked.append(tile)
+
+        def place_scales(half):
+            plane = keep.tile([P, HALF], U8, name="x_plane%d" % half, align_bytes=64)
+            nc.vector.tensor_copy(plane[:].bitcast(I32), picked[half][:].bitcast(I32))
+            for e in range(2):
+                nc.sync.dma_start(plane[2 + e : P : 32, :].bitcast(I32), picked[half][16 + e : P : 32, :].bitcast(I32))
+            x_planes.append(plane)
+
+        gather_scales(0)
+        place_scales(0)
+        gather_scales(1)
+        pos_all = keep.tile([P, PACK * S], F32, name="pos_all", tag="early", align_bytes=64)
+        pos_tiles = []
+
+        def load_pos(g):
+            view = pos_all[:, g * PACK * PIECE : (g + 1) * PACK * PIECE].rearrange("p (t n) -> p t n", t=PACK)
+            nc.sync.dma_start(view, pos_rows[:, :, g * PIECE : (g + 1) * PIECE])
+            pos_tiles.append(view)
+
+        load_pos(0)
+        place_scales(1)
+        for g in range(1, 4):
+            load_pos(g)
+
+        x_codes = {}
+
+        def gather_words(g, tag):
+            tile = keep.tile([P, PIECE], U32, name=tag, tag=tag, align_bytes=64)
+            columns = PIECE // 16
+            nc.vector.tensor_copy(tile[:], word_table[:].bitcast(U32).indirect(offsets[:, g * columns : (g + 1) * columns]))
+            x_codes[g] = tile
+
+        for g in range(3):
+            gather_words(g, "x_codes%d" % g)
+
+        w1_grouped = keep.tile([P, PACK, P, PACK], BF16, name="w1_grouped", tag="w1_grouped", align_bytes=64)
+        cast_out = w1_grouped[:].rearrange("p t m j -> p m t j")
+        cast_in = w1_raw[:].rearrange("p j (m t) -> p m t j", t=PACK)
+        nc.scalar.copy(cast_out[:, W1_ON_VECTOR:], cast_in[:, W1_ON_VECTOR:])
+        nc.vector.tensor_copy(cast_out[:, :W1_ON_VECTOR], cast_in[:, :W1_ON_VECTOR])
+        w1_codes = keep.tile([P, PACK, P], U32, name="w1_codes", align_bytes=64)
+        w1_plane = keep.tile([P, PACK, P], U8, name="w1_plane", align_bytes=64)
+        for t in range(PACK):
+            nc.vector.quantize_mx(
+                out=w1_codes[:, t, :].bitcast(FP8X4),
+                scales=w1_plane[:, t, :],
+                in_=w1_grouped[:, t, :, :].rearrange("p m j -> p (m j)"),
+            )
+        gather_words(3, "w1_grouped")
+
+        out_rows = out.rearrange("(u p) s -> p u s", p=P)
+        h_sum = {}
+        h_mx = {}
+
+        def first_layer(c):
+            start, width = CHUNKS[c]
+            g, inside = divmod(start, PIECE)
+            per_bank = BANK // width
+            summed = ring.tile([P, PACK, width], BF16, name="summed", align_bytes=64)
+            for t0 in range(0, PACK, per_bank):
+                bank = psum_h.tile([P, per_bank, width], F32, name="bank_h")
+                for t in range(t0, t0 + per_bank):
+                    nc.tensor.matmul_mx(
+                        out=bank[:, t - t0, :],
+                        lhsT=w1_codes[:, t, :].bitcast(FP8X4),
+                        lhsT_scale=w1_plane[:, t, :],
+                        rhs=x_codes[g][:, inside : inside + width].bitcast(FP8X4),
+                        rhs_scale=x_planes[start // HALF][:, start % HALF : start % HALF + width],
+                        start=True,
+                        stop=True,
+                    )
+                nc.vector.tensor_tensor(
+                    summed[:, t0 : t0 + per_bank, :], bank[:], pos_tiles[g][:, t0 : t0 + per_bank, inside : inside + width], ADD
+                )
+            h_sum[c] = summed
+
+        def relu(c):
+            start, width = CHUNKS[c]
+            grouped = ring.tile([P, width, PACK], BF16, name="grouped", align_bytes=64)
+            dst = grouped[:].rearrange("p (c i) t -> p c t i", i=4)
+            src = h_sum[c][:].rearrange("p t (c i) -> p c t i", i=4)
+            cut = (width - RELU_ON_VECTOR[c]) // 4
+            if cut > 0:
+                nc.scalar.activation(dst[:, :cut], src[:, :cut], RELU)
+            if cut < width // 4:
+                nc.vector.tensor_scalar(dst[:, cut:], src[:, cut:], 0.0, None, MAX)
+            h_mx[c] = grouped
+
+        def second_layer(c):
+            start, width = CHUNKS[c]
+            codes = ring.tile([P, width], U32, name="h_codes", align_bytes=64)
+            plane = ring.tile([P, width], U8, name="h_plane", align_bytes=64)
+            nc.vector.quantize_mx(out=codes[:].bitcast(FP8X4), scales=plane[:], in_=h_mx[c][:].rearrange("p n t -> p (n t)"))
+            bank = psum_o.tile([P, N // P, width], F32, name="bank_o")
+            for u in range(N // P):
+                nc.tensor.matmul_mx(
+                    out=bank[:, u, :],
+                    lhsT=w2_codes[:, 2 * P * u : 2 * P * (u + 1)].bitcast(FP4X4),
+                    lhsT_scale=w2_plane[:, P * u : P * (u + 1)],
+                    rhs=codes[:].bitcast(FP8X4),
+                    rhs_scale=plane[:],
+                    start=True,
+                    stop=True,
+                )
+            result = ring.tile([P, N // P, width], F32, name="result", align_bytes=64)
+            nc.scalar.copy(result[:], bank[:])
+            nc.sync.dma_start(out_rows[:, :, start : start + width], result[:])
+
+        for c in range(len(CHUNKS) + 1):
+            if c < len(CHUNKS):
+                first_layer(c)
+                relu(c)
+            if c > 0:
+                second_layer(c - 1)

@@ -21,33 +21,31 @@ P = 128
 PACK = 4
 BANK = 512
 PIECE = 256
-HALF = 512
 CHUNKS = ((0, 256), (256, 256), (512, 256), (768, 128), (896, 128))
-RELU_ON_VECTOR = (0, 0, 64, 64, 128)
-W1_ON_VECTOR = 84
+RELU_ON_VECTOR = (0, 0, 0, 0, 128)
+W1_ON_VECTOR = 80
 
 
 def tile_picked_phpq_relu_p_kernel(tc, x_words, x_scales, w1, w2_words, w2_scales, pos, offs, out):
     nc = tc.nc
     with ExitStack() as ctx:
         keep = ctx.enter_context(tc.tile_pool(name="keep", bufs=1))
-        ring = ctx.enter_context(tc.tile_pool(name="ring", bufs=5))
-        psum_h = ctx.enter_context(tc.psum_pool(name="psum_h", bufs=6))
-        psum_o = ctx.enter_context(tc.psum_pool(name="psum_o", bufs=2))
+        shared = ctx.enter_context(tc.tile_pool(name="shared", bufs=1))
+        ring = ctx.enter_context(tc.tile_pool(name="ring", bufs=6))
+        psum = ctx.enter_context(tc.psum_pool(name="psum", bufs=1))
 
         offsets = keep.tile([P, S // 16], U16, name="offsets")
         nc.sync.dma_start(offsets[:], offs)
 
-        scale_table = keep.tile([P, T], U8, name="scale_table", tag="early", align_bytes=64)
+        scale_table = shared.tile([P, T], U8, name="scale_table", offset=3072, align_bytes=64)
         nc.gpsimd.memset(scale_table[:].bitcast(I32), 0)
         w2_codes = keep.tile([P, 2 * N], U8, name="w2_codes", align_bytes=64)
         nc.sync.dma_start(w2_codes[:].bitcast(I32), w2_words[0].bitcast(I32))
-        for e in range(2):
-            nc.sync.dma_start(scale_table[e:P:16, :].bitcast(I32), x_scales[0, e:16:2, :].bitcast(I32))
+        nc.sync.dma_start(scale_table[0:P:8, :].bitcast(I32), x_scales[0].bitcast(I32))
 
         word_table = keep.tile([P, T], I32, name="word_table", align_bytes=64)
         nc.sync.dma_start(word_table[:], x_words[0].rearrange("p n t -> p (n t)").bitcast(I32))
-        w1_raw = keep.tile([P, PACK, H], F32, name="w1_raw", align_bytes=64)
+        w1_raw = keep.tile([P, PACK, H], F32, name="w1_raw", tag="w1_raw", align_bytes=64)
         nc.sync.dma_start(w1_raw[:], w1.rearrange("(p j) c -> p j c", j=PACK))
 
         w2_plane = keep.tile([P, N], U8, name="w2_plane", align_bytes=64)
@@ -62,63 +60,42 @@ def tile_picked_phpq_relu_p_kernel(tc, x_words, x_scales, w1, w2_words, w2_scale
 
         pos_rows = pos.rearrange("(p t) s -> p t s", t=PACK)
 
-        x_planes = []
-        picked = []
+        pos_views = {}
 
-        def gather_scales(half):
-            columns = HALF // 16
-            tile = keep.tile([P, HALF], U8, name="picked%d" % half, align_bytes=64)
-            nc.vector.tensor_copy(tile[:], scale_table[:].indirect(offsets[:, half * columns : (half + 1) * columns]))
-            picked.append(tile)
+        def load_pos(g, tile):
+            start = g * PIECE
+            nc.sync.dma_start(tile[:], pos_rows[:, :, start : start + PIECE])
+            for chunk_start, chunk_width in CHUNKS:
+                if start <= chunk_start < start + PIECE:
+                    pos_views[chunk_start] = tile[:, :, chunk_start - start : chunk_start - start + chunk_width]
 
-        def place_scales(half):
-            plane = keep.tile([P, HALF], U8, name="x_plane%d" % half, align_bytes=64)
-            nc.vector.tensor_copy(plane[:].bitcast(I32), picked[half][:].bitcast(I32))
-            for e in range(2):
-                nc.sync.dma_start(plane[2 + e : P : 32, :].bitcast(I32), picked[half][16 + e : P : 32, :].bitcast(I32))
-            x_planes.append(plane)
+        load_pos(0, keep.tile([P, PACK, PIECE], F32, name="pos0", align_bytes=64))
+        x_plane = keep.tile([P, S], U8, name="x_plane", align_bytes=64)
+        nc.vector.memset(x_plane[:].bitcast(I32), 0)
+        picked = keep.tile([P, S], U8, name="picked", align_bytes=64)
+        nc.vector.tensor_copy(picked[:], scale_table[:].indirect(offsets[:]))
+        for r in range(4):
+            nc.sync.dma_start(x_plane[r:P:32, :].bitcast(I32), picked[8 * r : P : 32, :].bitcast(I32))
+        load_pos(1, shared.tile([P, PACK, PIECE], F32, name="pos1", offset=0, align_bytes=64))
+        load_pos(2, shared.tile([P, PACK, PIECE], F32, name="pos2", offset=4096, align_bytes=64))
 
-        gather_scales(0)
-        place_scales(0)
-        gather_scales(1)
-        pos_all = keep.tile([P, PACK * S], F32, name="pos_all", tag="early", align_bytes=64)
-        pos_tiles = []
-
-        def load_pos(g):
-            view = pos_all[:, g * PACK * PIECE : (g + 1) * PACK * PIECE].rearrange("p (t n) -> p t n", t=PACK)
-            nc.sync.dma_start(view, pos_rows[:, :, g * PIECE : (g + 1) * PIECE])
-            pos_tiles.append(view)
-
-        load_pos(0)
-        place_scales(1)
-        for g in range(1, 4):
-            load_pos(g)
-
-        x_codes = {}
-
-        def gather_words(g, tag):
-            tile = keep.tile([P, PIECE], U32, name=tag, tag=tag, align_bytes=64)
-            columns = PIECE // 16
-            nc.vector.tensor_copy(tile[:], word_table[:].bitcast(U32).indirect(offsets[:, g * columns : (g + 1) * columns]))
-            x_codes[g] = tile
-
-        for g in range(3):
-            gather_words(g, "x_codes%d" % g)
+        x_codes = keep.tile([P, S], U32, name="x_codes", align_bytes=64)
+        nc.vector.tensor_copy(x_codes[:], word_table[:].bitcast(U32).indirect(offsets[:]))
 
         w1_grouped = keep.tile([P, PACK, P, PACK], BF16, name="w1_grouped", tag="w1_grouped", align_bytes=64)
-        cast_out = w1_grouped[:].rearrange("p t m j -> p m t j")
-        cast_in = w1_raw[:].rearrange("p j (m t) -> p m t j", t=PACK)
+        cast_out = w1_grouped[:].rearrange("p t m j -> p m j t")
+        cast_in = w1_raw[:].rearrange("p j (m t) -> p m j t", t=PACK)
         nc.scalar.copy(cast_out[:, W1_ON_VECTOR:], cast_in[:, W1_ON_VECTOR:])
         nc.vector.tensor_copy(cast_out[:, :W1_ON_VECTOR], cast_in[:, :W1_ON_VECTOR])
+        load_pos(3, keep.tile([P, PACK, 256], F32, name="pos3", tag="w1_raw", align_bytes=64))
         w1_codes = keep.tile([P, PACK, P], U32, name="w1_codes", align_bytes=64)
         w1_plane = keep.tile([P, PACK, P], U8, name="w1_plane", align_bytes=64)
-        for t in range(PACK):
+        for t in range(0, PACK, 2):
             nc.vector.quantize_mx(
-                out=w1_codes[:, t, :].bitcast(FP8X4),
-                scales=w1_plane[:, t, :],
-                in_=w1_grouped[:, t, :, :].rearrange("p m j -> p (m j)"),
+                out=w1_codes[:, t : t + 2, :].rearrange("p t m -> p (t m)").bitcast(FP8X4),
+                scales=w1_plane[:, t : t + 2, :].rearrange("p t m -> p (t m)"),
+                in_=w1_grouped[:, t : t + 2, :, :].rearrange("p t m j -> p (t m j)"),
             )
-        gather_words(3, "w1_grouped")
 
         out_rows = out.rearrange("(u p) s -> p u s", p=P)
         h_sum = {}
@@ -126,44 +103,59 @@ def tile_picked_phpq_relu_p_kernel(tc, x_words, x_scales, w1, w2_words, w2_scale
 
         def first_layer(c):
             start, width = CHUNKS[c]
-            g, inside = divmod(start, PIECE)
             per_bank = BANK // width
             summed = ring.tile([P, PACK, width], BF16, name="summed", align_bytes=64)
             for t0 in range(0, PACK, per_bank):
-                bank = psum_h.tile([P, per_bank, width], F32, name="bank_h")
+                bank = psum.tile([P, per_bank, width], F32, name="bank", tag="bank%d" % (start // 128 + t0 // per_bank))
                 for t in range(t0, t0 + per_bank):
                     nc.tensor.matmul_mx(
                         out=bank[:, t - t0, :],
                         lhsT=w1_codes[:, t, :].bitcast(FP8X4),
                         lhsT_scale=w1_plane[:, t, :],
-                        rhs=x_codes[g][:, inside : inside + width].bitcast(FP8X4),
-                        rhs_scale=x_planes[start // HALF][:, start % HALF : start % HALF + width],
+                        rhs=x_codes[:, start : start + width].bitcast(FP8X4),
+                        rhs_scale=x_plane[:, start : start + width],
                         start=True,
                         stop=True,
                     )
                 nc.vector.tensor_tensor(
-                    summed[:, t0 : t0 + per_bank, :], bank[:], pos_tiles[g][:, t0 : t0 + per_bank, inside : inside + width], ADD
+                    summed[:, t0 : t0 + per_bank, :], bank[:], pos_views[start][:, t0 : t0 + per_bank, :], ADD
                 )
             h_sum[c] = summed
 
-        def relu(c):
-            start, width = CHUNKS[c]
-            grouped = ring.tile([P, width, PACK], BF16, name="grouped", align_bytes=64)
-            dst = grouped[:].rearrange("p (c i) t -> p c t i", i=4)
+        def relu_views(c):
+            dst = h_mx[c][:].rearrange("p (c i) t -> p c t i", i=4)
             src = h_sum[c][:].rearrange("p t (c i) -> p c t i", i=4)
-            cut = (width - RELU_ON_VECTOR[c]) // 4
+            return dst, src, (CHUNKS[c][1] - RELU_ON_VECTOR[c]) // 4
+
+        def relu_scalar(c):
+            h_mx[c] = ring.tile([P, CHUNKS[c][1], PACK], BF16, name="grouped", align_bytes=64)
+            dst, src, cut = relu_views(c)
             if cut > 0:
                 nc.scalar.activation(dst[:, :cut], src[:, :cut], RELU)
-            if cut < width // 4:
+
+        def relu_vector(c):
+            dst, src, cut = relu_views(c)
+            if RELU_ON_VECTOR[c] > 0:
                 nc.vector.tensor_scalar(dst[:, cut:], src[:, cut:], 0.0, None, MAX)
-            h_mx[c] = grouped
+
+        h_planes = {}
 
         def second_layer(c):
+            quantise(c)
+            multiply(c)
+
+        def quantise(c):
             start, width = CHUNKS[c]
             codes = ring.tile([P, width], U32, name="h_codes", align_bytes=64)
             plane = ring.tile([P, width], U8, name="h_plane", align_bytes=64)
             nc.vector.quantize_mx(out=codes[:].bitcast(FP8X4), scales=plane[:], in_=h_mx[c][:].rearrange("p n t -> p (n t)"))
-            bank = psum_o.tile([P, N // P, width], F32, name="bank_o")
+            h_planes[c] = (codes, plane)
+
+        def multiply(c):
+            start, width = CHUNKS[c]
+            codes, plane = h_planes[c]
+            result = ring.tile([P, N // P, width], F32, name="result", align_bytes=64)
+            bank = psum.tile([P, N // P, width], F32, name="bank", tag="bank%d" % (start // 128))
             for u in range(N // P):
                 nc.tensor.matmul_mx(
                     out=bank[:, u, :],
@@ -174,13 +166,21 @@ def tile_picked_phpq_relu_p_kernel(tc, x_words, x_scales, w1, w2_words, w2_scale
                     start=True,
                     stop=True,
                 )
-            result = ring.tile([P, N // P, width], F32, name="result", align_bytes=64)
-            nc.scalar.copy(result[:], bank[:])
-            nc.sync.dma_start(out_rows[:, :, start : start + width], result[:])
+            if c == len(CHUNKS) - 2:
+                nc.vector.tensor_copy(result[:], bank[:])
+            else:
+                nc.scalar.copy(result[:], bank[:])
+            queue = nc.scalar if c == len(CHUNKS) - 1 else nc.sync
+            queue.dma_start(out_rows[:, :, start : start + width], result[:])
 
-        for c in range(len(CHUNKS) + 1):
-            if c < len(CHUNKS):
-                first_layer(c)
-                relu(c)
-            if c > 0:
-                second_layer(c - 1)
+        count = len(CHUNKS)
+        for step in range(count):
+            first_layer(step)
+            relu_scalar(step)
+            if 0 < step < count - 1:
+                second_layer(step - 1)
+        relu_vector(count - 1)
+        quantise(count - 2)
+        quantise(count - 1)
+        multiply(count - 2)
+        multiply(count - 1)

@@ -21,23 +21,24 @@ P = 128
 PACK = 4
 BANK = 512
 PIECE = 256
+W1_ON_VECTOR = 84
+H_BANKS = ((0, 1), (2, 3), (4, 5), (4,), (5,))
+OUT_BANKS = (0, 2, 1, 3, 6)
 CHUNKS = ((0, 256), (256, 256), (512, 256), (768, 128), (896, 128))
-RELU_ON_VECTOR = (0, 0, 0, 0, 128)
-W1_ON_VECTOR = 80
+GATHERS = ((0, 768), (768, 256))
 
 
 def tile_picked_phpq_relu_p_kernel(tc, x_words, x_scales, w1, w2_words, w2_scales, pos, offs, out):
     nc = tc.nc
     with ExitStack() as ctx:
         keep = ctx.enter_context(tc.tile_pool(name="keep", bufs=1))
-        shared = ctx.enter_context(tc.tile_pool(name="shared", bufs=1))
         ring = ctx.enter_context(tc.tile_pool(name="ring", bufs=6))
         psum = ctx.enter_context(tc.psum_pool(name="psum", bufs=1))
 
         offsets = keep.tile([P, S // 16], U16, name="offsets")
         nc.sync.dma_start(offsets[:], offs)
 
-        scale_table = shared.tile([P, T], U8, name="scale_table", offset=3072, align_bytes=64)
+        scale_table = keep.tile([P, T], U8, name="scale_table", tag="early", align_bytes=64)
         nc.gpsimd.memset(scale_table[:].bitcast(I32), 0)
         w2_codes = keep.tile([P, 2 * N], U8, name="w2_codes", align_bytes=64)
         nc.sync.dma_start(w2_codes[:].bitcast(I32), w2_words[0].bitcast(I32))
@@ -45,14 +46,13 @@ def tile_picked_phpq_relu_p_kernel(tc, x_words, x_scales, w1, w2_words, w2_scale
 
         word_table = keep.tile([P, T], I32, name="word_table", align_bytes=64)
         nc.sync.dma_start(word_table[:], x_words[0].rearrange("p n t -> p (n t)").bitcast(I32))
-        w1_raw = keep.tile([P, PACK, H], F32, name="w1_raw", tag="w1_raw", align_bytes=64)
+        w1_raw = keep.tile([P, PACK, H], F32, name="w1_raw", align_bytes=64)
         nc.sync.dma_start(w1_raw[:], w1.rearrange("(p j) c -> p j c", j=PACK))
 
         w2_plane = keep.tile([P, N], U8, name="w2_plane", align_bytes=64)
         nc.vector.memset(w2_plane[:].bitcast(I32), 0)
         for q in range(4):
-            queue = nc.gpsimd if q < 3 else nc.sync
-            queue.dma_start(w2_plane[32 * q : 32 * q + 4, :].bitcast(I32), w2_scales[0, 4 * q : 4 * q + 4, :].bitcast(I32))
+            nc.gpsimd.dma_start(w2_plane[32 * q : 32 * q + 4, :].bitcast(I32), w2_scales[0, 4 * q : 4 * q + 4, :].bitcast(I32))
 
         warm = keep.tile([P, 8], F32, name="warm")
         nc.vector.memset(warm[:, 0:1], 0.0)
@@ -62,32 +62,46 @@ def tile_picked_phpq_relu_p_kernel(tc, x_words, x_scales, w1, w2_words, w2_scale
 
         pos_views = {}
 
-        def load_pos(g, tile):
-            start = g * PIECE
-            nc.sync.dma_start(tile[:], pos_rows[:, :, start : start + PIECE])
+        def load_pos(start, t0, room):
+            tile = room.rearrange("p (t n) -> p t n", n=PIECE)
+            planes = tile.shape[1]
+            nc.sync.dma_start(tile, pos_rows[:, t0 : t0 + planes, start : start + PIECE])
             for chunk_start, chunk_width in CHUNKS:
                 if start <= chunk_start < start + PIECE:
-                    pos_views[chunk_start] = tile[:, :, chunk_start - start : chunk_start - start + chunk_width]
+                    per_bank = BANK // chunk_width
+                    for t in range(0, planes, per_bank):
+                        pos_views[chunk_start, t0 + t] = tile[:, t : t + per_bank, chunk_start - start : chunk_start - start + chunk_width]
 
-        load_pos(0, keep.tile([P, PACK, PIECE], F32, name="pos0", align_bytes=64))
+        pos_first = keep.tile([P, 2 * PIECE], F32, name="pos_first", align_bytes=64)
+        load_pos(0, 0, pos_first[:])
         x_plane = keep.tile([P, S], U8, name="x_plane", align_bytes=64)
         nc.vector.memset(x_plane[:].bitcast(I32), 0)
         picked = keep.tile([P, S], U8, name="picked", align_bytes=64)
         nc.vector.tensor_copy(picked[:], scale_table[:].indirect(offsets[:]))
         for r in range(4):
             nc.sync.dma_start(x_plane[r:P:32, :].bitcast(I32), picked[8 * r : P : 32, :].bitcast(I32))
-        load_pos(1, shared.tile([P, PACK, PIECE], F32, name="pos1", offset=0, align_bytes=64))
-        load_pos(2, shared.tile([P, PACK, PIECE], F32, name="pos2", offset=4096, align_bytes=64))
+        pos_rest = keep.tile([P, PACK * S - 2 * PIECE], F32, name="pos_rest", tag="early", align_bytes=64)
+        load_pos(0, 2, pos_rest[:, : 2 * PIECE])
+        for g in range(1, 4):
+            load_pos(g * PIECE, 0, pos_rest[:, (4 * g - 2) * PIECE : (4 * g + 2) * PIECE])
 
-        x_codes = keep.tile([P, S], U32, name="x_codes", align_bytes=64)
-        nc.vector.tensor_copy(x_codes[:], word_table[:].bitcast(U32).indirect(offsets[:]))
+        x_codes = {}
+
+        def gather_words(g, tag):
+            start, width = GATHERS[g]
+            tile = keep.tile([P, width], U32, name=tag, tag=tag, align_bytes=64)
+            nc.vector.tensor_copy(tile[:], word_table[:].bitcast(U32).indirect(offsets[:, start // 16 : (start + width) // 16]))
+            for chunk_start, chunk_width in CHUNKS:
+                if start <= chunk_start < start + width:
+                    x_codes[chunk_start] = tile[:, chunk_start - start : chunk_start - start + chunk_width]
+
+        gather_words(0, "x_codes")
 
         w1_grouped = keep.tile([P, PACK, P, PACK], BF16, name="w1_grouped", tag="w1_grouped", align_bytes=64)
         cast_out = w1_grouped[:].rearrange("p t m j -> p m j t")
         cast_in = w1_raw[:].rearrange("p j (m t) -> p m j t", t=PACK)
         nc.scalar.copy(cast_out[:, W1_ON_VECTOR:], cast_in[:, W1_ON_VECTOR:])
         nc.vector.tensor_copy(cast_out[:, :W1_ON_VECTOR], cast_in[:, :W1_ON_VECTOR])
-        load_pos(3, keep.tile([P, PACK, 256], F32, name="pos3", tag="w1_raw", align_bytes=64))
         w1_codes = keep.tile([P, PACK, P], U32, name="w1_codes", align_bytes=64)
         w1_plane = keep.tile([P, PACK, P], U8, name="w1_plane", align_bytes=64)
         for t in range(0, PACK, 2):
@@ -97,6 +111,8 @@ def tile_picked_phpq_relu_p_kernel(tc, x_words, x_scales, w1, w2_words, w2_scale
                 in_=w1_grouped[:, t : t + 2, :, :].rearrange("p t m j -> p (t m j)"),
             )
 
+        gather_words(1, "w1_grouped")
+
         out_rows = out.rearrange("(u p) s -> p u s", p=P)
         h_sum = {}
         h_mx = {}
@@ -104,45 +120,43 @@ def tile_picked_phpq_relu_p_kernel(tc, x_words, x_scales, w1, w2_words, w2_scale
         def first_layer(c):
             start, width = CHUNKS[c]
             per_bank = BANK // width
-            summed = ring.tile([P, PACK, width], BF16, name="summed", align_bytes=64)
+            woven = per_bank == PACK
+            summed = ring.tile([P, width, PACK] if woven else [P, PACK, width], BF16, name="summed", align_bytes=64)
             for t0 in range(0, PACK, per_bank):
-                bank = psum.tile([P, per_bank, width], F32, name="bank", tag="bank%d" % (start // 128 + t0 // per_bank))
+                bank = psum.tile([P, per_bank, width], F32, name="bank", tag="bank%d" % H_BANKS[c][t0 // per_bank])
                 for t in range(t0, t0 + per_bank):
                     nc.tensor.matmul_mx(
                         out=bank[:, t - t0, :],
                         lhsT=w1_codes[:, t, :].bitcast(FP8X4),
                         lhsT_scale=w1_plane[:, t, :],
-                        rhs=x_codes[:, start : start + width].bitcast(FP8X4),
+                        rhs=x_codes[start].bitcast(FP8X4),
                         rhs_scale=x_plane[:, start : start + width],
                         start=True,
                         stop=True,
                     )
-                nc.vector.tensor_tensor(
-                    summed[:, t0 : t0 + per_bank, :], bank[:], pos_views[start][:, t0 : t0 + per_bank, :], ADD
-                )
+                if woven:
+                    nc.vector.tensor_tensor(
+                        summed[:].rearrange("p (c i) t -> p c t i", i=4),
+                        bank[:].rearrange("p t (c i) -> p c t i", i=4),
+                        pos_views[start, t0].rearrange("p t (c i) -> p c t i", i=4),
+                        ADD,
+                    )
+                else:
+                    nc.vector.tensor_tensor(summed[:, t0 : t0 + per_bank, :], bank[:], pos_views[start, t0], ADD)
             h_sum[c] = summed
 
-        def relu_views(c):
-            dst = h_mx[c][:].rearrange("p (c i) t -> p c t i", i=4)
-            src = h_sum[c][:].rearrange("p t (c i) -> p c t i", i=4)
-            return dst, src, (CHUNKS[c][1] - RELU_ON_VECTOR[c]) // 4
-
-        def relu_scalar(c):
-            h_mx[c] = ring.tile([P, CHUNKS[c][1], PACK], BF16, name="grouped", align_bytes=64)
-            dst, src, cut = relu_views(c)
-            if cut > 0:
-                nc.scalar.activation(dst[:, :cut], src[:, :cut], RELU)
-
-        def relu_vector(c):
-            dst, src, cut = relu_views(c)
-            if RELU_ON_VECTOR[c] > 0:
-                nc.vector.tensor_scalar(dst[:, cut:], src[:, cut:], 0.0, None, MAX)
+        def relu(c):
+            grouped = ring.tile([P, CHUNKS[c][1], PACK], BF16, name="grouped", align_bytes=64)
+            if BANK // CHUNKS[c][1] == PACK:
+                nc.vector.tensor_scalar(grouped[:], h_sum[c][:], 0.0, None, MAX)
+            else:
+                dst = grouped[:].rearrange("p (c i) t -> p c t i", i=4)
+                src = h_sum[c][:].rearrange("p t (c i) -> p c t i", i=4)
+                nc.scalar.activation(dst, src, RELU)
+            h_mx[c] = grouped
 
         h_planes = {}
-
-        def second_layer(c):
-            quantise(c)
-            multiply(c)
+        banks = {}
 
         def quantise(c):
             start, width = CHUNKS[c]
@@ -154,8 +168,7 @@ def tile_picked_phpq_relu_p_kernel(tc, x_words, x_scales, w1, w2_words, w2_scale
         def multiply(c):
             start, width = CHUNKS[c]
             codes, plane = h_planes[c]
-            result = ring.tile([P, N // P, width], F32, name="result", align_bytes=64)
-            bank = psum.tile([P, N // P, width], F32, name="bank", tag="bank%d" % (start // 128))
+            bank = psum.tile([P, N // P, width], F32, name="bank", tag="bank%d" % OUT_BANKS[c])
             for u in range(N // P):
                 nc.tensor.matmul_mx(
                     out=bank[:, u, :],
@@ -166,21 +179,33 @@ def tile_picked_phpq_relu_p_kernel(tc, x_words, x_scales, w1, w2_words, w2_scale
                     start=True,
                     stop=True,
                 )
-            if c == len(CHUNKS) - 2:
-                nc.vector.tensor_copy(result[:], bank[:])
-            else:
-                nc.scalar.copy(result[:], bank[:])
-            queue = nc.scalar if c == len(CHUNKS) - 1 else nc.sync
-            queue.dma_start(out_rows[:, :, start : start + width], result[:])
+            banks[c] = bank
 
-        count = len(CHUNKS)
-        for step in range(count):
-            first_layer(step)
-            relu_scalar(step)
-            if 0 < step < count - 1:
-                second_layer(step - 1)
-        relu_vector(count - 1)
-        quantise(count - 2)
-        quantise(count - 1)
-        multiply(count - 2)
-        multiply(count - 1)
+        def store(c):
+            start, width = CHUNKS[c]
+            result = ring.tile([P, N // P, width], F32, name="result", align_bytes=64)
+            if c == 3:
+                nc.vector.tensor_copy(result[:], banks[c][:])
+            else:
+                nc.scalar.copy(result[:], banks[c][:])
+            nc.sync.dma_start(out_rows[:, :, start : start + width], result[:])
+
+        for c in range(3):
+            first_layer(c)
+            relu(c)
+        for c in range(2):
+            quantise(c)
+            multiply(c)
+            store(c)
+        first_layer(3)
+        quantise(2)
+        multiply(2)
+        first_layer(4)
+        relu(3)
+        relu(4)
+        store(2)
+        for c in (3, 4):
+            quantise(c)
+            multiply(c)
+        for c in (3, 4):
+            store(c)

@@ -15,75 +15,82 @@ FP8X4 = mybir.dt.float8_e4m3fn_x4
 FP4X4 = mybir.dt.float4_e2m1fn_x4
 ADD = mybir.AluOpType.add
 MAX = mybir.AluOpType.max
+MIN = mybir.AluOpType.min
 RELU = mybir.ActivationFunctionType.Relu
+COPY = mybir.ActivationFunctionType.Copy
 
+LARGEST = 3.4028234663852886e38
 P = 128
 PACK = 4
-BANK = 512
-PIECE = 256
-W1_ON_VECTOR = 84
-H_BANKS = ((0, 1), (2, 3), (4, 5), (4,), (5,))
-OUT_BANKS = (0, 2, 1, 3, 6)
-CHUNKS = ((0, 256), (256, 256), (512, 256), (768, 128), (896, 128))
+CHUNK = 128
+W1_PIECE = 128
+W1_LAST_ON_VECTOR = 20
+POS_PIECES = ((0, 128), (128, 128), (256, 256), (512, 256), (768, 256))
+GROUPS = ((0, 2), (2, 2), (4, 2), (6, 1), (7, 1))
 GATHERS = ((0, 768), (768, 256))
+H_BANKS = 3
+CLEARED_BY_VECTOR = 192
 
 
 def tile_picked_phpq_relu_p_kernel(tc, x_words, x_scales, w1, w2_words, w2_scales, pos, offs, out):
     nc = tc.nc
     with ExitStack() as ctx:
         keep = ctx.enter_context(tc.tile_pool(name="keep", bufs=1))
-        ring = ctx.enter_context(tc.tile_pool(name="ring", bufs=6))
+        shared = ctx.enter_context(tc.tile_pool(name="shared", bufs=1))
         psum = ctx.enter_context(tc.psum_pool(name="psum", bufs=1))
 
+        w1_rows = w1.rearrange("(p j) c -> p j c", j=PACK)
+        w1_raw = []
+
+        def load_w1(a):
+            tile = keep.tile([P, PACK, W1_PIECE], F32, name="w1_raw%d" % a, align_bytes=64)
+            nc.sync.dma_start(tile[:], w1_rows[:, :, a * W1_PIECE : (a + 1) * W1_PIECE])
+            w1_raw.append(tile)
+
+        scale_tile = shared.tile([P, T], U8, name="scale_tile", offset=T // 2, align_bytes=64)
+        scale_table = scale_tile[:]
+        nc.gpsimd.memset(scale_table.bitcast(I32)[:, CLEARED_BY_VECTOR:], 0)
+        nc.vector.memset(scale_table.bitcast(I32)[:, :CLEARED_BY_VECTOR], 0)
+        load_w1(0)
         offsets = keep.tile([P, S // 16], U16, name="offsets")
         nc.sync.dma_start(offsets[:], offs)
-
-        scale_table = keep.tile([P, T], U8, name="scale_table", tag="early", align_bytes=64)
-        nc.gpsimd.memset(scale_table[:].bitcast(I32), 0)
-        w2_codes = keep.tile([P, 2 * N], U8, name="w2_codes", align_bytes=64)
-        nc.sync.dma_start(w2_codes[:].bitcast(I32), w2_words[0].bitcast(I32))
-        nc.sync.dma_start(scale_table[0:P:8, :].bitcast(I32), x_scales[0].bitcast(I32))
+        nc.sync.dma_start(scale_tile[0:P:8, :].bitcast(I32), x_scales[0].bitcast(I32))
 
         word_table = keep.tile([P, T], I32, name="word_table", align_bytes=64)
         nc.sync.dma_start(word_table[:], x_words[0].rearrange("p n t -> p (n t)").bitcast(I32))
-        w1_raw = keep.tile([P, PACK, H], F32, name="w1_raw", align_bytes=64)
-        nc.sync.dma_start(w1_raw[:], w1.rearrange("(p j) c -> p j c", j=PACK))
+        for a in range(1, H // W1_PIECE):
+            load_w1(a)
 
         w2_plane = keep.tile([P, N], U8, name="w2_plane", align_bytes=64)
         nc.vector.memset(w2_plane[:].bitcast(I32), 0)
         for q in range(4):
             nc.gpsimd.dma_start(w2_plane[32 * q : 32 * q + 4, :].bitcast(I32), w2_scales[0, 4 * q : 4 * q + 4, :].bitcast(I32))
 
-        warm = keep.tile([P, 8], F32, name="warm")
-        nc.vector.memset(warm[:, 0:1], 0.0)
-        nc.scalar.activation(warm[:, 4:5], warm[:, 0:1], RELU)
-
         pos_rows = pos.rearrange("(p t) s -> p t s", t=PACK)
-
         pos_views = {}
 
-        def load_pos(start, t0, room):
-            tile = room.rearrange("p (t n) -> p t n", n=PIECE)
-            planes = tile.shape[1]
-            nc.sync.dma_start(tile, pos_rows[:, t0 : t0 + planes, start : start + PIECE])
-            for chunk_start, chunk_width in CHUNKS:
-                if start <= chunk_start < start + PIECE:
-                    per_bank = BANK // chunk_width
-                    for t in range(0, planes, per_bank):
-                        pos_views[chunk_start, t0 + t] = tile[:, t : t + per_bank, chunk_start - start : chunk_start - start + chunk_width]
+        def load_pos(g, room):
+            start, width = POS_PIECES[g]
+            tile = room.rearrange("p (t n) -> p t n", t=PACK)
+            nc.sync.dma_start(tile, pos_rows[:, :, start : start + width])
+            for c0 in range(0, width, CHUNK):
+                pos_views[(start + c0) // CHUNK] = tile[:, :, c0 : c0 + CHUNK]
 
-        pos_first = keep.tile([P, 2 * PIECE], F32, name="pos_first", align_bytes=64)
-        load_pos(0, 0, pos_first[:])
         x_plane = keep.tile([P, S], U8, name="x_plane", align_bytes=64)
         nc.vector.memset(x_plane[:].bitcast(I32), 0)
         picked = keep.tile([P, S], U8, name="picked", align_bytes=64)
-        nc.vector.tensor_copy(picked[:], scale_table[:].indirect(offsets[:]))
+        nc.vector.tensor_copy(picked[:], scale_table.indirect(offsets[:]))
         for r in range(4):
             nc.sync.dma_start(x_plane[r:P:32, :].bitcast(I32), picked[8 * r : P : 32, :].bitcast(I32))
-        pos_rest = keep.tile([P, PACK * S - 2 * PIECE], F32, name="pos_rest", tag="early", align_bytes=64)
-        load_pos(0, 2, pos_rest[:, : 2 * PIECE])
-        for g in range(1, 4):
-            load_pos(g * PIECE, 0, pos_rest[:, (4 * g - 2) * PIECE : (4 * g + 2) * PIECE])
+        for g, (start, width) in enumerate(POS_PIECES):
+            if g < 2:
+                room = shared.tile([P, PACK * width], F32, name="pos%d" % g, offset=g * (T + 2 * N), align_bytes=64)
+            else:
+                room = keep.tile([P, PACK * width], F32, name="pos%d" % g, tag="w1_raw%d" % (g - 1), align_bytes=64)
+            load_pos(g, room[:])
+            if g == 1:
+                w2_codes = shared.tile([P, 2 * N], U8, name="w2_codes", offset=T, align_bytes=64)
+                nc.sync.dma_start(w2_codes[:].bitcast(I32), w2_words[0].bitcast(I32))
 
         x_codes = {}
 
@@ -91,17 +98,21 @@ def tile_picked_phpq_relu_p_kernel(tc, x_words, x_scales, w1, w2_words, w2_scale
             start, width = GATHERS[g]
             tile = keep.tile([P, width], U32, name=tag, tag=tag, align_bytes=64)
             nc.vector.tensor_copy(tile[:], word_table[:].bitcast(U32).indirect(offsets[:, start // 16 : (start + width) // 16]))
-            for chunk_start, chunk_width in CHUNKS:
-                if start <= chunk_start < start + width:
-                    x_codes[chunk_start] = tile[:, chunk_start - start : chunk_start - start + chunk_width]
+            for c0 in range(0, width, CHUNK):
+                x_codes[(start + c0) // CHUNK] = tile[:, c0 : c0 + CHUNK]
 
         gather_words(0, "x_codes")
 
         w1_grouped = keep.tile([P, PACK, P, PACK], BF16, name="w1_grouped", tag="w1_grouped", align_bytes=64)
         cast_out = w1_grouped[:].rearrange("p t m j -> p m j t")
-        cast_in = w1_raw[:].rearrange("p j (m t) -> p m j t", t=PACK)
-        nc.scalar.copy(cast_out[:, W1_ON_VECTOR:], cast_in[:, W1_ON_VECTOR:])
-        nc.vector.tensor_copy(cast_out[:, :W1_ON_VECTOR], cast_in[:, :W1_ON_VECTOR])
+        per_piece = W1_PIECE // PACK
+        last = H // W1_PIECE - 1
+        for a in range(last + 1):
+            cast_in = w1_raw[a][:].rearrange("p j (m t) -> p m j t", t=PACK)
+            split = W1_LAST_ON_VECTOR if a == last else 0
+            nc.scalar.activation(cast_out[:, a * per_piece + split : (a + 1) * per_piece], cast_in[:, split:], COPY)
+            if split:
+                nc.vector.tensor_copy(cast_out[:, a * per_piece : a * per_piece + split], cast_in[:, :split])
         w1_codes = keep.tile([P, PACK, P], U32, name="w1_codes", align_bytes=64)
         w1_plane = keep.tile([P, PACK, P], U8, name="w1_plane", align_bytes=64)
         for t in range(0, PACK, 2):
@@ -114,64 +125,64 @@ def tile_picked_phpq_relu_p_kernel(tc, x_words, x_scales, w1, w2_words, w2_scale
         gather_words(1, "w1_grouped")
 
         out_rows = out.rearrange("(u p) s -> p u s", p=P)
-        h_sum = {}
-        h_mx = {}
+        chunks = S // CHUNK
+        summed = [keep.tile([P, CHUNK, PACK], BF16, name="summed%d" % c, align_bytes=64) for c in range(chunks)]
+        hidden = {}
+        for first_chunk, count in GROUPS:
+            tile = keep.tile([P, count, CHUNK * PACK], BF16, name="hidden%d" % first_chunk, align_bytes=64)
+            for i in range(count):
+                hidden[first_chunk + i] = tile[:, i, :]
+            hidden[first_chunk, count] = tile[:].rearrange("p a n -> p (a n)")
 
         def first_layer(c):
-            start, width = CHUNKS[c]
-            per_bank = BANK // width
-            woven = per_bank == PACK
-            summed = ring.tile([P, width, PACK] if woven else [P, PACK, width], BF16, name="summed", align_bytes=64)
-            for t0 in range(0, PACK, per_bank):
-                bank = psum.tile([P, per_bank, width], F32, name="bank", tag="bank%d" % H_BANKS[c][t0 // per_bank])
-                for t in range(t0, t0 + per_bank):
-                    nc.tensor.matmul_mx(
-                        out=bank[:, t - t0, :],
-                        lhsT=w1_codes[:, t, :].bitcast(FP8X4),
-                        lhsT_scale=w1_plane[:, t, :],
-                        rhs=x_codes[start].bitcast(FP8X4),
-                        rhs_scale=x_plane[:, start : start + width],
-                        start=True,
-                        stop=True,
-                    )
-                if woven:
-                    nc.vector.tensor_tensor(
-                        summed[:].rearrange("p (c i) t -> p c t i", i=4),
-                        bank[:].rearrange("p t (c i) -> p c t i", i=4),
-                        pos_views[start, t0].rearrange("p t (c i) -> p c t i", i=4),
-                        ADD,
-                    )
-                else:
-                    nc.vector.tensor_tensor(summed[:, t0 : t0 + per_bank, :], bank[:], pos_views[start, t0], ADD)
-            h_sum[c] = summed
+            bank = psum.tile([P, PACK, CHUNK], F32, name="bank", tag="bank%d" % (c % H_BANKS))
+            for t in range(PACK):
+                nc.tensor.matmul_mx(
+                    out=bank[:, t, :],
+                    lhsT=w1_codes[:, t, :].bitcast(FP8X4),
+                    lhsT_scale=w1_plane[:, t, :],
+                    rhs=x_codes[c].bitcast(FP8X4),
+                    rhs_scale=x_plane[:, c * CHUNK : (c + 1) * CHUNK],
+                    start=True,
+                    stop=True,
+                )
+            nc.vector.tensor_tensor(
+                summed[c][:].rearrange("p (c i) t -> p c t i", i=4),
+                bank[:].rearrange("p t (c i) -> p c t i", i=4),
+                pos_views[c].rearrange("p t (c i) -> p c t i", i=4),
+                ADD,
+            )
 
-        def relu(c):
-            grouped = ring.tile([P, CHUNKS[c][1], PACK], BF16, name="grouped", align_bytes=64)
-            if BANK // CHUNKS[c][1] == PACK:
-                nc.vector.tensor_scalar(grouped[:], h_sum[c][:], 0.0, None, MAX)
+        def relu(c, engine):
+            src = summed[c][:].rearrange("p n t -> p (n t)")
+            dst = hidden[c]
+            if engine == "vector":
+                nc.vector.tensor_scalar(dst, src, 0.0, None, MAX)
+            elif engine == "gpsimd":
+                nc.gpsimd.tensor_scalar(dst, src, LARGEST, 0.0, MIN, MAX)
             else:
-                dst = grouped[:].rearrange("p (c i) t -> p c t i", i=4)
-                src = h_sum[c][:].rearrange("p t (c i) -> p c t i", i=4)
                 nc.scalar.activation(dst, src, RELU)
-            h_mx[c] = grouped
 
-        h_planes = {}
-        banks = {}
+        planes = {}
 
-        def quantise(c):
-            start, width = CHUNKS[c]
-            codes = ring.tile([P, width], U32, name="h_codes", align_bytes=64)
-            plane = ring.tile([P, width], U8, name="h_plane", align_bytes=64)
-            nc.vector.quantize_mx(out=codes[:].bitcast(FP8X4), scales=plane[:], in_=h_mx[c][:].rearrange("p n t -> p (n t)"))
-            h_planes[c] = (codes, plane)
+        def quantise(d):
+            width = GROUPS[d][1] * CHUNK
+            if d < 3:
+                codes = keep.tile([P, width], U32, name="h_codes%d" % d, tag="w1_raw%d" % (d + 1), align_bytes=64)
+            else:
+                codes = keep.tile([P, width], U32, name="h_codes%d" % d, align_bytes=64)
+            plane = keep.tile([P, width], U8, name="h_plane%d" % d, align_bytes=64)
+            nc.vector.quantize_mx(out=codes[:].bitcast(FP8X4), scales=plane[:], in_=hidden[GROUPS[d]])
+            planes[d] = (codes, plane)
 
-        def multiply(c):
-            start, width = CHUNKS[c]
-            codes, plane = h_planes[c]
-            bank = psum.tile([P, N // P, width], F32, name="bank", tag="bank%d" % OUT_BANKS[c])
+        def second_layer(d):
+            width = GROUPS[d][1] * CHUNK
+            codes, plane = planes[d]
+            both = psum.tile([P, 2, width], F32, name="bank", tag="bank%d" % (3 + d))
+            banks = [both[:, u, :] for u in range(2)]
             for u in range(N // P):
                 nc.tensor.matmul_mx(
-                    out=bank[:, u, :],
+                    out=banks[u],
                     lhsT=w2_codes[:, 2 * P * u : 2 * P * (u + 1)].bitcast(FP4X4),
                     lhsT_scale=w2_plane[:, P * u : P * (u + 1)],
                     rhs=codes[:].bitcast(FP8X4),
@@ -179,33 +190,32 @@ def tile_picked_phpq_relu_p_kernel(tc, x_words, x_scales, w1, w2_words, w2_scale
                     start=True,
                     stop=True,
                 )
-            banks[c] = bank
-
-        def store(c):
-            start, width = CHUNKS[c]
-            result = ring.tile([P, N // P, width], F32, name="result", align_bytes=64)
-            if c == 3:
-                nc.vector.tensor_copy(result[:], banks[c][:])
+            start = GROUPS[d][0] * CHUNK
+            result = keep.tile([P, 2, width], F32, name="result%d" % d, align_bytes=64)
+            if d == len(GROUPS) - 1:
+                nc.vector.tensor_copy(result[:], both[:])
             else:
-                nc.scalar.copy(result[:], banks[c][:])
+                nc.scalar.copy(result[:], both[:])
             nc.sync.dma_start(out_rows[:, :, start : start + width], result[:])
 
-        for c in range(3):
+        for c in range(4):
             first_layer(c)
-            relu(c)
-        for c in range(2):
-            quantise(c)
-            multiply(c)
-            store(c)
-        first_layer(3)
-        quantise(2)
-        multiply(2)
+            relu(c, "scalar")
+        quantise(0)
         first_layer(4)
-        relu(3)
-        relu(4)
-        store(2)
-        for c in (3, 4):
-            quantise(c)
-            multiply(c)
-        for c in (3, 4):
-            store(c)
+        relu(4, "scalar")
+        second_layer(0)
+        first_layer(5)
+        relu(5, "scalar")
+        quantise(1)
+        second_layer(1)
+        first_layer(6)
+        relu(6, "scalar")
+        first_layer(7)
+        quantise(2)
+        second_layer(2)
+        relu(7, "vector")
+        quantise(3)
+        second_layer(3)
+        quantise(4)
+        second_layer(4)

@@ -23,13 +23,11 @@ LARGEST = 3.4028234663852886e38
 P = 128
 PACK = 4
 CHUNK = 128
-W1_PIECE = 128
-W1_LAST_ON_VECTOR = 20
-POS_PIECES = ((0, 128), (128, 128), (256, 256), (512, 256), (768, 256))
+POS_PIECES = ((0, 256), (256, 256), (512, 256), (768, 128), (896, 128))
 GROUPS = ((0, 2), (2, 2), (4, 2), (6, 1), (7, 1))
-GATHERS = ((0, 768), (768, 256))
+GATHERS = ((0, 256), (256, 256), (512, 512))
 H_BANKS = 3
-CLEARED_BY_VECTOR = 192
+PLAIN = 2
 
 
 def tile_picked_phpq_relu_p_kernel(tc, x_words, x_scales, w1, w2_words, w2_scales, pos, offs, out):
@@ -39,32 +37,28 @@ def tile_picked_phpq_relu_p_kernel(tc, x_words, x_scales, w1, w2_words, w2_scale
         shared = ctx.enter_context(tc.tile_pool(name="shared", bufs=1))
         psum = ctx.enter_context(tc.psum_pool(name="psum", bufs=1))
 
-        w1_rows = w1.rearrange("(p j) c -> p j c", j=PACK)
-        w1_raw = []
-
-        def load_w1(a):
-            tile = keep.tile([P, PACK, W1_PIECE], F32, name="w1_raw%d" % a, align_bytes=64)
-            nc.sync.dma_start(tile[:], w1_rows[:, :, a * W1_PIECE : (a + 1) * W1_PIECE])
-            w1_raw.append(tile)
-
-        scale_tile = shared.tile([P, T], U8, name="scale_tile", offset=T // 2, align_bytes=64)
+        scale_tile = shared.tile([P, T], U8, name="scale_tile", offset=3072, align_bytes=64)
         scale_table = scale_tile[:]
-        nc.gpsimd.memset(scale_table.bitcast(I32)[:, CLEARED_BY_VECTOR:], 0)
-        nc.vector.memset(scale_table.bitcast(I32)[:, :CLEARED_BY_VECTOR], 0)
-        load_w1(0)
+        nc.gpsimd.memset(scale_table.bitcast(I32), 0)
+        w1_raw = keep.tile([P, PACK, H], F32, name="w1_raw", align_bytes=64)
+        w1_rows = w1.rearrange("(p j) c -> p j c", j=PACK)
+        nc.sync.dma_start(w1_raw[:, :1, :], w1_rows[:, :1, :])
         offsets = keep.tile([P, S // 16], U16, name="offsets")
         nc.sync.dma_start(offsets[:], offs)
         nc.sync.dma_start(scale_tile[0:P:8, :].bitcast(I32), x_scales[0].bitcast(I32))
 
+        nc.sync.dma_start(w1_raw[:, 1:, :], w1_rows[:, 1:, :])
         word_table = keep.tile([P, T], I32, name="word_table", align_bytes=64)
         nc.sync.dma_start(word_table[:], x_words[0].rearrange("p n t -> p (n t)").bitcast(I32))
-        for a in range(1, H // W1_PIECE):
-            load_w1(a)
 
         w2_plane = keep.tile([P, N], U8, name="w2_plane", align_bytes=64)
         nc.vector.memset(w2_plane[:].bitcast(I32), 0)
         for q in range(4):
             nc.gpsimd.dma_start(w2_plane[32 * q : 32 * q + 4, :].bitcast(I32), w2_scales[0, 4 * q : 4 * q + 4, :].bitcast(I32))
+
+        zero = keep.tile([P, 16], F32, name="zero")
+        nc.vector.memset(zero[:, 0:1], 0.0)
+        nc.scalar.activation(zero[:, 8:9], zero[:, 0:1], RELU)
 
         pos_rows = pos.rearrange("(p t) s -> p t s", t=PACK)
         pos_views = {}
@@ -76,21 +70,24 @@ def tile_picked_phpq_relu_p_kernel(tc, x_words, x_scales, w1, w2_words, w2_scale
             for c0 in range(0, width, CHUNK):
                 pos_views[(start + c0) // CHUNK] = tile[:, :, c0 : c0 + CHUNK]
 
+        pos0 = keep.tile([P, PACK * POS_PIECES[0][1]], F32, name="pos0", align_bytes=64)
+        load_pos(0, pos0[:])
         x_plane = keep.tile([P, S], U8, name="x_plane", align_bytes=64)
         nc.vector.memset(x_plane[:].bitcast(I32), 0)
         picked = keep.tile([P, S], U8, name="picked", align_bytes=64)
         nc.vector.tensor_copy(picked[:], scale_table.indirect(offsets[:]))
         for r in range(4):
             nc.sync.dma_start(x_plane[r:P:32, :].bitcast(I32), picked[8 * r : P : 32, :].bitcast(I32))
-        for g, (start, width) in enumerate(POS_PIECES):
-            if g < 2:
-                room = shared.tile([P, PACK * width], F32, name="pos%d" % g, offset=g * (T + 2 * N), align_bytes=64)
-            else:
-                room = keep.tile([P, PACK * width], F32, name="pos%d" % g, tag="w1_raw%d" % (g - 1), align_bytes=64)
-            load_pos(g, room[:])
-            if g == 1:
-                w2_codes = shared.tile([P, 2 * N], U8, name="w2_codes", offset=T, align_bytes=64)
-                nc.sync.dma_start(w2_codes[:].bitcast(I32), w2_words[0].bitcast(I32))
+        pos1 = shared.tile([P, PACK * POS_PIECES[1][1]], F32, name="pos1", offset=0, align_bytes=64)
+        load_pos(1, pos1[:])
+        w2_codes = shared.tile([P, 2 * N], U8, name="w2_codes", offset=4096, align_bytes=64)
+        nc.sync.dma_start(w2_codes[:].bitcast(I32), w2_words[0].bitcast(I32))
+        pos2 = shared.tile([P, PACK * POS_PIECES[2][1]], F32, name="pos2", offset=4608, align_bytes=64)
+        load_pos(2, pos2[:])
+        pos3 = keep.tile([P, PACK * POS_PIECES[3][1]], F32, name="pos3", tag="picked", align_bytes=64)
+        load_pos(3, pos3[:])
+        pos4 = keep.tile([P, PACK * POS_PIECES[4][1]], F32, name="pos4", tag="w1_raw", align_bytes=64)
+        load_pos(4, pos4[:])
 
         x_codes = {}
 
@@ -101,18 +98,11 @@ def tile_picked_phpq_relu_p_kernel(tc, x_words, x_scales, w1, w2_words, w2_scale
             for c0 in range(0, width, CHUNK):
                 x_codes[(start + c0) // CHUNK] = tile[:, c0 : c0 + CHUNK]
 
-        gather_words(0, "x_codes")
-
         w1_grouped = keep.tile([P, PACK, P, PACK], BF16, name="w1_grouped", tag="w1_grouped", align_bytes=64)
         cast_out = w1_grouped[:].rearrange("p t m j -> p m j t")
-        per_piece = W1_PIECE // PACK
-        last = H // W1_PIECE - 1
-        for a in range(last + 1):
-            cast_in = w1_raw[a][:].rearrange("p j (m t) -> p m j t", t=PACK)
-            split = W1_LAST_ON_VECTOR if a == last else 0
-            nc.scalar.activation(cast_out[:, a * per_piece + split : (a + 1) * per_piece], cast_in[:, split:], COPY)
-            if split:
-                nc.vector.tensor_copy(cast_out[:, a * per_piece : a * per_piece + split], cast_in[:, :split])
+        cast_in = w1_raw[:].rearrange("p j (m t) -> p m j t", t=PACK)
+        nc.scalar.activation(cast_out[:, :, :, 2:], cast_in[:, :, :, 2:], COPY)
+        nc.vector.tensor_copy(cast_out[:, :, :, :2], cast_in[:, :, :, :2])
         w1_codes = keep.tile([P, PACK, P], U32, name="w1_codes", align_bytes=64)
         w1_plane = keep.tile([P, PACK, P], U8, name="w1_plane", align_bytes=64)
         for t in range(0, PACK, 2):
@@ -122,7 +112,9 @@ def tile_picked_phpq_relu_p_kernel(tc, x_words, x_scales, w1, w2_words, w2_scale
                 in_=w1_grouped[:, t : t + 2, :, :].rearrange("p t m j -> p (t m j)"),
             )
 
-        gather_words(1, "w1_grouped")
+        gather_words(0, "x_codes0")
+        gather_words(1, "x_codes1")
+        gather_words(2, "x_codes2")
 
         out_rows = out.rearrange("(u p) s -> p u s", p=P)
         chunks = S // CHUNK
@@ -133,6 +125,8 @@ def tile_picked_phpq_relu_p_kernel(tc, x_words, x_scales, w1, w2_words, w2_scale
             for i in range(count):
                 hidden[first_chunk + i] = tile[:, i, :]
             hidden[first_chunk, count] = tile[:].rearrange("p a n -> p (a n)")
+
+        plain_sum = keep.tile([P, PACK, CHUNK], BF16, name="plain_sum", align_bytes=64)
 
         def first_layer(c):
             bank = psum.tile([P, PACK, CHUNK], F32, name="bank", tag="bank%d" % (c % H_BANKS))
@@ -146,6 +140,11 @@ def tile_picked_phpq_relu_p_kernel(tc, x_words, x_scales, w1, w2_words, w2_scale
                     start=True,
                     stop=True,
                 )
+            if c == PLAIN:
+                product = keep.tile([P, PACK, CHUNK], F32, name="product", align_bytes=64)
+                nc.scalar.copy(product[:], bank[:])
+                nc.gpsimd.tensor_tensor(plain_sum[:], product[:], pos_views[c], ADD)
+                return
             nc.vector.tensor_tensor(
                 summed[c][:].rearrange("p (c i) t -> p c t i", i=4),
                 bank[:].rearrange("p t (c i) -> p c t i", i=4),
@@ -156,19 +155,30 @@ def tile_picked_phpq_relu_p_kernel(tc, x_words, x_scales, w1, w2_words, w2_scale
         def relu(c, engine):
             src = summed[c][:].rearrange("p n t -> p (n t)")
             dst = hidden[c]
-            if engine == "vector":
+            if c == PLAIN:
+                nc.scalar.activation(
+                    dst.rearrange("p (c i t) -> p c t i", i=4, t=PACK),
+                    plain_sum[:].rearrange("p t (c i) -> p c t i", i=4),
+                    RELU,
+                    bias=zero[:, 8:9],
+                )
+            elif engine == "vector":
                 nc.vector.tensor_scalar(dst, src, 0.0, None, MAX)
             elif engine == "gpsimd":
                 nc.gpsimd.tensor_scalar(dst, src, LARGEST, 0.0, MIN, MAX)
             else:
-                nc.scalar.activation(dst, src, RELU)
+                nc.scalar.activation(dst, src, RELU, bias=zero[:, 8:9])
 
         planes = {}
 
         def quantise(d):
             width = GROUPS[d][1] * CHUNK
-            if d < 3:
-                codes = keep.tile([P, width], U32, name="h_codes%d" % d, tag="w1_raw%d" % (d + 1), align_bytes=64)
+            if d < 2:
+                codes = shared.tile([P, width], U32, name="h_codes%d" % d, offset=6144 * d, align_bytes=64)
+            elif d == 2:
+                codes = keep.tile([P, width], U32, name="h_codes%d" % d, tag="picked", align_bytes=64)
+            elif d == 3:
+                codes = keep.tile([P, width], U32, name="h_codes%d" % d, tag="w1_raw", align_bytes=64)
             else:
                 codes = keep.tile([P, width], U32, name="h_codes%d" % d, align_bytes=64)
             plane = keep.tile([P, width], U8, name="h_plane%d" % d, align_bytes=64)
@@ -198,12 +208,17 @@ def tile_picked_phpq_relu_p_kernel(tc, x_words, x_scales, w1, w2_words, w2_scale
                 nc.scalar.copy(result[:], both[:])
             nc.sync.dma_start(out_rows[:, :, start : start + width], result[:])
 
-        for c in range(4):
-            first_layer(c)
-            relu(c, "scalar")
+        first_layer(0)
+        first_layer(2)
+        relu(0, "scalar")
+        first_layer(1)
+        relu(1, "scalar")
+        first_layer(3)
+        relu(2, "scalar")
+        relu(3, "gpsimd")
         quantise(0)
         first_layer(4)
-        relu(4, "scalar")
+        relu(4, "gpsimd")
         second_layer(0)
         first_layer(5)
         relu(5, "scalar")
@@ -211,11 +226,11 @@ def tile_picked_phpq_relu_p_kernel(tc, x_words, x_scales, w1, w2_words, w2_scale
         second_layer(1)
         first_layer(6)
         relu(6, "scalar")
-        first_layer(7)
         quantise(2)
+        first_layer(7)
         second_layer(2)
-        relu(7, "vector")
         quantise(3)
+        relu(7, "vector")
         second_layer(3)
         quantise(4)
         second_layer(4)

@@ -15,11 +15,9 @@ FP8X4 = mybir.dt.float8_e4m3fn_x4
 FP4X4 = mybir.dt.float4_e2m1fn_x4
 ADD = mybir.AluOpType.add
 MAX = mybir.AluOpType.max
-MIN = mybir.AluOpType.min
 RELU = mybir.ActivationFunctionType.Relu
 COPY = mybir.ActivationFunctionType.Copy
 
-LARGEST = 3.4028234663852886e38
 P = 128
 PACK = 4
 CHUNK = 128
@@ -164,8 +162,6 @@ def tile_picked_phpq_relu_p_kernel(tc, x_words, x_scales, w1, w2_words, w2_scale
                 )
             elif engine == "vector":
                 nc.vector.tensor_scalar(dst, src, 0.0, None, MAX)
-            elif engine == "gpsimd":
-                nc.gpsimd.tensor_scalar(dst, src, LARGEST, 0.0, MIN, MAX)
             else:
                 nc.scalar.activation(dst, src, RELU, bias=zero[:, 8:9])
 
@@ -173,14 +169,7 @@ def tile_picked_phpq_relu_p_kernel(tc, x_words, x_scales, w1, w2_words, w2_scale
 
         def quantise(d):
             width = GROUPS[d][1] * CHUNK
-            if d < 2:
-                codes = shared.tile([P, width], U32, name="h_codes%d" % d, offset=6144 * d, align_bytes=64)
-            elif d == 2:
-                codes = keep.tile([P, width], U32, name="h_codes%d" % d, tag="picked", align_bytes=64)
-            elif d == 3:
-                codes = keep.tile([P, width], U32, name="h_codes%d" % d, tag="w1_raw", align_bytes=64)
-            else:
-                codes = keep.tile([P, width], U32, name="h_codes%d" % d, align_bytes=64)
+            codes = keep.tile([P, width], U32, name="h_codes%d" % d, align_bytes=64)
             plane = keep.tile([P, width], U8, name="h_plane%d" % d, align_bytes=64)
             nc.vector.quantize_mx(out=codes[:].bitcast(FP8X4), scales=plane[:], in_=hidden[GROUPS[d]])
             planes[d] = (codes, plane)
@@ -215,10 +204,10 @@ def tile_picked_phpq_relu_p_kernel(tc, x_words, x_scales, w1, w2_words, w2_scale
         relu(1, "scalar")
         first_layer(3)
         relu(2, "scalar")
-        relu(3, "gpsimd")
+        relu(3, "scalar")
         quantise(0)
         first_layer(4)
-        relu(4, "gpsimd")
+        relu(4, "scalar")
         second_layer(0)
         first_layer(5)
         relu(5, "scalar")

@@ -21,11 +21,12 @@ COPY = mybir.ActivationFunctionType.Copy
 P = 128
 PACK = 4
 CHUNK = 128
-POS_PIECES = ((0, 256), (256, 256), (512, 256), (768, 128), (896, 128))
+POS_PIECES = ((0, 128), (128, 384), (512, 256), (768, 128), (896, 128))
 GROUPS = ((0, 2), (2, 2), (4, 2), (6, 1), (7, 1))
-GATHERS = ((0, 256), (256, 256), (512, 512))
+GATHERS = ((0, 768), (768, 256))
+X_FIRST = 256
 H_BANKS = 3
-PLAIN = 2
+PLAIN = 6
 
 
 def tile_picked_phpq_relu_p_kernel(tc, x_words, x_scales, w1, w2_words, w2_scales, pos, offs, out):
@@ -35,19 +36,19 @@ def tile_picked_phpq_relu_p_kernel(tc, x_words, x_scales, w1, w2_words, w2_scale
         shared = ctx.enter_context(tc.tile_pool(name="shared", bufs=1))
         psum = ctx.enter_context(tc.psum_pool(name="psum", bufs=1))
 
-        scale_tile = shared.tile([P, T], U8, name="scale_tile", offset=3072, align_bytes=64)
+        scale_tile = shared.tile([P, T], U8, name="scale_tile", offset=5120, align_bytes=64)
         scale_table = scale_tile[:]
-        nc.gpsimd.memset(scale_table.bitcast(I32), 0)
-        w1_raw = keep.tile([P, PACK, H], F32, name="w1_raw", align_bytes=64)
-        w1_rows = w1.rearrange("(p j) c -> p j c", j=PACK)
-        nc.sync.dma_start(w1_raw[:, :1, :], w1_rows[:, :1, :])
+        word_table = keep.tile([P, T], I32, name="word_table", align_bytes=64)
+        x_rows = x_words[0].rearrange("p n t -> p (n t)").bitcast(I32)
+        nc.sync.dma_start(word_table[:, :X_FIRST], x_rows[:, :X_FIRST])
         offsets = keep.tile([P, S // 16], U16, name="offsets")
         nc.sync.dma_start(offsets[:], offs)
+        nc.gpsimd.memset(scale_table.bitcast(I32)[:, T // 8 :], 0)
+        nc.vector.memset(scale_table.bitcast(I32)[:, : T // 8], 0)
         nc.sync.dma_start(scale_tile[0:P:8, :].bitcast(I32), x_scales[0].bitcast(I32))
-
-        nc.sync.dma_start(w1_raw[:, 1:, :], w1_rows[:, 1:, :])
-        word_table = keep.tile([P, T], I32, name="word_table", align_bytes=64)
-        nc.sync.dma_start(word_table[:], x_words[0].rearrange("p n t -> p (n t)").bitcast(I32))
+        nc.sync.dma_start(word_table[:, X_FIRST:], x_rows[:, X_FIRST:])
+        w1_raw = keep.tile([P, PACK, H], F32, name="w1_raw", align_bytes=64)
+        nc.sync.dma_start(w1_raw[:], w1.rearrange("(p j) c -> p j c", j=PACK))
 
         w2_plane = keep.tile([P, N], U8, name="w2_plane", align_bytes=64)
         nc.vector.memset(w2_plane[:].bitcast(I32), 0)
@@ -78,9 +79,9 @@ def tile_picked_phpq_relu_p_kernel(tc, x_words, x_scales, w1, w2_words, w2_scale
             nc.sync.dma_start(x_plane[r:P:32, :].bitcast(I32), picked[8 * r : P : 32, :].bitcast(I32))
         pos1 = shared.tile([P, PACK * POS_PIECES[1][1]], F32, name="pos1", offset=0, align_bytes=64)
         load_pos(1, pos1[:])
-        w2_codes = shared.tile([P, 2 * N], U8, name="w2_codes", offset=4096, align_bytes=64)
+        w2_codes = shared.tile([P, 2 * N], U8, name="w2_codes", offset=6144, align_bytes=64)
         nc.sync.dma_start(w2_codes[:].bitcast(I32), w2_words[0].bitcast(I32))
-        pos2 = shared.tile([P, PACK * POS_PIECES[2][1]], F32, name="pos2", offset=4608, align_bytes=64)
+        pos2 = shared.tile([P, PACK * POS_PIECES[2][1]], F32, name="pos2", offset=6656, align_bytes=64)
         load_pos(2, pos2[:])
         pos3 = keep.tile([P, PACK * POS_PIECES[3][1]], F32, name="pos3", tag="picked", align_bytes=64)
         load_pos(3, pos3[:])
@@ -96,6 +97,8 @@ def tile_picked_phpq_relu_p_kernel(tc, x_words, x_scales, w1, w2_words, w2_scale
             for c0 in range(0, width, CHUNK):
                 x_codes[(start + c0) // CHUNK] = tile[:, c0 : c0 + CHUNK]
 
+        gather_words(0, "x_codes")
+
         w1_grouped = keep.tile([P, PACK, P, PACK], BF16, name="w1_grouped", tag="w1_grouped", align_bytes=64)
         cast_out = w1_grouped[:].rearrange("p t m j -> p m j t")
         cast_in = w1_raw[:].rearrange("p j (m t) -> p m j t", t=PACK)
@@ -110,9 +113,7 @@ def tile_picked_phpq_relu_p_kernel(tc, x_words, x_scales, w1, w2_words, w2_scale
                 in_=w1_grouped[:, t : t + 2, :, :].rearrange("p t m j -> p (t m j)"),
             )
 
-        gather_words(0, "x_codes0")
-        gather_words(1, "x_codes1")
-        gather_words(2, "x_codes2")
+        gather_words(1, "w1_grouped")
 
         out_rows = out.rearrange("(u p) s -> p u s", p=P)
         chunks = S // CHUNK
@@ -123,8 +124,6 @@ def tile_picked_phpq_relu_p_kernel(tc, x_words, x_scales, w1, w2_words, w2_scale
             for i in range(count):
                 hidden[first_chunk + i] = tile[:, i, :]
             hidden[first_chunk, count] = tile[:].rearrange("p a n -> p (a n)")
-
-        plain_sum = keep.tile([P, PACK, CHUNK], BF16, name="plain_sum", align_bytes=64)
 
         def first_layer(c):
             bank = psum.tile([P, PACK, CHUNK], F32, name="bank", tag="bank%d" % (c % H_BANKS))
@@ -138,10 +137,8 @@ def tile_picked_phpq_relu_p_kernel(tc, x_words, x_scales, w1, w2_words, w2_scale
                     start=True,
                     stop=True,
                 )
-            if c == PLAIN:
-                product = keep.tile([P, PACK, CHUNK], F32, name="product", align_bytes=64)
-                nc.scalar.copy(product[:], bank[:])
-                nc.gpsimd.tensor_tensor(plain_sum[:], product[:], pos_views[c], ADD)
+            if c < PLAIN:
+                nc.vector.tensor_tensor(summed[c][:].rearrange("p n t -> p (n t)").rearrange("p (t n) -> p t n", t=PACK), bank[:], pos_views[c], ADD)
                 return
             nc.vector.tensor_tensor(
                 summed[c][:].rearrange("p (c i) t -> p c t i", i=4),
@@ -153,10 +150,10 @@ def tile_picked_phpq_relu_p_kernel(tc, x_words, x_scales, w1, w2_words, w2_scale
         def relu(c, engine):
             src = summed[c][:].rearrange("p n t -> p (n t)")
             dst = hidden[c]
-            if c == PLAIN:
+            if c < PLAIN:
                 nc.scalar.activation(
                     dst.rearrange("p (c i t) -> p c t i", i=4, t=PACK),
-                    plain_sum[:].rearrange("p t (c i) -> p c t i", i=4),
+                    src.rearrange("p (t c i) -> p c t i", i=4, t=PACK),
                     RELU,
                     bias=zero[:, 8:9],
                 )
@@ -169,7 +166,14 @@ def tile_picked_phpq_relu_p_kernel(tc, x_words, x_scales, w1, w2_words, w2_scale
 
         def quantise(d):
             width = GROUPS[d][1] * CHUNK
-            codes = keep.tile([P, width], U32, name="h_codes%d" % d, align_bytes=64)
+            if d < 2:
+                codes = shared.tile([P, width], U32, name="h_codes%d" % d, offset=8192 * d, align_bytes=64)
+            elif d == 2:
+                codes = keep.tile([P, width], U32, name="h_codes%d" % d, tag="picked", align_bytes=64)
+            elif d == 3:
+                codes = keep.tile([P, width], U32, name="h_codes%d" % d, tag="w1_raw", align_bytes=64)
+            else:
+                codes = keep.tile([P, width], U32, name="h_codes%d" % d, align_bytes=64)
             plane = keep.tile([P, width], U8, name="h_plane%d" % d, align_bytes=64)
             nc.vector.quantize_mx(out=codes[:].bitcast(FP8X4), scales=plane[:], in_=hidden[GROUPS[d]])
             planes[d] = (codes, plane)
@@ -197,14 +201,9 @@ def tile_picked_phpq_relu_p_kernel(tc, x_words, x_scales, w1, w2_words, w2_scale
                 nc.scalar.copy(result[:], both[:])
             nc.sync.dma_start(out_rows[:, :, start : start + width], result[:])
 
-        first_layer(0)
-        first_layer(2)
-        relu(0, "scalar")
-        first_layer(1)
-        relu(1, "scalar")
-        first_layer(3)
-        relu(2, "scalar")
-        relu(3, "scalar")
+        for c in range(4):
+            first_layer(c)
+            relu(c, "scalar")
         quantise(0)
         first_layer(4)
         relu(4, "scalar")
@@ -214,10 +213,10 @@ def tile_picked_phpq_relu_p_kernel(tc, x_words, x_scales, w1, w2_words, w2_scale
         quantise(1)
         second_layer(1)
         first_layer(6)
-        relu(6, "scalar")
         quantise(2)
-        first_layer(7)
+        relu(6, "vector")
         second_layer(2)
+        first_layer(7)
         quantise(3)
         relu(7, "vector")
         second_layer(3)

@@ -23,9 +23,11 @@ PACK = 4
 CHUNK = 128
 POS_PIECES = ((0, 128), (128, 384), (512, 256), (768, 128), (896, 128))
 GROUPS = ((0, 2), (2, 2), (4, 2), (6, 1), (7, 1))
-GATHERS = ((0, 768), (768, 256))
+GATHERS = ((0, 512), (512, 256), (768, 256))
 X_FIRST = 256
 H_BANKS = 3
+WARM_UPS = 3
+WARM_WIDTH = 512
 PLAIN = 6
 
 
@@ -83,10 +85,6 @@ def tile_picked_phpq_relu_p_kernel(tc, x_words, x_scales, w1, w2_words, w2_scale
         nc.sync.dma_start(w2_codes[:].bitcast(I32), w2_words[0].bitcast(I32))
         pos2 = shared.tile([P, PACK * POS_PIECES[2][1]], F32, name="pos2", offset=6656, align_bytes=64)
         load_pos(2, pos2[:])
-        pos3 = keep.tile([P, PACK * POS_PIECES[3][1]], F32, name="pos3", tag="picked", align_bytes=64)
-        load_pos(3, pos3[:])
-        pos4 = keep.tile([P, PACK * POS_PIECES[4][1]], F32, name="pos4", tag="w1_raw", align_bytes=64)
-        load_pos(4, pos4[:])
 
         x_codes = {}
 
@@ -96,8 +94,22 @@ def tile_picked_phpq_relu_p_kernel(tc, x_words, x_scales, w1, w2_words, w2_scale
             nc.vector.tensor_copy(tile[:], word_table[:].bitcast(U32).indirect(offsets[:, start // 16 : (start + width) // 16]))
             for c0 in range(0, width, CHUNK):
                 x_codes[(start + c0) // CHUNK] = tile[:, c0 : c0 + CHUNK]
+            return tile
 
-        gather_words(0, "x_codes")
+        x_first = gather_words(0, "x_codes0")
+        gather_words(1, "x_codes1")
+
+        idle = psum.tile([P, WARM_WIDTH], F32, name="bank", tag="bank7")
+        for i in range(WARM_UPS):
+            nc.tensor.matmul_mx(
+                out=idle[:],
+                lhsT=x_codes[0].bitcast(FP8X4),
+                lhsT_scale=picked[:, :CHUNK],
+                rhs=x_first[:, :WARM_WIDTH].bitcast(FP8X4),
+                rhs_scale=picked[:, :WARM_WIDTH],
+                start=True,
+                stop=True,
+            )
 
         w1_grouped = keep.tile([P, PACK, P, PACK], BF16, name="w1_grouped", tag="w1_grouped", align_bytes=64)
         cast_out = w1_grouped[:].rearrange("p t m j -> p m j t")
@@ -113,7 +125,11 @@ def tile_picked_phpq_relu_p_kernel(tc, x_words, x_scales, w1, w2_words, w2_scale
                 in_=w1_grouped[:, t : t + 2, :, :].rearrange("p t m j -> p (t m j)"),
             )
 
-        gather_words(1, "w1_grouped")
+        gather_words(2, "w1_grouped")
+        pos3 = keep.tile([P, PACK * POS_PIECES[3][1]], F32, name="pos3", tag="picked", align_bytes=64)
+        load_pos(3, pos3[:])
+        pos4 = keep.tile([P, PACK * POS_PIECES[4][1]], F32, name="pos4", tag="w1_raw", align_bytes=64)
+        load_pos(4, pos4[:])
 
         out_rows = out.rearrange("(u p) s -> p u s", p=P)
         chunks = S // CHUNK

@@ -20,15 +20,19 @@ COPY = mybir.ActivationFunctionType.Copy
 
 P = 128
 PACK = 4
+LIST_ROWS = 16
 CHUNK = 128
-POS_PIECES = ((0, 128), (128, 384), (512, 256), (768, 128), (896, 128))
-GROUPS = ((0, 2), (2, 2), (4, 2), (6, 1), (7, 1))
-GATHERS = ((0, 512), (512, 256), (768, 256))
+CHUNKS = S // CHUNK
+WEAVE = 4
+
 X_FIRST = 256
+POS_LOADS = ((0, 128), (128, 384), (512, 256), (768, 256))
+GATHERS = ((0, 512), (512, 256), (768, 256))
+GROUPS = ((0, 2), (2, 2), (4, 2), (6, 1), (7, 1))
+FIRST_ON_VECTOR = 6
 H_BANKS = 3
 WARM_UPS = 3
 WARM_WIDTH = 512
-PLAIN = 6
 
 
 def tile_picked_phpq_relu_p_kernel(tc, x_words, x_scales, w1, w2_words, w2_scales, pos, offs, out):
@@ -38,18 +42,20 @@ def tile_picked_phpq_relu_p_kernel(tc, x_words, x_scales, w1, w2_words, w2_scale
         shared = ctx.enter_context(tc.tile_pool(name="shared", bufs=1))
         psum = ctx.enter_context(tc.psum_pool(name="psum", bufs=1))
 
-        scale_tile = shared.tile([P, T], U8, name="scale_tile", offset=5120, align_bytes=64)
-        scale_table = scale_tile[:]
+        w2_at = 4 * PACK * POS_LOADS[1][1]
+        scale_table = shared.tile([P, T], U8, name="scale_table", offset=w2_at - T // 2, align_bytes=64)
+
         word_table = keep.tile([P, T], I32, name="word_table", align_bytes=64)
         x_rows = x_words[0].rearrange("p n t -> p (n t)").bitcast(I32)
         nc.sync.dma_start(word_table[:, :X_FIRST], x_rows[:, :X_FIRST])
-        offsets = keep.tile([P, S // 16], U16, name="offsets")
+        offsets = keep.tile([P, S // LIST_ROWS], U16, name="offsets")
         nc.sync.dma_start(offsets[:], offs)
-        nc.gpsimd.memset(scale_table.bitcast(I32)[:, T // 8 :], 0)
-        nc.vector.memset(scale_table.bitcast(I32)[:, : T // 8], 0)
-        nc.sync.dma_start(scale_tile[0:P:8, :].bitcast(I32), x_scales[0].bitcast(I32))
+        half = T // 4 // 2
+        nc.gpsimd.memset(scale_table[:].bitcast(I32)[:, half:], 0)
+        nc.vector.memset(scale_table[:].bitcast(I32)[:, :half], 0)
+        nc.sync.dma_start(scale_table[0:P:8, :].bitcast(I32), x_scales[0].bitcast(I32))
         nc.sync.dma_start(word_table[:, X_FIRST:], x_rows[:, X_FIRST:])
-        w1_raw = keep.tile([P, PACK, H], F32, name="w1_raw", align_bytes=64)
+        w1_raw = keep.tile([P, PACK, H], F32, name="w1_raw", tag="w1_raw", align_bytes=64)
         nc.sync.dma_start(w1_raw[:], w1.rearrange("(p j) c -> p j c", j=PACK))
 
         w2_plane = keep.tile([P, N], U8, name="w2_plane", align_bytes=64)
@@ -57,53 +63,55 @@ def tile_picked_phpq_relu_p_kernel(tc, x_words, x_scales, w1, w2_words, w2_scale
         for q in range(4):
             nc.gpsimd.dma_start(w2_plane[32 * q : 32 * q + 4, :].bitcast(I32), w2_scales[0, 4 * q : 4 * q + 4, :].bitcast(I32))
 
-        zero = keep.tile([P, 16], F32, name="zero")
-        nc.vector.memset(zero[:, 0:1], 0.0)
-        nc.scalar.activation(zero[:, 8:9], zero[:, 0:1], RELU)
+        zeros = keep.tile([P, 16], F32, name="zeros")
+        zero_bias = zeros[:, 8:9]
+        nc.vector.memset(zeros[:, 0:1], 0.0)
+        nc.scalar.activation(zero_bias, zeros[:, 0:1], RELU)
 
         pos_rows = pos.rearrange("(p t) s -> p t s", t=PACK)
-        pos_views = {}
+        pos_chunk = {}
 
-        def load_pos(g, room):
-            start, width = POS_PIECES[g]
-            tile = room.rearrange("p (t n) -> p t n", t=PACK)
-            nc.sync.dma_start(tile, pos_rows[:, :, start : start + width])
+        def load_pos(g, pool, **place):
+            start, width = POS_LOADS[g]
+            flat = pool.tile([P, PACK * width], F32, name="pos%d" % g, align_bytes=64, **place)
+            rows = flat[:].rearrange("p (t n) -> p t n", t=PACK)
+            nc.sync.dma_start(rows, pos_rows[:, :, start : start + width])
             for c0 in range(0, width, CHUNK):
-                pos_views[(start + c0) // CHUNK] = tile[:, :, c0 : c0 + CHUNK]
+                pos_chunk[(start + c0) // CHUNK] = rows[:, :, c0 : c0 + CHUNK]
 
-        pos0 = keep.tile([P, PACK * POS_PIECES[0][1]], F32, name="pos0", align_bytes=64)
-        load_pos(0, pos0[:])
+        load_pos(0, keep)
+
         x_plane = keep.tile([P, S], U8, name="x_plane", align_bytes=64)
         nc.vector.memset(x_plane[:].bitcast(I32), 0)
-        picked = keep.tile([P, S], U8, name="picked", align_bytes=64)
-        nc.vector.tensor_copy(picked[:], scale_table.indirect(offsets[:]))
+        picked = keep.tile([P, S], U8, name="picked", tag="picked", align_bytes=64)
+        nc.vector.tensor_copy(picked[:], scale_table[:].indirect(offsets[:]))
         for r in range(4):
             nc.sync.dma_start(x_plane[r:P:32, :].bitcast(I32), picked[8 * r : P : 32, :].bitcast(I32))
-        pos1 = shared.tile([P, PACK * POS_PIECES[1][1]], F32, name="pos1", offset=0, align_bytes=64)
-        load_pos(1, pos1[:])
-        w2_codes = shared.tile([P, 2 * N], U8, name="w2_codes", offset=6144, align_bytes=64)
-        nc.sync.dma_start(w2_codes[:].bitcast(I32), w2_words[0].bitcast(I32))
-        pos2 = shared.tile([P, PACK * POS_PIECES[2][1]], F32, name="pos2", offset=6656, align_bytes=64)
-        load_pos(2, pos2[:])
 
-        x_codes = {}
+        load_pos(1, shared, offset=0)
+        w2_codes = shared.tile([P, 2 * N], U8, name="w2_codes", offset=w2_at, align_bytes=64)
+        nc.sync.dma_start(w2_codes[:].bitcast(I32), w2_words[0].bitcast(I32))
+        load_pos(2, shared, offset=w2_at + 2 * N)
+
+        x_chunk = {}
 
         def gather_words(g, tag):
             start, width = GATHERS[g]
-            tile = keep.tile([P, width], U32, name=tag, tag=tag, align_bytes=64)
-            nc.vector.tensor_copy(tile[:], word_table[:].bitcast(U32).indirect(offsets[:, start // 16 : (start + width) // 16]))
+            words = keep.tile([P, width], U32, name="x_codes%d" % g, tag=tag, align_bytes=64)
+            entries = offsets[:, start // LIST_ROWS : (start + width) // LIST_ROWS]
+            nc.vector.tensor_copy(words[:], word_table[:].bitcast(U32).indirect(entries))
             for c0 in range(0, width, CHUNK):
-                x_codes[(start + c0) // CHUNK] = tile[:, c0 : c0 + CHUNK]
-            return tile
+                x_chunk[(start + c0) // CHUNK] = words[:, c0 : c0 + CHUNK]
+            return words
 
         x_first = gather_words(0, "x_codes0")
         gather_words(1, "x_codes1")
 
-        idle = psum.tile([P, WARM_WIDTH], F32, name="bank", tag="bank7")
-        for i in range(WARM_UPS):
+        unread = psum.tile([P, WARM_WIDTH], F32, name="unread", tag="bank%d" % (H_BANKS + len(GROUPS) - 1))
+        for repeat in range(WARM_UPS):
             nc.tensor.matmul_mx(
-                out=idle[:],
-                lhsT=x_codes[0].bitcast(FP8X4),
+                out=unread[:],
+                lhsT=x_chunk[0].bitcast(FP8X4),
                 lhsT_scale=picked[:, :CHUNK],
                 rhs=x_first[:, :WARM_WIDTH].bitcast(FP8X4),
                 rhs_scale=picked[:, :WARM_WIDTH],
@@ -111,7 +119,7 @@ def tile_picked_phpq_relu_p_kernel(tc, x_words, x_scales, w1, w2_words, w2_scale
                 stop=True,
             )
 
-        w1_grouped = keep.tile([P, PACK, P, PACK], BF16, name="w1_grouped", tag="w1_grouped", align_bytes=64)
+        w1_grouped = keep.tile([P, PACK, P, PACK], BF16, name="w1_grouped", align_bytes=64)
         cast_out = w1_grouped[:].rearrange("p t m j -> p m j t")
         cast_in = w1_raw[:].rearrange("p j (m t) -> p m j t", t=PACK)
         nc.scalar.activation(cast_out[:, :, :, 2:], cast_in[:, :, :, 2:], COPY)
@@ -125,83 +133,62 @@ def tile_picked_phpq_relu_p_kernel(tc, x_words, x_scales, w1, w2_words, w2_scale
                 in_=w1_grouped[:, t : t + 2, :, :].rearrange("p t m j -> p (t m j)"),
             )
 
-        gather_words(2, "w1_grouped")
-        pos3 = keep.tile([P, PACK * POS_PIECES[3][1]], F32, name="pos3", tag="picked", align_bytes=64)
-        load_pos(3, pos3[:])
-        pos4 = keep.tile([P, PACK * POS_PIECES[4][1]], F32, name="pos4", tag="w1_raw", align_bytes=64)
-        load_pos(4, pos4[:])
+        gather_words(2, "w1_raw")
+        load_pos(3, keep, tag="picked")
 
         out_rows = out.rearrange("(u p) s -> p u s", p=P)
-        chunks = S // CHUNK
-        summed = [keep.tile([P, CHUNK, PACK], BF16, name="summed%d" % c, align_bytes=64) for c in range(chunks)]
-        hidden = {}
+        summed = [keep.tile([P, CHUNK * PACK], BF16, name="summed%d" % c, align_bytes=64) for c in range(CHUNKS)]
+        h_group = []
+        h_chunk = []
         for first_chunk, count in GROUPS:
-            tile = keep.tile([P, count, CHUNK * PACK], BF16, name="hidden%d" % first_chunk, align_bytes=64)
-            for i in range(count):
-                hidden[first_chunk + i] = tile[:, i, :]
-            hidden[first_chunk, count] = tile[:].rearrange("p a n -> p (a n)")
+            hidden = keep.tile([P, count, CHUNK * PACK], BF16, name="hidden%d" % first_chunk, align_bytes=64)
+            h_group.append(hidden[:].rearrange("p a n -> p (a n)"))
+            h_chunk.extend(hidden[:, a, :] for a in range(count))
+
+        def woven(flat):
+            return flat.rearrange("p (c i t) -> p c t i", i=WEAVE, t=PACK)
+
+        def side_by_side(rows):
+            return rows.rearrange("p t (c i) -> p c t i", i=WEAVE)
 
         def first_layer(c):
-            bank = psum.tile([P, PACK, CHUNK], F32, name="bank", tag="bank%d" % (c % H_BANKS))
+            bank = psum.tile([P, PACK, CHUNK], F32, name="h_bank", tag="bank%d" % (c % H_BANKS))
             for t in range(PACK):
                 nc.tensor.matmul_mx(
                     out=bank[:, t, :],
                     lhsT=w1_codes[:, t, :].bitcast(FP8X4),
                     lhsT_scale=w1_plane[:, t, :],
-                    rhs=x_codes[c].bitcast(FP8X4),
+                    rhs=x_chunk[c].bitcast(FP8X4),
                     rhs_scale=x_plane[:, c * CHUNK : (c + 1) * CHUNK],
                     start=True,
                     stop=True,
                 )
-            if c < PLAIN:
-                nc.vector.tensor_tensor(summed[c][:].rearrange("p n t -> p (n t)").rearrange("p (t n) -> p t n", t=PACK), bank[:], pos_views[c], ADD)
-                return
-            nc.vector.tensor_tensor(
-                summed[c][:].rearrange("p (c i) t -> p c t i", i=4),
-                bank[:].rearrange("p t (c i) -> p c t i", i=4),
-                pos_views[c].rearrange("p t (c i) -> p c t i", i=4),
-                ADD,
-            )
-
-        def relu(c, engine):
-            src = summed[c][:].rearrange("p n t -> p (n t)")
-            dst = hidden[c]
-            if c < PLAIN:
-                nc.scalar.activation(
-                    dst.rearrange("p (c i t) -> p c t i", i=4, t=PACK),
-                    src.rearrange("p (t c i) -> p c t i", i=4, t=PACK),
-                    RELU,
-                    bias=zero[:, 8:9],
-                )
-            elif engine == "vector":
-                nc.vector.tensor_scalar(dst, src, 0.0, None, MAX)
+            if c < FIRST_ON_VECTOR:
+                rows = summed[c][:].rearrange("p (t n) -> p t n", t=PACK)
+                nc.vector.tensor_tensor(rows, bank[:], pos_chunk[c], ADD)
+                nc.scalar.activation(woven(h_chunk[c]), side_by_side(rows), RELU, bias=zero_bias)
             else:
-                nc.scalar.activation(dst, src, RELU, bias=zero[:, 8:9])
+                nc.vector.tensor_tensor(woven(summed[c][:]), side_by_side(bank[:]), side_by_side(pos_chunk[c]), ADD)
 
-        planes = {}
+        def relu_on_vector(c):
+            nc.vector.tensor_scalar(h_chunk[c], summed[c][:], 0.0, None, MAX)
+
+        h_mx = {}
 
         def quantise(d):
             width = GROUPS[d][1] * CHUNK
-            if d < 2:
-                codes = shared.tile([P, width], U32, name="h_codes%d" % d, offset=8192 * d, align_bytes=64)
-            elif d == 2:
-                codes = keep.tile([P, width], U32, name="h_codes%d" % d, tag="picked", align_bytes=64)
-            elif d == 3:
-                codes = keep.tile([P, width], U32, name="h_codes%d" % d, tag="w1_raw", align_bytes=64)
-            else:
-                codes = keep.tile([P, width], U32, name="h_codes%d" % d, align_bytes=64)
+            codes = keep.tile([P, width], U32, name="h_codes%d" % d, align_bytes=64)
             plane = keep.tile([P, width], U8, name="h_plane%d" % d, align_bytes=64)
-            nc.vector.quantize_mx(out=codes[:].bitcast(FP8X4), scales=plane[:], in_=hidden[GROUPS[d]])
-            planes[d] = (codes, plane)
+            nc.vector.quantize_mx(out=codes[:].bitcast(FP8X4), scales=plane[:], in_=h_group[d])
+            h_mx[d] = (codes, plane)
 
         def second_layer(d):
-            width = GROUPS[d][1] * CHUNK
-            codes, plane = planes[d]
-            both = psum.tile([P, 2, width], F32, name="bank", tag="bank%d" % (3 + d))
-            banks = [both[:, u, :] for u in range(2)]
+            start, width = GROUPS[d][0] * CHUNK, GROUPS[d][1] * CHUNK
+            codes, plane = h_mx[d]
+            bank = psum.tile([P, N // P, width], F32, name="out_bank", tag="bank%d" % (H_BANKS + d))
             for u in range(N // P):
                 nc.tensor.matmul_mx(
-                    out=banks[u],
+                    out=bank[:, u, :],
                     lhsT=w2_codes[:, 2 * P * u : 2 * P * (u + 1)].bitcast(FP4X4),
                     lhsT_scale=w2_plane[:, P * u : P * (u + 1)],
                     rhs=codes[:].bitcast(FP8X4),
@@ -209,32 +196,28 @@ def tile_picked_phpq_relu_p_kernel(tc, x_words, x_scales, w1, w2_words, w2_scale
                     start=True,
                     stop=True,
                 )
-            start = GROUPS[d][0] * CHUNK
-            result = keep.tile([P, 2, width], F32, name="result%d" % d, align_bytes=64)
+            result = keep.tile([P, N // P, width], F32, name="result%d" % d, align_bytes=64)
             if d == len(GROUPS) - 1:
-                nc.vector.tensor_copy(result[:], both[:])
+                nc.vector.tensor_copy(result[:], bank[:])
             else:
-                nc.scalar.copy(result[:], both[:])
+                nc.scalar.copy(result[:], bank[:])
             nc.sync.dma_start(out_rows[:, :, start : start + width], result[:])
 
         for c in range(4):
             first_layer(c)
-            relu(c, "scalar")
         quantise(0)
         first_layer(4)
-        relu(4, "scalar")
         second_layer(0)
         first_layer(5)
-        relu(5, "scalar")
         quantise(1)
         second_layer(1)
         first_layer(6)
         quantise(2)
-        relu(6, "vector")
+        relu_on_vector(6)
         second_layer(2)
         first_layer(7)
         quantise(3)
-        relu(7, "vector")
+        relu_on_vector(7)
         second_layer(3)
         quantise(4)
         second_layer(4)

@@ -26,7 +26,7 @@ CHUNKS = S // CHUNK
 WEAVE = 4
 
 X_FIRST = 256
-POS_LOADS = ((0, 128), (128, 384), (512, 256), (768, 256))
+POS_LOADS = ((0, 256), (256, 256), (512, 256), (768, 256))
 GATHERS = ((0, 512), (512, 256), (768, 256))
 GROUPS = ((0, 2), (2, 2), (4, 2), (6, 1), (7, 1))
 FIRST_ON_VECTOR = 6
@@ -42,7 +42,7 @@ def tile_picked_phpq_relu_p_kernel(tc, x_words, x_scales, w1, w2_words, w2_scale
         shared = ctx.enter_context(tc.tile_pool(name="shared", bufs=1))
         psum = ctx.enter_context(tc.psum_pool(name="psum", bufs=1))
 
-        w2_at = 4 * PACK * POS_LOADS[1][1]
+        w2_at = 4 * PACK * POS_LOADS[0][1]
         scale_table = shared.tile([P, T], U8, name="scale_table", offset=w2_at - T // 2, align_bytes=64)
 
         word_table = keep.tile([P, T], I32, name="word_table", align_bytes=64)
@@ -79,19 +79,19 @@ def tile_picked_phpq_relu_p_kernel(tc, x_words, x_scales, w1, w2_words, w2_scale
             for c0 in range(0, width, CHUNK):
                 pos_chunk[(start + c0) // CHUNK] = rows[:, :, c0 : c0 + CHUNK]
 
-        load_pos(0, keep)
 
         x_plane = keep.tile([P, S], U8, name="x_plane", align_bytes=64)
         nc.vector.memset(x_plane[:].bitcast(I32), 0)
-        picked = keep.tile([P, S], U8, name="picked", tag="picked", align_bytes=64)
+        late_at = w2_at + 2 * N + 4 * PACK * (POS_LOADS[1][1] + POS_LOADS[2][1])
+        picked = shared.tile([P, S], U8, name="picked", offset=late_at - S // 2, align_bytes=64)
         nc.vector.tensor_copy(picked[:], scale_table[:].indirect(offsets[:]))
         for r in range(4):
             nc.sync.dma_start(x_plane[r:P:32, :].bitcast(I32), picked[8 * r : P : 32, :].bitcast(I32))
 
-        load_pos(1, shared, offset=0)
+        load_pos(0, shared, offset=0)
+        load_pos(1, shared, offset=w2_at + 2 * N)
         w2_codes = shared.tile([P, 2 * N], U8, name="w2_codes", offset=w2_at, align_bytes=64)
         nc.sync.dma_start(w2_codes[:].bitcast(I32), w2_words[0].bitcast(I32))
-        load_pos(2, shared, offset=w2_at + 2 * N)
 
         x_chunk = {}
 
@@ -134,7 +134,8 @@ def tile_picked_phpq_relu_p_kernel(tc, x_words, x_scales, w1, w2_words, w2_scale
             )
 
         gather_words(2, "w1_raw")
-        load_pos(3, keep, tag="picked")
+        load_pos(2, shared, offset=late_at - 4 * PACK * POS_LOADS[2][1])
+        load_pos(3, shared, offset=late_at)
 
         out_rows = out.rearrange("(u p) s -> p u s", p=P)
         summed = [keep.tile([P, CHUNK * PACK], BF16, name="summed%d" % c, align_bytes=64) for c in range(CHUNKS)]

@@ -24,10 +24,11 @@ LIST_ROWS = 16
 CHUNK = 128
 CHUNKS = S // CHUNK
 WEAVE = 4
+WEAVE_ADD = 2
 
 X_FIRST = 256
 POS_LOADS = ((0, 256), (256, 256), (512, 256), (768, 256))
-GATHERS = ((0, 512), (512, 256), (768, 256))
+GATHERS = ((0, 512), (512, 512))
 GROUPS = ((0, 2), (2, 2), (4, 2), (6, 1), (7, 1))
 FIRST_ON_VECTOR = 6
 H_BANKS = 3
@@ -50,9 +51,7 @@ def tile_picked_phpq_relu_p_kernel(tc, x_words, x_scales, w1, w2_words, w2_scale
         nc.sync.dma_start(word_table[:, :X_FIRST], x_rows[:, :X_FIRST])
         offsets = keep.tile([P, S // LIST_ROWS], U16, name="offsets")
         nc.sync.dma_start(offsets[:], offs)
-        half = T // 4 // 2
-        nc.gpsimd.memset(scale_table[:].bitcast(I32)[:, half:], 0)
-        nc.vector.memset(scale_table[:].bitcast(I32)[:, :half], 0)
+        nc.vector.memset(scale_table[:].bitcast(I32), 0)
         nc.sync.dma_start(scale_table[0:P:8, :].bitcast(I32), x_scales[0].bitcast(I32))
         nc.sync.dma_start(word_table[:, X_FIRST:], x_rows[:, X_FIRST:])
         w1_raw = keep.tile([P, PACK, H], F32, name="w1_raw", tag="w1_raw", align_bytes=64)
@@ -133,7 +132,6 @@ def tile_picked_phpq_relu_p_kernel(tc, x_words, x_scales, w1, w2_words, w2_scale
                 in_=w1_grouped[:, t : t + 2, :, :].rearrange("p t m j -> p (t m j)"),
             )
 
-        gather_words(2, "w1_raw")
         load_pos(2, shared, offset=late_at - 4 * PACK * POS_LOADS[2][1])
         load_pos(3, shared, offset=late_at)
 
@@ -146,17 +144,20 @@ def tile_picked_phpq_relu_p_kernel(tc, x_words, x_scales, w1, w2_words, w2_scale
             h_group.append(hidden[:].rearrange("p a n -> p (a n)"))
             h_chunk.extend(hidden[:, a, :] for a in range(count))
 
-        def woven(flat):
-            return flat.rearrange("p (c i t) -> p c t i", i=WEAVE, t=PACK)
+        def woven(flat, run=WEAVE):
+            return flat.rearrange("p (c i t) -> p c t i", i=run, t=PACK)
 
-        def side_by_side(rows):
-            return rows.rearrange("p t (c i) -> p c t i", i=WEAVE)
+        def side_by_side(rows, run=WEAVE):
+            return rows.rearrange("p t (c i) -> p c t i", i=run)
 
         def first_layer(c):
             bank = psum.tile([P, PACK, CHUNK], F32, name="h_bank", tag="bank%d" % (c % H_BANKS))
+            early = bank
+            if c == 0:
+                early = psum.tile([P, PACK, CHUNK], F32, name="early_bank", tag="bank%d" % (H_BANKS + len(GROUPS) - 2))
             for t in range(PACK):
                 nc.tensor.matmul_mx(
-                    out=bank[:, t, :],
+                    out=(early if t < 2 else bank)[:, t, :],
                     lhsT=w1_codes[:, t, :].bitcast(FP8X4),
                     lhsT_scale=w1_plane[:, t, :],
                     rhs=x_chunk[c].bitcast(FP8X4),
@@ -166,10 +167,14 @@ def tile_picked_phpq_relu_p_kernel(tc, x_words, x_scales, w1, w2_words, w2_scale
                 )
             if c < FIRST_ON_VECTOR:
                 rows = summed[c][:].rearrange("p (t n) -> p t n", t=PACK)
-                nc.vector.tensor_tensor(rows, bank[:], pos_chunk[c], ADD)
+                if c == 0:
+                    nc.vector.tensor_tensor(rows[:, :2, :], early[:, :2, :], pos_chunk[c][:, :2, :], ADD)
+                    nc.vector.tensor_tensor(rows[:, 2:, :], bank[:, 2:, :], pos_chunk[c][:, 2:, :], ADD)
+                else:
+                    nc.vector.tensor_tensor(rows, bank[:], pos_chunk[c], ADD)
                 nc.scalar.activation(woven(h_chunk[c]), side_by_side(rows), RELU, bias=zero_bias)
             else:
-                nc.vector.tensor_tensor(woven(summed[c][:]), side_by_side(bank[:]), side_by_side(pos_chunk[c]), ADD)
+                nc.vector.tensor_tensor(woven(summed[c][:], WEAVE_ADD), side_by_side(bank[:], WEAVE_ADD), side_by_side(pos_chunk[c], WEAVE_ADD), ADD)
 
         def relu_on_vector(c):
             nc.vector.tensor_scalar(h_chunk[c], summed[c][:], 0.0, None, MAX)
@@ -187,9 +192,13 @@ def tile_picked_phpq_relu_p_kernel(tc, x_words, x_scales, w1, w2_words, w2_scale
             start, width = GROUPS[d][0] * CHUNK, GROUPS[d][1] * CHUNK
             codes, plane = h_mx[d]
             bank = psum.tile([P, N // P, width], F32, name="out_bank", tag="bank%d" % (H_BANKS + d))
+            last = d == len(GROUPS) - 1
+            other = bank
+            if last:
+                other = psum.tile([P, N // P, width], F32, name="other_bank", tag="bank0")
             for u in range(N // P):
                 nc.tensor.matmul_mx(
-                    out=bank[:, u, :],
+                    out=(other if u == 0 else bank)[:, u, :],
                     lhsT=w2_codes[:, 2 * P * u : 2 * P * (u + 1)].bitcast(FP4X4),
                     lhsT_scale=w2_plane[:, P * u : P * (u + 1)],
                     rhs=codes[:].bitcast(FP8X4),
@@ -197,9 +206,13 @@ def tile_picked_phpq_relu_p_kernel(tc, x_words, x_scales, w1, w2_words, w2_scale
                     start=True,
                     stop=True,
                 )
-            result = keep.tile([P, N // P, width], F32, name="result%d" % d, align_bytes=64)
+            if d == 0:
+                result = shared.tile([P, N // P, width], F32, name="result0", offset=late_at - 4 * PACK * POS_LOADS[2][1], align_bytes=64)
+            else:
+                result = keep.tile([P, N // P, width], F32, name="result%d" % d, align_bytes=64)
             if d == len(GROUPS) - 1:
-                nc.vector.tensor_copy(result[:], bank[:])
+                nc.vector.tensor_copy(result[:, 0, :], other[:, 0, :])
+                nc.scalar.copy(result[:, 1, :], bank[:, 1, :])
             else:
                 nc.scalar.copy(result[:], bank[:])
             nc.sync.dma_start(out_rows[:, :, start : start + width], result[:])
@@ -208,8 +221,8 @@ def tile_picked_phpq_relu_p_kernel(tc, x_words, x_scales, w1, w2_words, w2_scale
             first_layer(c)
         quantise(0)
         first_layer(4)
-        second_layer(0)
         first_layer(5)
+        second_layer(0)
         quantise(1)
         second_layer(1)
         first_layer(6)

@@ -28,7 +28,8 @@ WEAVE_ADD = 2
 
 X_FIRST = 256
 POS_LOADS = ((0, 256), (256, 256), (512, 256), (768, 256))
-GATHERS = ((0, 512), (512, 512))
+GATHERS = ((0, 512), (512, 256), (768, 256))
+ON_SCALAR = 88
 GROUPS = ((0, 2), (2, 2), (4, 2), (6, 1), (7, 1))
 FIRST_ON_VECTOR = 6
 H_BANKS = 3
@@ -43,8 +44,9 @@ def tile_picked_phpq_relu_p_kernel(tc, x_words, x_scales, w1, w2_words, w2_scale
         shared = ctx.enter_context(tc.tile_pool(name="shared", bufs=1))
         psum = ctx.enter_context(tc.psum_pool(name="psum", bufs=1))
 
-        w2_at = 4 * PACK * POS_LOADS[0][1]
-        scale_table = shared.tile([P, T], U8, name="scale_table", offset=w2_at - T // 2, align_bytes=64)
+        pos_bytes = 4 * PACK * POS_LOADS[0][1]
+        w2_at = 3 * pos_bytes
+        scale_table = shared.tile([P, T], U8, name="scale_table", offset=pos_bytes - T // 2, align_bytes=64)
 
         word_table = keep.tile([P, T], I32, name="word_table", align_bytes=64)
         x_rows = x_words[0].rearrange("p n t -> p (n t)").bitcast(I32)
@@ -81,16 +83,13 @@ def tile_picked_phpq_relu_p_kernel(tc, x_words, x_scales, w1, w2_words, w2_scale
 
         x_plane = keep.tile([P, S], U8, name="x_plane", align_bytes=64)
         nc.vector.memset(x_plane[:].bitcast(I32), 0)
-        late_at = w2_at + 2 * N + 4 * PACK * (POS_LOADS[1][1] + POS_LOADS[2][1])
-        picked = shared.tile([P, S], U8, name="picked", offset=late_at - S // 2, align_bytes=64)
+        picked = shared.tile([P, S], U8, name="picked", offset=w2_at - N, align_bytes=64)
         nc.vector.tensor_copy(picked[:], scale_table[:].indirect(offsets[:]))
         for r in range(4):
             nc.sync.dma_start(x_plane[r:P:32, :].bitcast(I32), picked[8 * r : P : 32, :].bitcast(I32))
 
         load_pos(0, shared, offset=0)
-        load_pos(1, shared, offset=w2_at + 2 * N)
-        w2_codes = shared.tile([P, 2 * N], U8, name="w2_codes", offset=w2_at, align_bytes=64)
-        nc.sync.dma_start(w2_codes[:].bitcast(I32), w2_words[0].bitcast(I32))
+        load_pos(1, shared, offset=pos_bytes)
 
         x_chunk = {}
 
@@ -118,22 +117,32 @@ def tile_picked_phpq_relu_p_kernel(tc, x_words, x_scales, w1, w2_words, w2_scale
                 stop=True,
             )
 
-        w1_grouped = keep.tile([P, PACK, P, PACK], BF16, name="w1_grouped", align_bytes=64)
-        cast_out = w1_grouped[:].rearrange("p t m j -> p m j t")
+        w1_grouped = [
+            keep.tile([P, 2, P, PACK], BF16, name="w1_grouped%d" % pair, tag="w1_grouped%d" % pair, align_bytes=64)
+            for pair in range(2)
+        ]
+        cast_out = [grouped[:].rearrange("p t m j -> p m j t") for grouped in w1_grouped]
         cast_in = w1_raw[:].rearrange("p j (m t) -> p m j t", t=PACK)
-        nc.scalar.activation(cast_out[:, :, :, 2:], cast_in[:, :, :, 2:], COPY)
-        nc.vector.tensor_copy(cast_out[:, :, :, :2], cast_in[:, :, :, :2])
-        w1_codes = keep.tile([P, PACK, P], U32, name="w1_codes", align_bytes=64)
+        nc.scalar.activation(cast_out[0][:, :ON_SCALAR], cast_in[:, :ON_SCALAR, :, :2], COPY)
+        nc.vector.tensor_copy(cast_out[0][:, ON_SCALAR:], cast_in[:, ON_SCALAR:, :, :2])
+        nc.vector.tensor_copy(cast_out[1], cast_in[:, :, :, 2:])
+        w1_pairs = [
+            keep.tile([P, 2, P], U32, name="w1_codes0", align_bytes=64),
+            keep.tile([P, 2, P], U32, name="w1_codes1", tag="w1_raw", align_bytes=64),
+        ]
         w1_plane = keep.tile([P, PACK, P], U8, name="w1_plane", align_bytes=64)
         for t in range(0, PACK, 2):
             nc.vector.quantize_mx(
-                out=w1_codes[:, t : t + 2, :].rearrange("p t m -> p (t m)").bitcast(FP8X4),
+                out=w1_pairs[t // 2][:].rearrange("p t m -> p (t m)").bitcast(FP8X4),
                 scales=w1_plane[:, t : t + 2, :].rearrange("p t m -> p (t m)"),
-                in_=w1_grouped[:, t : t + 2, :, :].rearrange("p t m j -> p (t m j)"),
+                in_=w1_grouped[t // 2][:].rearrange("p t m j -> p (t m j)"),
             )
 
-        load_pos(2, shared, offset=late_at - 4 * PACK * POS_LOADS[2][1])
-        load_pos(3, shared, offset=late_at)
+        load_pos(2, shared, offset=2 * pos_bytes)
+        w2_codes = shared.tile([P, 2 * N], U8, name="w2_codes", offset=w2_at, align_bytes=64)
+        nc.sync.dma_start(w2_codes[:].bitcast(I32), w2_words[0].bitcast(I32))
+        load_pos(3, shared, offset=w2_at + 2 * N)
+        gather_words(2, "w1_grouped0")
 
         out_rows = out.rearrange("(u p) s -> p u s", p=P)
         summed = [keep.tile([P, CHUNK * PACK], BF16, name="summed%d" % c, align_bytes=64) for c in range(CHUNKS)]
@@ -158,7 +167,7 @@ def tile_picked_phpq_relu_p_kernel(tc, x_words, x_scales, w1, w2_words, w2_scale
             for t in range(PACK):
                 nc.tensor.matmul_mx(
                     out=(early if t < 2 else bank)[:, t, :],
-                    lhsT=w1_codes[:, t, :].bitcast(FP8X4),
+                    lhsT=w1_pairs[t // 2][:, t % 2, :].bitcast(FP8X4),
                     lhsT_scale=w1_plane[:, t, :],
                     rhs=x_chunk[c].bitcast(FP8X4),
                     rhs_scale=x_plane[:, c * CHUNK : (c + 1) * CHUNK],
@@ -207,7 +216,7 @@ def tile_picked_phpq_relu_p_kernel(tc, x_words, x_scales, w1, w2_words, w2_scale
                     stop=True,
                 )
             if d == 0:
-                result = shared.tile([P, N // P, width], F32, name="result0", offset=late_at - 4 * PACK * POS_LOADS[2][1], align_bytes=64)
+                result = shared.tile([P, N // P, width], F32, name="result0", offset=2 * pos_bytes, align_bytes=64)
             else:
                 result = keep.tile([P, N // P, width], F32, name="result%d" % d, align_bytes=64)
             if d == len(GROUPS) - 1:

@@ -27,9 +27,9 @@ WEAVE = 4
 WEAVE_ADD = 2
 
 X_FIRST = 256
-POS_LOADS = ((0, 256), (256, 256), (512, 256), (768, 256))
+POS_LOADS = ((0, 256), (256, 256), (512, 256), (768, 128), (896, 128))
 GATHERS = ((0, 512), (512, 256), (768, 256))
-ON_SCALAR = 88
+ON_SCALAR = 40
 GROUPS = ((0, 2), (2, 2), (4, 2), (6, 1), (7, 1))
 FIRST_ON_VECTOR = 6
 H_BANKS = 3
@@ -42,6 +42,7 @@ def tile_picked_phpq_relu_p_kernel(tc, x_words, x_scales, w1, w2_words, w2_scale
     with ExitStack() as ctx:
         keep = ctx.enter_context(tc.tile_pool(name="keep", bufs=1))
         shared = ctx.enter_context(tc.tile_pool(name="shared", bufs=1))
+        sums = ctx.enter_context(tc.tile_pool(name="sums", bufs=1))
         psum = ctx.enter_context(tc.psum_pool(name="psum", bufs=1))
 
         pos_bytes = 4 * PACK * POS_LOADS[0][1]
@@ -56,8 +57,11 @@ def tile_picked_phpq_relu_p_kernel(tc, x_words, x_scales, w1, w2_words, w2_scale
         nc.vector.memset(scale_table[:].bitcast(I32), 0)
         nc.sync.dma_start(scale_table[0:P:8, :].bitcast(I32), x_scales[0].bitcast(I32))
         nc.sync.dma_start(word_table[:, X_FIRST:], x_rows[:, X_FIRST:])
-        w1_raw = keep.tile([P, PACK, H], F32, name="w1_raw", tag="w1_raw", align_bytes=64)
-        nc.sync.dma_start(w1_raw[:], w1.rearrange("(p j) c -> p j c", j=PACK))
+        w1_rows = w1.rearrange("(p j) c -> p j c", j=PACK)
+        w1_left = keep.tile([P, PACK, H // 2], F32, name="w1_left", align_bytes=64)
+        nc.sync.dma_start(w1_left[:], w1_rows[:, :, : H // 2])
+        w1_right = keep.tile([P, PACK, H // 2], F32, name="w1_right", tag="w1_raw", align_bytes=64)
+        nc.sync.dma_start(w1_right[:], w1_rows[:, :, H // 2 :])
 
         w2_plane = keep.tile([P, N], U8, name="w2_plane", align_bytes=64)
         nc.vector.memset(w2_plane[:].bitcast(I32), 0)
@@ -122,10 +126,14 @@ def tile_picked_phpq_relu_p_kernel(tc, x_words, x_scales, w1, w2_words, w2_scale
             for pair in range(2)
         ]
         cast_out = [grouped[:].rearrange("p t m j -> p m j t") for grouped in w1_grouped]
-        cast_in = w1_raw[:].rearrange("p j (m t) -> p m j t", t=PACK)
-        nc.scalar.activation(cast_out[0][:, :ON_SCALAR], cast_in[:, :ON_SCALAR, :, :2], COPY)
-        nc.vector.tensor_copy(cast_out[0][:, ON_SCALAR:], cast_in[:, ON_SCALAR:, :, :2])
-        nc.vector.tensor_copy(cast_out[1], cast_in[:, :, :, 2:])
+        left_in = w1_left[:].rearrange("p j (m t) -> p m j t", t=PACK)
+        right_in = w1_right[:].rearrange("p j (m t) -> p m j t", t=PACK)
+        mid = P // 2
+        nc.scalar.activation(cast_out[1][:, :mid], left_in[:, :, :, 2:], COPY)
+        nc.scalar.activation(cast_out[0][:, :mid], left_in[:, :, :, :2], COPY)
+        nc.scalar.activation(cast_out[0][:, mid : mid + ON_SCALAR], right_in[:, :ON_SCALAR, :, :2], COPY)
+        nc.vector.tensor_copy(cast_out[0][:, mid + ON_SCALAR :], right_in[:, ON_SCALAR:, :, :2])
+        nc.vector.tensor_copy(cast_out[1][:, mid:], right_in[:, :, :, 2:])
         w1_pairs = [
             keep.tile([P, 2, P], U32, name="w1_codes0", align_bytes=64),
             keep.tile([P, 2, P], U32, name="w1_codes1", tag="w1_raw", align_bytes=64),
@@ -139,17 +147,23 @@ def tile_picked_phpq_relu_p_kernel(tc, x_words, x_scales, w1, w2_words, w2_scale
             )
 
         load_pos(2, shared, offset=2 * pos_bytes)
+        load_pos(3, keep, tag="w1_grouped1")
         w2_codes = shared.tile([P, 2 * N], U8, name="w2_codes", offset=w2_at, align_bytes=64)
         nc.sync.dma_start(w2_codes[:].bitcast(I32), w2_words[0].bitcast(I32))
-        load_pos(3, shared, offset=w2_at + 2 * N)
+        load_pos(4, shared, offset=w2_at + 2 * N)
         gather_words(2, "w1_grouped0")
 
         out_rows = out.rearrange("(u p) s -> p u s", p=P)
-        summed = [keep.tile([P, CHUNK * PACK], BF16, name="summed%d" % c, align_bytes=64) for c in range(CHUNKS)]
+        sum_bytes = 2 * CHUNK * PACK
+        sum_at = {0: 0, 1: 2, 2: 4, 3: 6, 4: 2, 5: 9, 6: 6, 7: 8}
+        summed = {}
         h_group = []
         h_chunk = []
         for first_chunk, count in GROUPS:
-            hidden = keep.tile([P, count, CHUNK * PACK], BF16, name="hidden%d" % first_chunk, align_bytes=64)
+            if first_chunk == 6:
+                hidden = sums.tile([P, count, CHUNK * PACK], BF16, name="hidden6", offset=10 * sum_bytes // 2, align_bytes=64)
+            else:
+                hidden = keep.tile([P, count, CHUNK * PACK], BF16, name="hidden%d" % first_chunk, align_bytes=64)
             h_group.append(hidden[:].rearrange("p a n -> p (a n)"))
             h_chunk.extend(hidden[:, a, :] for a in range(count))
 
@@ -160,6 +174,7 @@ def tile_picked_phpq_relu_p_kernel(tc, x_words, x_scales, w1, w2_words, w2_scale
             return rows.rearrange("p t (c i) -> p c t i", i=run)
 
         def first_layer(c):
+            summed[c] = sums.tile([P, CHUNK * PACK], BF16, name="summed%d" % c, offset=sum_at[c] * sum_bytes // 2, align_bytes=64)
             bank = psum.tile([P, PACK, CHUNK], F32, name="h_bank", tag="bank%d" % (c % H_BANKS))
             early = bank
             if c == 0:

@@ -27,9 +27,10 @@ WEAVE = 4
 WEAVE_ADD = 2
 
 X_FIRST = 256
-POS_LOADS = ((0, 256), (256, 256), (512, 256), (768, 128), (896, 128))
-GATHERS = ((0, 512), (512, 256), (768, 256))
-ON_SCALAR = 40
+POS_EARLY = ((0, 128), (128, 128), (256, 128), (384, 128), (512, 256))
+POS_LATE = ((768, 128), (896, 128))
+W1_PIECES = 4
+GATHERS = ((0, 512), (512, 512))
 GROUPS = ((0, 2), (2, 2), (4, 2), (6, 1), (7, 1))
 FIRST_ON_VECTOR = 6
 H_BANKS = 3
@@ -45,9 +46,8 @@ def tile_picked_phpq_relu_p_kernel(tc, x_words, x_scales, w1, w2_words, w2_scale
         sums = ctx.enter_context(tc.tile_pool(name="sums", bufs=1))
         psum = ctx.enter_context(tc.psum_pool(name="psum", bufs=1))
 
-        pos_bytes = 4 * PACK * POS_LOADS[0][1]
-        w2_at = 3 * pos_bytes
-        scale_table = shared.tile([P, T], U8, name="scale_table", offset=pos_bytes - T // 2, align_bytes=64)
+        early_bytes = 4 * PACK * sum(width for start, width in POS_EARLY)
+        scale_table = shared.tile([P, T], U8, name="scale_table", offset=0, align_bytes=64)
 
         word_table = keep.tile([P, T], I32, name="word_table", align_bytes=64)
         x_rows = x_words[0].rearrange("p n t -> p (n t)").bitcast(I32)
@@ -58,10 +58,12 @@ def tile_picked_phpq_relu_p_kernel(tc, x_words, x_scales, w1, w2_words, w2_scale
         nc.sync.dma_start(scale_table[0:P:8, :].bitcast(I32), x_scales[0].bitcast(I32))
         nc.sync.dma_start(word_table[:, X_FIRST:], x_rows[:, X_FIRST:])
         w1_rows = w1.rearrange("(p j) c -> p j c", j=PACK)
-        w1_left = keep.tile([P, PACK, H // 2], F32, name="w1_left", align_bytes=64)
-        nc.sync.dma_start(w1_left[:], w1_rows[:, :, : H // 2])
-        w1_right = keep.tile([P, PACK, H // 2], F32, name="w1_right", tag="w1_raw", align_bytes=64)
-        nc.sync.dma_start(w1_right[:], w1_rows[:, :, H // 2 :])
+        piece = H // W1_PIECES
+        w1_raw = []
+        for g in range(W1_PIECES):
+            raw = keep.tile([P, PACK, piece], F32, name="w1_raw%d" % g, tag="w1_raw%d" % g, align_bytes=64)
+            nc.sync.dma_start(raw[:], w1_rows[:, :, g * piece : (g + 1) * piece])
+            w1_raw.append(raw)
 
         w2_plane = keep.tile([P, N], U8, name="w2_plane", align_bytes=64)
         nc.vector.memset(w2_plane[:].bitcast(I32), 0)
@@ -76,24 +78,24 @@ def tile_picked_phpq_relu_p_kernel(tc, x_words, x_scales, w1, w2_words, w2_scale
         pos_rows = pos.rearrange("(p t) s -> p t s", t=PACK)
         pos_chunk = {}
 
-        def load_pos(g, pool, **place):
-            start, width = POS_LOADS[g]
-            flat = pool.tile([P, PACK * width], F32, name="pos%d" % g, align_bytes=64, **place)
-            rows = flat[:].rearrange("p (t n) -> p t n", t=PACK)
-            nc.sync.dma_start(rows, pos_rows[:, :, start : start + width])
-            for c0 in range(0, width, CHUNK):
-                pos_chunk[(start + c0) // CHUNK] = rows[:, :, c0 : c0 + CHUNK]
-
+        def load_pos(loads, name, offset):
+            first = loads[0][0]
+            total = sum(width for start, width in loads)
+            flat = shared.tile([P, PACK * total], F32, name=name, offset=offset, align_bytes=64)
+            for start, width in loads:
+                rows = flat[:, PACK * (start - first) : PACK * (start - first + width)].rearrange("p (t n) -> p t n", t=PACK)
+                nc.sync.dma_start(rows, pos_rows[:, :, start : start + width])
+                for c0 in range(0, width, CHUNK):
+                    pos_chunk[(start + c0) // CHUNK] = rows[:, :, c0 : c0 + CHUNK]
 
         x_plane = keep.tile([P, S], U8, name="x_plane", align_bytes=64)
         nc.vector.memset(x_plane[:].bitcast(I32), 0)
-        picked = shared.tile([P, S], U8, name="picked", offset=w2_at - N, align_bytes=64)
+        picked = shared.tile([P, S], U8, name="picked", offset=early_bytes, align_bytes=64)
         nc.vector.tensor_copy(picked[:], scale_table[:].indirect(offsets[:]))
         for r in range(4):
             nc.sync.dma_start(x_plane[r:P:32, :].bitcast(I32), picked[8 * r : P : 32, :].bitcast(I32))
 
-        load_pos(0, shared, offset=0)
-        load_pos(1, shared, offset=pos_bytes)
+        load_pos(POS_EARLY, "pos_early", 0)
 
         x_chunk = {}
 
@@ -126,17 +128,18 @@ def tile_picked_phpq_relu_p_kernel(tc, x_words, x_scales, w1, w2_words, w2_scale
             for pair in range(2)
         ]
         cast_out = [grouped[:].rearrange("p t m j -> p m j t") for grouped in w1_grouped]
-        left_in = w1_left[:].rearrange("p j (m t) -> p m j t", t=PACK)
-        right_in = w1_right[:].rearrange("p j (m t) -> p m j t", t=PACK)
-        mid = P // 2
-        nc.scalar.activation(cast_out[1][:, :mid], left_in[:, :, :, 2:], COPY)
-        nc.scalar.activation(cast_out[0][:, :mid], left_in[:, :, :, :2], COPY)
-        nc.scalar.activation(cast_out[0][:, mid : mid + ON_SCALAR], right_in[:, :ON_SCALAR, :, :2], COPY)
-        nc.vector.tensor_copy(cast_out[0][:, mid + ON_SCALAR :], right_in[:, ON_SCALAR:, :, :2])
-        nc.vector.tensor_copy(cast_out[1][:, mid:], right_in[:, :, :, 2:])
+        span = piece // PACK
+        for g in range(W1_PIECES):
+            cast_in = w1_raw[g][:].rearrange("p j (m t) -> p m j t", t=PACK)
+            columns = slice(g * span, (g + 1) * span)
+            nc.scalar.activation(cast_out[0][:, columns], cast_in[:, :, :, :2], COPY)
+            if g < W1_PIECES - 1:
+                nc.scalar.activation(cast_out[1][:, columns], cast_in[:, :, :, 2:], COPY)
+            else:
+                nc.vector.tensor_copy(cast_out[1][:, columns], cast_in[:, :, :, 2:])
         w1_pairs = [
             keep.tile([P, 2, P], U32, name="w1_codes0", align_bytes=64),
-            keep.tile([P, 2, P], U32, name="w1_codes1", tag="w1_raw", align_bytes=64),
+            keep.tile([P, 2, P], U32, name="w1_codes1", tag="w1_raw%d" % (W1_PIECES - 1), align_bytes=64),
         ]
         w1_plane = keep.tile([P, PACK, P], U8, name="w1_plane", align_bytes=64)
         for t in range(0, PACK, 2):
@@ -146,12 +149,9 @@ def tile_picked_phpq_relu_p_kernel(tc, x_words, x_scales, w1, w2_words, w2_scale
                 in_=w1_grouped[t // 2][:].rearrange("p t m j -> p (t m j)"),
             )
 
-        load_pos(2, shared, offset=2 * pos_bytes)
-        load_pos(3, keep, tag="w1_grouped1")
-        w2_codes = shared.tile([P, 2 * N], U8, name="w2_codes", offset=w2_at, align_bytes=64)
+        w2_codes = shared.tile([P, 2 * N], U8, name="w2_codes", offset=early_bytes, align_bytes=64)
         nc.sync.dma_start(w2_codes[:].bitcast(I32), w2_words[0].bitcast(I32))
-        load_pos(4, shared, offset=w2_at + 2 * N)
-        gather_words(2, "w1_grouped0")
+        load_pos(POS_LATE, "pos_late", early_bytes + 2 * N)
 
         out_rows = out.rearrange("(u p) s -> p u s", p=P)
         sum_bytes = 2 * CHUNK * PACK
@@ -231,7 +231,7 @@ def tile_picked_phpq_relu_p_kernel(tc, x_words, x_scales, w1, w2_words, w2_scale
                     stop=True,
                 )
             if d == 0:
-                result = shared.tile([P, N // P, width], F32, name="result0", offset=2 * pos_bytes, align_bytes=64)
+                result = shared.tile([P, N // P, width], F32, name="result0", offset=0, align_bytes=64)
             else:
                 result = keep.tile([P, N // P, width], F32, name="result%d" % d, align_bytes=64)
             if d == len(GROUPS) - 1:

@@ -27,9 +27,9 @@ WEAVE = 4
 WEAVE_ADD = 2
 
 X_FIRST = 256
-POS_EARLY = ((0, 128), (128, 128), (256, 128), (384, 128), (512, 256))
+POS_EARLY = ((0, 256), (256, 256), (512, 256))
 POS_LATE = ((768, 128), (896, 128))
-W1_PIECES = 4
+ON_SCALAR = 96
 GATHERS = ((0, 512), (512, 512))
 GROUPS = ((0, 2), (2, 2), (4, 2), (6, 1), (7, 1))
 FIRST_ON_VECTOR = 6
@@ -58,12 +58,8 @@ def tile_picked_phpq_relu_p_kernel(tc, x_words, x_scales, w1, w2_words, w2_scale
         nc.sync.dma_start(scale_table[0:P:8, :].bitcast(I32), x_scales[0].bitcast(I32))
         nc.sync.dma_start(word_table[:, X_FIRST:], x_rows[:, X_FIRST:])
         w1_rows = w1.rearrange("(p j) c -> p j c", j=PACK)
-        piece = H // W1_PIECES
-        w1_raw = []
-        for g in range(W1_PIECES):
-            raw = keep.tile([P, PACK, piece], F32, name="w1_raw%d" % g, tag="w1_raw%d" % g, align_bytes=64)
-            nc.sync.dma_start(raw[:], w1_rows[:, :, g * piece : (g + 1) * piece])
-            w1_raw.append(raw)
+        w1_raw = keep.tile([P, PACK, H], F32, name="w1_raw", tag="w1_raw", align_bytes=64)
+        nc.sync.dma_start(w1_raw[:], w1_rows)
 
         w2_plane = keep.tile([P, N], U8, name="w2_plane", align_bytes=64)
         nc.vector.memset(w2_plane[:].bitcast(I32), 0)
@@ -78,7 +74,7 @@ def tile_picked_phpq_relu_p_kernel(tc, x_words, x_scales, w1, w2_words, w2_scale
         pos_rows = pos.rearrange("(p t) s -> p t s", t=PACK)
         pos_chunk = {}
 
-        def load_pos(loads, name, offset):
+        def load_pos(loads, name, offset, between=None):
             first = loads[0][0]
             total = sum(width for start, width in loads)
             flat = shared.tile([P, PACK * total], F32, name=name, offset=offset, align_bytes=64)
@@ -87,6 +83,8 @@ def tile_picked_phpq_relu_p_kernel(tc, x_words, x_scales, w1, w2_words, w2_scale
                 nc.sync.dma_start(rows, pos_rows[:, :, start : start + width])
                 for c0 in range(0, width, CHUNK):
                     pos_chunk[(start + c0) // CHUNK] = rows[:, :, c0 : c0 + CHUNK]
+                if between and start == first:
+                    between()
 
         x_plane = keep.tile([P, S], U8, name="x_plane", align_bytes=64)
         nc.vector.memset(x_plane[:].bitcast(I32), 0)
@@ -128,18 +126,13 @@ def tile_picked_phpq_relu_p_kernel(tc, x_words, x_scales, w1, w2_words, w2_scale
             for pair in range(2)
         ]
         cast_out = [grouped[:].rearrange("p t m j -> p m j t") for grouped in w1_grouped]
-        span = piece // PACK
-        for g in range(W1_PIECES):
-            cast_in = w1_raw[g][:].rearrange("p j (m t) -> p m j t", t=PACK)
-            columns = slice(g * span, (g + 1) * span)
-            nc.scalar.activation(cast_out[0][:, columns], cast_in[:, :, :, :2], COPY)
-            if g < W1_PIECES - 1:
-                nc.scalar.activation(cast_out[1][:, columns], cast_in[:, :, :, 2:], COPY)
-            else:
-                nc.vector.tensor_copy(cast_out[1][:, columns], cast_in[:, :, :, 2:])
+        cast_in = w1_raw[:].rearrange("p j (m t) -> p m j t", t=PACK)
+        nc.scalar.activation(cast_out[0][:, :ON_SCALAR], cast_in[:, :ON_SCALAR, :, :2], COPY)
+        nc.vector.tensor_copy(cast_out[0][:, ON_SCALAR:], cast_in[:, ON_SCALAR:, :, :2])
+        nc.vector.tensor_copy(cast_out[1], cast_in[:, :, :, 2:])
         w1_pairs = [
             keep.tile([P, 2, P], U32, name="w1_codes0", align_bytes=64),
-            keep.tile([P, 2, P], U32, name="w1_codes1", tag="w1_raw%d" % (W1_PIECES - 1), align_bytes=64),
+            keep.tile([P, 2, P], U32, name="w1_codes1", tag="w1_raw", align_bytes=64),
         ]
         w1_plane = keep.tile([P, PACK, P], U8, name="w1_plane", align_bytes=64)
         for t in range(0, PACK, 2):
@@ -150,8 +143,7 @@ def tile_picked_phpq_relu_p_kernel(tc, x_words, x_scales, w1, w2_words, w2_scale
             )
 
         w2_codes = shared.tile([P, 2 * N], U8, name="w2_codes", offset=early_bytes, align_bytes=64)
-        nc.sync.dma_start(w2_codes[:].bitcast(I32), w2_words[0].bitcast(I32))
-        load_pos(POS_LATE, "pos_late", early_bytes + 2 * N)
+        load_pos(POS_LATE, "pos_late", early_bytes + 2 * N, lambda: nc.sync.dma_start(w2_codes[:].bitcast(I32), w2_words[0].bitcast(I32)))
 
         out_rows = out.rearrange("(u p) s -> p u s", p=P)
         sum_bytes = 2 * CHUNK * PACK

@@ -29,7 +29,7 @@ WEAVE_ADD = 2
 X_FIRST = 256
 POS_EARLY = ((0, 256), (256, 256), (512, 256))
 POS_LATE = ((768, 128), (896, 128))
-ON_SCALAR = 96
+ON_SCALAR = (108, 40)
 GATHERS = ((0, 512), (512, 512))
 GROUPS = ((0, 2), (2, 2), (4, 2), (6, 1), (7, 1))
 FIRST_ON_VECTOR = 6
@@ -60,6 +60,8 @@ def tile_picked_phpq_relu_p_kernel(tc, x_words, x_scales, w1, w2_words, w2_scale
         w1_rows = w1.rearrange("(p j) c -> p j c", j=PACK)
         w1_raw = keep.tile([P, PACK, H], F32, name="w1_raw", tag="w1_raw", align_bytes=64)
         nc.sync.dma_start(w1_raw[:], w1_rows)
+        w2_codes = keep.tile([P, 2 * N], U8, name="w2_codes", align_bytes=64)
+        nc.sync.dma_start(w2_codes[:].bitcast(I32), w2_words[0].bitcast(I32))
 
         w2_plane = keep.tile([P, N], U8, name="w2_plane", align_bytes=64)
         nc.vector.memset(w2_plane[:].bitcast(I32), 0)
@@ -74,7 +76,7 @@ def tile_picked_phpq_relu_p_kernel(tc, x_words, x_scales, w1, w2_words, w2_scale
         pos_rows = pos.rearrange("(p t) s -> p t s", t=PACK)
         pos_chunk = {}
 
-        def load_pos(loads, name, offset, between=None):
+        def load_pos(loads, name, offset):
             first = loads[0][0]
             total = sum(width for start, width in loads)
             flat = shared.tile([P, PACK * total], F32, name=name, offset=offset, align_bytes=64)
@@ -83,8 +85,6 @@ def tile_picked_phpq_relu_p_kernel(tc, x_words, x_scales, w1, w2_words, w2_scale
                 nc.sync.dma_start(rows, pos_rows[:, :, start : start + width])
                 for c0 in range(0, width, CHUNK):
                     pos_chunk[(start + c0) // CHUNK] = rows[:, :, c0 : c0 + CHUNK]
-                if between and start == first:
-                    between()
 
         x_plane = keep.tile([P, S], U8, name="x_plane", align_bytes=64)
         nc.vector.memset(x_plane[:].bitcast(I32), 0)
@@ -127,9 +127,10 @@ def tile_picked_phpq_relu_p_kernel(tc, x_words, x_scales, w1, w2_words, w2_scale
         ]
         cast_out = [grouped[:].rearrange("p t m j -> p m j t") for grouped in w1_grouped]
         cast_in = w1_raw[:].rearrange("p j (m t) -> p m j t", t=PACK)
-        nc.scalar.activation(cast_out[0][:, :ON_SCALAR], cast_in[:, :ON_SCALAR, :, :2], COPY)
-        nc.vector.tensor_copy(cast_out[0][:, ON_SCALAR:], cast_in[:, ON_SCALAR:, :, :2])
-        nc.vector.tensor_copy(cast_out[1], cast_in[:, :, :, 2:])
+        for pair in range(2):
+            tiles = slice(2 * pair, 2 * pair + 2)
+            nc.scalar.activation(cast_out[pair][:, : ON_SCALAR[pair]], cast_in[:, : ON_SCALAR[pair], :, tiles], COPY)
+            nc.vector.tensor_copy(cast_out[pair][:, ON_SCALAR[pair] :], cast_in[:, ON_SCALAR[pair] :, :, tiles])
         w1_pairs = [
             keep.tile([P, 2, P], U32, name="w1_codes0", align_bytes=64),
             keep.tile([P, 2, P], U32, name="w1_codes1", tag="w1_raw", align_bytes=64),
@@ -142,22 +143,24 @@ def tile_picked_phpq_relu_p_kernel(tc, x_words, x_scales, w1, w2_words, w2_scale
                 in_=w1_grouped[t // 2][:].rearrange("p t m j -> p (t m j)"),
             )
 
-        w2_codes = shared.tile([P, 2 * N], U8, name="w2_codes", offset=early_bytes, align_bytes=64)
-        load_pos(POS_LATE, "pos_late", early_bytes + 2 * N, lambda: nc.sync.dma_start(w2_codes[:].bitcast(I32), w2_words[0].bitcast(I32)))
+        load_pos(POS_LATE, "pos_late", early_bytes)
 
         out_rows = out.rearrange("(u p) s -> p u s", p=P)
         sum_bytes = 2 * CHUNK * PACK
         sum_at = {0: 0, 1: 2, 2: 4, 3: 6, 4: 2, 5: 9, 6: 6, 7: 8}
         summed = {}
-        h_group = []
-        h_chunk = []
-        for first_chunk, count in GROUPS:
+        h_group = {}
+        h_chunk = {}
+
+        def rectified_tile(d):
+            first_chunk, count = GROUPS[d]
             if first_chunk == 6:
                 hidden = sums.tile([P, count, CHUNK * PACK], BF16, name="hidden6", offset=10 * sum_bytes // 2, align_bytes=64)
             else:
-                hidden = keep.tile([P, count, CHUNK * PACK], BF16, name="hidden%d" % first_chunk, align_bytes=64)
-            h_group.append(hidden[:].rearrange("p a n -> p (a n)"))
-            h_chunk.extend(hidden[:, a, :] for a in range(count))
+                hidden = keep.tile([P, count, CHUNK * PACK], BF16, name="hidden%d" % first_chunk, tag="h_codes0" if first_chunk == 4 else "hidden%d" % first_chunk, align_bytes=64)
+            h_group[d] = hidden[:].rearrange("p a n -> p (a n)")
+            for a in range(count):
+                h_chunk[first_chunk + a] = hidden[:, a, :]
 
         def woven(flat, run=WEAVE):
             return flat.rearrange("p (c i t) -> p c t i", i=run, t=PACK)
@@ -199,10 +202,18 @@ def tile_picked_phpq_relu_p_kernel(tc, x_words, x_scales, w1, w2_words, w2_scale
 
         def quantise(d):
             width = GROUPS[d][1] * CHUNK
-            codes = keep.tile([P, width], U32, name="h_codes%d" % d, align_bytes=64)
+            codes = keep.tile([P, width], U32, name="h_codes%d" % d, tag="h_codes%d" % d, align_bytes=64)
             plane = keep.tile([P, width], U8, name="h_plane%d" % d, align_bytes=64)
             nc.vector.quantize_mx(out=codes[:].bitcast(FP8X4), scales=plane[:], in_=h_group[d])
             h_mx[d] = (codes, plane)
+
+        first_result = []
+
+        def first_result_half(u):
+            width = GROUPS[0][1] * CHUNK
+            half = keep.tile([P, width], F32, name="result0_%d" % u, tag="hidden2" if u else "result0", align_bytes=64)
+            nc.scalar.copy(half[:], first_result[u])
+            nc.sync.dma_start(out_rows[:, u, :width], half[:])
 
         def second_layer(d):
             start, width = GROUPS[d][0] * CHUNK, GROUPS[d][1] * CHUNK
@@ -212,6 +223,8 @@ def tile_picked_phpq_relu_p_kernel(tc, x_words, x_scales, w1, w2_words, w2_scale
             other = bank
             if last:
                 other = psum.tile([P, N // P, width], F32, name="other_bank", tag="bank0")
+            if d == 0:
+                other = psum.tile([P, N // P, width], F32, name="other_bank", tag="bank6")
             for u in range(N // P):
                 nc.tensor.matmul_mx(
                     out=(other if u == 0 else bank)[:, u, :],
@@ -223,7 +236,8 @@ def tile_picked_phpq_relu_p_kernel(tc, x_words, x_scales, w1, w2_words, w2_scale
                     stop=True,
                 )
             if d == 0:
-                result = shared.tile([P, N // P, width], F32, name="result0", offset=0, align_bytes=64)
+                first_result.extend([other[:, 0, :], bank[:, 1, :]])
+                return
             else:
                 result = keep.tile([P, N // P, width], F32, name="result%d" % d, align_bytes=64)
             if d == len(GROUPS) - 1:
@@ -233,13 +247,19 @@ def tile_picked_phpq_relu_p_kernel(tc, x_words, x_scales, w1, w2_words, w2_scale
                 nc.scalar.copy(result[:], bank[:])
             nc.sync.dma_start(out_rows[:, :, start : start + width], result[:])
 
+        rectified_tile(0)
+        rectified_tile(1)
         for c in range(4):
             first_layer(c)
         quantise(0)
+        second_layer(0)
+        first_result_half(0)
+        for d in range(2, len(GROUPS)):
+            rectified_tile(d)
         first_layer(4)
         first_layer(5)
-        second_layer(0)
         quantise(1)
+        first_result_half(1)
         second_layer(1)
         first_layer(6)
         quantise(2)

@@ -34,8 +34,6 @@ GATHERS = ((0, 512), (512, 512))
 GROUPS = ((0, 2), (2, 2), (4, 2), (6, 1), (7, 1))
 FIRST_ON_VECTOR = 6
 H_BANKS = 3
-WARM_UPS = 3
-WARM_WIDTH = 512
 
 
 def tile_picked_phpq_relu_p_kernel(tc, x_words, x_scales, w1, w2_words, w2_scales, pos, offs, out):
@@ -106,20 +104,8 @@ def tile_picked_phpq_relu_p_kernel(tc, x_words, x_scales, w1, w2_words, w2_scale
                 x_chunk[(start + c0) // CHUNK] = words[:, c0 : c0 + CHUNK]
             return words
 
-        x_first = gather_words(0, "x_codes0")
+        gather_words(0, "x_codes0")
         gather_words(1, "x_codes1")
-
-        unread = psum.tile([P, WARM_WIDTH], F32, name="unread", tag="bank%d" % (H_BANKS + len(GROUPS) - 1))
-        for repeat in range(WARM_UPS):
-            nc.tensor.matmul_mx(
-                out=unread[:],
-                lhsT=x_chunk[0].bitcast(FP8X4),
-                lhsT_scale=picked[:, :CHUNK],
-                rhs=x_first[:, :WARM_WIDTH].bitcast(FP8X4),
-                rhs_scale=picked[:, :WARM_WIDTH],
-                start=True,
-                stop=True,
-            )
 
         w1_grouped = [
             keep.tile([P, 2, P, PACK], BF16, name="w1_grouped%d" % pair, tag="w1_grouped%d" % pair, align_bytes=64)

@@ -30,7 +30,7 @@ X_FIRST = 256
 POS_EARLY = ((0, 256), (256, 256), (512, 256))
 POS_LATE = ((768, 128), (896, 128))
 ON_SCALAR = (108, 40)
-GATHERS = ((0, 512), (512, 512))
+GATHERS = ((0, 256), (256, 512), (768, 256))
 GROUPS = ((0, 2), (2, 2), (4, 2), (6, 1), (7, 1))
 FIRST_ON_VECTOR = 6
 H_BANKS = 3
@@ -54,10 +54,10 @@ def tile_picked_phpq_relu_p_kernel(tc, x_words, x_scales, w1, w2_words, w2_scale
         nc.sync.dma_start(offsets[:], offs)
         nc.vector.memset(scale_table[:].bitcast(I32), 0)
         nc.sync.dma_start(scale_table[0:P:8, :].bitcast(I32), x_scales[0].bitcast(I32))
-        nc.sync.dma_start(word_table[:, X_FIRST:], x_rows[:, X_FIRST:])
         w1_rows = w1.rearrange("(p j) c -> p j c", j=PACK)
         w1_raw = keep.tile([P, PACK, H], F32, name="w1_raw", tag="w1_raw", align_bytes=64)
         nc.sync.dma_start(w1_raw[:], w1_rows)
+        nc.sync.dma_start(word_table[:, X_FIRST:], x_rows[:, X_FIRST:])
         w2_codes = keep.tile([P, 2 * N], U8, name="w2_codes", align_bytes=64)
         nc.sync.dma_start(w2_codes[:].bitcast(I32), w2_words[0].bitcast(I32))
 
@@ -95,17 +95,15 @@ def tile_picked_phpq_relu_p_kernel(tc, x_words, x_scales, w1, w2_words, w2_scale
 
         x_chunk = {}
 
-        def gather_words(g, tag):
+        def gather_words(g, pool, **place):
             start, width = GATHERS[g]
-            words = keep.tile([P, width], U32, name="x_codes%d" % g, tag=tag, align_bytes=64)
+            words = pool.tile([P, width], U32, name="x_codes%d" % g, align_bytes=64, **place)
             entries = offsets[:, start // LIST_ROWS : (start + width) // LIST_ROWS]
             nc.vector.tensor_copy(words[:], word_table[:].bitcast(U32).indirect(entries))
             for c0 in range(0, width, CHUNK):
                 x_chunk[(start + c0) // CHUNK] = words[:, c0 : c0 + CHUNK]
             return words
 
-        gather_words(0, "x_codes0")
-        gather_words(1, "x_codes1")
 
         w1_grouped = [
             keep.tile([P, 2, P, PACK], BF16, name="w1_grouped%d" % pair, tag="w1_grouped%d" % pair, align_bytes=64)
@@ -130,6 +128,9 @@ def tile_picked_phpq_relu_p_kernel(tc, x_words, x_scales, w1, w2_words, w2_scale
             )
 
         load_pos(POS_LATE, "pos_late", early_bytes)
+
+        gather_words(0, keep)
+        gather_words(1, keep)
 
         out_rows = out.rearrange("(u p) s -> p u s", p=P)
         sum_bytes = 2 * CHUNK * PACK
@@ -157,12 +158,9 @@ def tile_picked_phpq_relu_p_kernel(tc, x_words, x_scales, w1, w2_words, w2_scale
         def first_layer(c):
             summed[c] = sums.tile([P, CHUNK * PACK], BF16, name="summed%d" % c, offset=sum_at[c] * sum_bytes // 2, align_bytes=64)
             bank = psum.tile([P, PACK, CHUNK], F32, name="h_bank", tag="bank%d" % (c % H_BANKS))
-            early = bank
-            if c == 0:
-                early = psum.tile([P, PACK, CHUNK], F32, name="early_bank", tag="bank%d" % (H_BANKS + len(GROUPS) - 2))
             for t in range(PACK):
                 nc.tensor.matmul_mx(
-                    out=(early if t < 2 else bank)[:, t, :],
+                    out=bank[:, t, :],
                     lhsT=w1_pairs[t // 2][:, t % 2, :].bitcast(FP8X4),
                     lhsT_scale=w1_plane[:, t, :],
                     rhs=x_chunk[c].bitcast(FP8X4),
@@ -172,11 +170,7 @@ def tile_picked_phpq_relu_p_kernel(tc, x_words, x_scales, w1, w2_words, w2_scale
                 )
             if c < FIRST_ON_VECTOR:
                 rows = summed[c][:].rearrange("p (t n) -> p t n", t=PACK)
-                if c == 0:
-                    nc.vector.tensor_tensor(rows[:, :2, :], early[:, :2, :], pos_chunk[c][:, :2, :], ADD)
-                    nc.vector.tensor_tensor(rows[:, 2:, :], bank[:, 2:, :], pos_chunk[c][:, 2:, :], ADD)
-                else:
-                    nc.vector.tensor_tensor(rows, bank[:], pos_chunk[c], ADD)
+                nc.vector.tensor_tensor(rows, bank[:], pos_chunk[c], ADD)
                 nc.scalar.activation(woven(h_chunk[c]), side_by_side(rows), RELU, bias=zero_bias)
             else:
                 nc.vector.tensor_tensor(woven(summed[c][:], WEAVE_ADD), side_by_side(bank[:], WEAVE_ADD), side_by_side(pos_chunk[c], WEAVE_ADD), ADD)
@@ -235,8 +229,11 @@ def tile_picked_phpq_relu_p_kernel(tc, x_words, x_scales, w1, w2_words, w2_scale
 
         rectified_tile(0)
         rectified_tile(1)
-        for c in range(4):
-            first_layer(c)
+        first_layer(0)
+        first_layer(1)
+        gather_words(2, sums, offset=0)
+        first_layer(2)
+        first_layer(3)
         quantise(0)
         second_layer(0)
         first_result_half(0)

@@ -22,18 +22,12 @@ P = 128
 PACK = 4
 LIST_ROWS = 16
 CHUNK = 128
-CHUNKS = S // CHUNK
+PAIR = 2 * CHUNK
 WEAVE = 4
 WEAVE_ADD = 2
-
 X_FIRST = 256
-POS_EARLY = ((0, 256), (256, 256), (512, 256))
-POS_LATE = ((768, 128), (896, 128))
 ON_SCALAR = (108, 40)
-GATHERS = ((0, 256), (256, 512), (768, 256))
-GROUPS = ((0, 2), (2, 2), (4, 2), (6, 1), (7, 1))
-FIRST_ON_VECTOR = 6
-H_BANKS = 3
+H_BANK = (0, 1, 2, 3, 4, 2, 3, 2)
 
 
 def tile_picked_phpq_relu_p_kernel(tc, x_words, x_scales, w1, w2_words, w2_scales, pos, offs, out):
@@ -44,9 +38,7 @@ def tile_picked_phpq_relu_p_kernel(tc, x_words, x_scales, w1, w2_words, w2_scale
         sums = ctx.enter_context(tc.tile_pool(name="sums", bufs=1))
         psum = ctx.enter_context(tc.psum_pool(name="psum", bufs=1))
 
-        early_bytes = 4 * PACK * sum(width for start, width in POS_EARLY)
         scale_table = shared.tile([P, T], U8, name="scale_table", offset=0, align_bytes=64)
-
         word_table = keep.tile([P, T], I32, name="word_table", align_bytes=64)
         x_rows = x_words[0].rearrange("p n t -> p (n t)").bitcast(I32)
         nc.sync.dma_start(word_table[:, :X_FIRST], x_rows[:, :X_FIRST])
@@ -57,56 +49,47 @@ def tile_picked_phpq_relu_p_kernel(tc, x_words, x_scales, w1, w2_words, w2_scale
         w1_rows = w1.rearrange("(p j) c -> p j c", j=PACK)
         w1_raw = keep.tile([P, PACK, H], F32, name="w1_raw", tag="w1_raw", align_bytes=64)
         nc.sync.dma_start(w1_raw[:], w1_rows)
-        nc.sync.dma_start(word_table[:, X_FIRST:], x_rows[:, X_FIRST:])
-        w2_codes = keep.tile([P, 2 * N], U8, name="w2_codes", align_bytes=64)
-        nc.sync.dma_start(w2_codes[:].bitcast(I32), w2_words[0].bitcast(I32))
 
-        w2_plane = keep.tile([P, N], U8, name="w2_plane", align_bytes=64)
-        nc.vector.memset(w2_plane[:].bitcast(I32), 0)
-        for q in range(4):
-            nc.gpsimd.dma_start(w2_plane[32 * q : 32 * q + 4, :].bitcast(I32), w2_scales[0, 4 * q : 4 * q + 4, :].bitcast(I32))
+        w2_rows = keep.tile([P, PACK, N // 4], I32, name="w2_rows", align_bytes=64)
+        nc.vector.memset(w2_rows[:, 0, :], 0)
+        nc.sync.dma_start(w2_rows[0:4], w2_scales[0].bitcast(I32).rearrange("(q r) n -> r q n", r=4))
+        w2_plane = w2_rows[:, 0, :].bitcast(U8)
+        nc.sync.dma_start(word_table[:, X_FIRST:], x_rows[:, X_FIRST:])
 
         zeros = keep.tile([P, 16], F32, name="zeros")
         zero_bias = zeros[:, 8:9]
         nc.vector.memset(zeros[:, 0:1], 0.0)
         nc.scalar.activation(zero_bias, zeros[:, 0:1], RELU)
 
-        pos_rows = pos.rearrange("(p t) s -> p t s", t=PACK)
-        pos_chunk = {}
-
-        def load_pos(loads, name, offset):
-            first = loads[0][0]
-            total = sum(width for start, width in loads)
-            flat = shared.tile([P, PACK * total], F32, name=name, offset=offset, align_bytes=64)
-            for start, width in loads:
-                rows = flat[:, PACK * (start - first) : PACK * (start - first + width)].rearrange("p (t n) -> p t n", t=PACK)
-                nc.sync.dma_start(rows, pos_rows[:, :, start : start + width])
-                for c0 in range(0, width, CHUNK):
-                    pos_chunk[(start + c0) // CHUNK] = rows[:, :, c0 : c0 + CHUNK]
-
         x_plane = keep.tile([P, S], U8, name="x_plane", align_bytes=64)
         nc.vector.memset(x_plane[:].bitcast(I32), 0)
+        early_bytes = 2 * N + 4 * PACK * 3 * PAIR
         picked = shared.tile([P, S], U8, name="picked", offset=early_bytes, align_bytes=64)
         nc.vector.tensor_copy(picked[:], scale_table[:].indirect(offsets[:]))
         for r in range(4):
             nc.sync.dma_start(x_plane[r:P:32, :].bitcast(I32), picked[8 * r : P : 32, :].bitcast(I32))
 
-        load_pos(POS_EARLY, "pos_early", 0)
+        pos_rows = pos.rearrange("(p t) s -> p t s", t=PACK)
+        pos_chunk = {}
 
-        x_chunk = {}
-
-        def gather_words(g, pool, **place):
-            start, width = GATHERS[g]
-            words = pool.tile([P, width], U32, name="x_codes%d" % g, align_bytes=64, **place)
-            entries = offsets[:, start // LIST_ROWS : (start + width) // LIST_ROWS]
-            nc.vector.tensor_copy(words[:], word_table[:].bitcast(U32).indirect(entries))
+        def load_pos(flat, first, start, width):
+            rows = flat[:, PACK * (start - first) : PACK * (start - first + width)].rearrange("p (t n) -> p t n", t=PACK)
+            nc.sync.dma_start(rows, pos_rows[:, :, start : start + width])
             for c0 in range(0, width, CHUNK):
-                x_chunk[(start + c0) // CHUNK] = words[:, c0 : c0 + CHUNK]
-            return words
+                pos_chunk[(start + c0) // CHUNK] = rows[:, :, c0 : c0 + CHUNK]
 
+        pos_early = shared.tile([P, PACK * 3 * PAIR], F32, name="pos_early", offset=2 * N, align_bytes=64)
+        w2_codes = shared.tile([P, 2 * N], U8, name="w2_codes", offset=0, align_bytes=64)
+        load_pos(pos_early, 0, 0, PAIR)
+        load_pos(pos_early, 0, PAIR, PAIR)
+        nc.sync.dma_start(w2_codes[:].bitcast(I32), w2_words[0].bitcast(I32))
+        load_pos(pos_early, 0, 2 * PAIR, PAIR)
+        pos_late = shared.tile([P, PACK * PAIR], F32, name="pos_late", offset=early_bytes, align_bytes=64)
+        load_pos(pos_late, 3 * PAIR, 3 * PAIR, CHUNK)
+        load_pos(pos_late, 3 * PAIR, 3 * PAIR + CHUNK, CHUNK)
 
         w1_grouped = [
-            keep.tile([P, 2, P, PACK], BF16, name="w1_grouped%d" % pair, tag="w1_grouped%d" % pair, align_bytes=64)
+            keep.tile([P, 2, P, PACK], BF16, name="w1_grouped%d" % pair, align_bytes=64)
             for pair in range(2)
         ]
         cast_out = [grouped[:].rearrange("p t m j -> p m j t") for grouped in w1_grouped]
@@ -120,44 +103,37 @@ def tile_picked_phpq_relu_p_kernel(tc, x_words, x_scales, w1, w2_words, w2_scale
             keep.tile([P, 2, P], U32, name="w1_codes1", tag="w1_raw", align_bytes=64),
         ]
         w1_plane = keep.tile([P, PACK, P], U8, name="w1_plane", align_bytes=64)
-        for t in range(0, PACK, 2):
+        for pair in range(2):
             nc.vector.quantize_mx(
-                out=w1_pairs[t // 2][:].rearrange("p t m -> p (t m)").bitcast(FP8X4),
-                scales=w1_plane[:, t : t + 2, :].rearrange("p t m -> p (t m)"),
-                in_=w1_grouped[t // 2][:].rearrange("p t m j -> p (t m j)"),
+                out=w1_pairs[pair][:].rearrange("p t m -> p (t m)").bitcast(FP8X4),
+                scales=w1_plane[:, 2 * pair : 2 * pair + 2, :].rearrange("p t m -> p (t m)"),
+                in_=w1_grouped[pair][:].rearrange("p t m j -> p (t m j)"),
             )
+        for q in range(1, 4):
+            nc.vector.tensor_copy(w2_rows[32 * q : 32 * q + 4, 0, :], w2_rows[0:4, q, :])
 
-        load_pos(POS_LATE, "pos_late", early_bytes)
+        x_chunk = {}
 
-        gather_words(0, keep)
-        gather_words(1, keep)
+        def gather_words(g, tag):
+            words = keep.tile([P, PAIR], U32, name="x_codes%d" % g, tag=tag, align_bytes=64)
+            entries = offsets[:, g * PAIR // LIST_ROWS : (g + 1) * PAIR // LIST_ROWS]
+            nc.vector.tensor_copy(words[:], word_table[:].bitcast(U32).indirect(entries))
+            x_chunk[2 * g] = words[:, :CHUNK]
+            x_chunk[2 * g + 1] = words[:, CHUNK:]
 
         out_rows = out.rearrange("(u p) s -> p u s", p=P)
-        sum_bytes = 2 * CHUNK * PACK
-        sum_at = {0: 0, 1: 2, 2: 4, 3: 6, 4: 2, 5: 9, 6: 6, 7: 8}
+        slot_bytes = 2 * CHUNK * PACK
+        banks = {}
         summed = {}
-        h_group = {}
-        h_chunk = {}
 
-        def rectified_tile(d):
-            first_chunk, count = GROUPS[d]
-            if first_chunk == 6:
-                hidden = sums.tile([P, count, CHUNK * PACK], BF16, name="hidden6", offset=10 * sum_bytes // 2, align_bytes=64)
-            else:
-                hidden = keep.tile([P, count, CHUNK * PACK], BF16, name="hidden%d" % first_chunk, tag="h_codes0" if first_chunk == 4 else "hidden%d" % first_chunk, align_bytes=64)
-            h_group[d] = hidden[:].rearrange("p a n -> p (a n)")
-            for a in range(count):
-                h_chunk[first_chunk + a] = hidden[:, a, :]
-
-        def woven(flat, run=WEAVE):
+        def woven(flat, run):
             return flat.rearrange("p (c i t) -> p c t i", i=run, t=PACK)
 
-        def side_by_side(rows, run=WEAVE):
+        def side_by_side(rows, run):
             return rows.rearrange("p t (c i) -> p c t i", i=run)
 
-        def first_layer(c):
-            summed[c] = sums.tile([P, CHUNK * PACK], BF16, name="summed%d" % c, offset=sum_at[c] * sum_bytes // 2, align_bytes=64)
-            bank = psum.tile([P, PACK, CHUNK], F32, name="h_bank", tag="bank%d" % (c % H_BANKS))
+        def products(c):
+            bank = psum.tile([P, PACK, CHUNK], F32, name="h_bank%d" % c, tag="bank%d" % H_BANK[c])
             for t in range(PACK):
                 nc.tensor.matmul_mx(
                     out=bank[:, t, :],
@@ -168,46 +144,45 @@ def tile_picked_phpq_relu_p_kernel(tc, x_words, x_scales, w1, w2_words, w2_scale
                     start=True,
                     stop=True,
                 )
-            if c < FIRST_ON_VECTOR:
-                rows = summed[c][:].rearrange("p (t n) -> p t n", t=PACK)
-                nc.vector.tensor_tensor(rows, bank[:], pos_chunk[c], ADD)
-                nc.scalar.activation(woven(h_chunk[c]), side_by_side(rows), RELU, bias=zero_bias)
-            else:
-                nc.vector.tensor_tensor(woven(summed[c][:], WEAVE_ADD), side_by_side(bank[:], WEAVE_ADD), side_by_side(pos_chunk[c], WEAVE_ADD), ADD)
+            banks[c] = bank
 
-        def relu_on_vector(c):
-            nc.vector.tensor_scalar(h_chunk[c], summed[c][:], 0.0, None, MAX)
+        def sum_tile(c, slot):
+            summed[c] = sums.tile([P, CHUNK * PACK], BF16, name="summed%d" % c, offset=slot * slot_bytes, align_bytes=64)
+            return summed[c][:]
 
-        h_mx = {}
+        def add_on_gpsimd(c, slot):
+            emptied = keep.tile([P, PACK, CHUNK], F32, name="emptied%d" % c, tag="emptied", align_bytes=64)
+            nc.scalar.copy(emptied[:], banks[c][:])
+            nc.gpsimd.tensor_tensor(sum_tile(c, slot).rearrange("p (t n) -> p t n", t=PACK), emptied[:], pos_chunk[c], ADD)
 
-        def quantise(d):
-            width = GROUPS[d][1] * CHUNK
-            codes = keep.tile([P, width], U32, name="h_codes%d" % d, tag="h_codes%d" % d, align_bytes=64)
-            plane = keep.tile([P, width], U8, name="h_plane%d" % d, align_bytes=64)
-            nc.vector.quantize_mx(out=codes[:].bitcast(FP8X4), scales=plane[:], in_=h_group[d])
-            h_mx[d] = (codes, plane)
+        def add_plain(c, slot):
+            nc.vector.tensor_tensor(sum_tile(c, slot).rearrange("p (t n) -> p t n", t=PACK), banks[c][:], pos_chunk[c], ADD)
 
-        first_result = []
+        def add_woven(c, slot):
+            nc.vector.tensor_tensor(woven(sum_tile(c, slot), WEAVE_ADD), side_by_side(banks[c][:], WEAVE_ADD), side_by_side(pos_chunk[c], WEAVE_ADD), ADD)
 
-        def first_result_half(u):
-            width = GROUPS[0][1] * CHUNK
-            half = keep.tile([P, width], F32, name="result0_%d" % u, tag="hidden2" if u else "result0", align_bytes=64)
-            nc.scalar.copy(half[:], first_result[u])
-            nc.sync.dma_start(out_rows[:, u, :width], half[:])
+        def relu_on_scalar(c, hidden):
+            rows = summed[c][:].rearrange("p (t n) -> p t n", t=PACK)
+            nc.scalar.activation(woven(hidden, WEAVE), side_by_side(rows, WEAVE), RELU, bias=zero_bias)
 
-        def second_layer(d):
-            start, width = GROUPS[d][0] * CHUNK, GROUPS[d][1] * CHUNK
-            codes, plane = h_mx[d]
-            bank = psum.tile([P, N // P, width], F32, name="out_bank", tag="bank%d" % (H_BANKS + d))
-            last = d == len(GROUPS) - 1
-            other = bank
-            if last:
-                other = psum.tile([P, N // P, width], F32, name="other_bank", tag="bank0")
-            if d == 0:
-                other = psum.tile([P, N // P, width], F32, name="other_bank", tag="bank6")
+        def relu_on_vector(c, hidden):
+            nc.vector.tensor_scalar(hidden, summed[c][:], 0.0, None, MAX)
+
+        def quantise(name, hidden):
+            width = hidden.shape[1] // PACK
+            codes = keep.tile([P, width], U32, name="h_codes" + name, tag="h_codes" + name, align_bytes=64)
+            plane = keep.tile([P, width], U8, name="h_plane" + name, align_bytes=64)
+            nc.vector.quantize_mx(out=codes[:].bitcast(FP8X4), scales=plane[:], in_=hidden)
+            return codes, plane
+
+        def second_layer(quantised, tags):
+            codes, plane = quantised
+            width = codes.shape[1]
+            tiles = [psum.tile([P, N // P, width], F32, name="out_" + tag, tag=tag) for tag in tags]
+            halves = [tiles[u % len(tiles)][:, u, :] for u in range(N // P)]
             for u in range(N // P):
                 nc.tensor.matmul_mx(
-                    out=(other if u == 0 else bank)[:, u, :],
+                    out=halves[u],
                     lhsT=w2_codes[:, 2 * P * u : 2 * P * (u + 1)].bitcast(FP4X4),
                     lhsT_scale=w2_plane[:, P * u : P * (u + 1)],
                     rhs=codes[:].bitcast(FP8X4),
@@ -215,42 +190,58 @@ def tile_picked_phpq_relu_p_kernel(tc, x_words, x_scales, w1, w2_words, w2_scale
                     start=True,
                     stop=True,
                 )
-            if d == 0:
-                first_result.extend([other[:, 0, :], bank[:, 1, :]])
-                return
-            else:
-                result = keep.tile([P, N // P, width], F32, name="result%d" % d, align_bytes=64)
-            if d == len(GROUPS) - 1:
-                nc.vector.tensor_copy(result[:, 0, :], other[:, 0, :])
-                nc.scalar.copy(result[:, 1, :], bank[:, 1, :])
-            else:
-                nc.scalar.copy(result[:], bank[:])
-            nc.sync.dma_start(out_rows[:, :, start : start + width], result[:])
+            return tiles
 
-        rectified_tile(0)
-        rectified_tile(1)
-        first_layer(0)
-        first_layer(1)
-        gather_words(2, sums, offset=0)
-        first_layer(2)
-        first_layer(3)
-        quantise(0)
-        second_layer(0)
-        first_result_half(0)
-        for d in range(2, len(GROUPS)):
-            rectified_tile(d)
-        first_layer(4)
-        first_layer(5)
-        quantise(1)
-        first_result_half(1)
-        second_layer(1)
-        first_layer(6)
-        quantise(2)
-        relu_on_vector(6)
-        second_layer(2)
-        first_layer(7)
-        quantise(3)
-        relu_on_vector(7)
-        second_layer(3)
-        quantise(4)
-        second_layer(4)
+        def store(bank, first_chunk):
+            width = bank.shape[2]
+            result = keep.tile([P, N // P, width], F32, name="result%d" % first_chunk, align_bytes=64)
+            nc.scalar.copy(result[:], bank[:])
+            nc.sync.dma_start(out_rows[:, :, first_chunk * CHUNK : first_chunk * CHUNK + width], result[:])
+
+        half = CHUNK * PACK
+        hidden01 = keep.tile([P, 2 * half], BF16, name="hidden01", align_bytes=64)
+
+        gather_words(0, "x_first")
+        gather_words(1, "x_second")
+        gather_words(2, "x_third")
+        products(0)
+        products(1)
+        add_on_gpsimd(0, 0)
+        add_plain(1, 1)
+        relu_on_scalar(1, hidden01[:, half:])
+        relu_on_scalar(0, hidden01[:, :half])
+        gather_words(3, "x_first")
+        products(2)
+        products(3)
+        products(4)
+        hidden23 = keep.tile([P, 2 * half], BF16, name="hidden23", tag="emptied", align_bytes=64)
+        add_plain(2, 2)
+        relu_on_scalar(2, hidden23[:, :half])
+        add_plain(3, 3)
+        relu_on_scalar(3, hidden23[:, half:])
+        products(5)
+        store(second_layer(quantise("01", hidden01[:]), ["bank0"])[0], 0)
+        hidden45 = keep.tile([P, 2 * half], BF16, name="hidden45", tag="h_codes01", align_bytes=64)
+        add_plain(4, 0)
+        relu_on_scalar(4, hidden45[:, :half])
+        products(6)
+        add_plain(5, 5)
+        relu_on_scalar(5, hidden45[:, half:])
+        products(7)
+        store(second_layer(quantise("23", hidden23[:]), ["bank1"])[0], 2)
+        add_woven(6, 3)
+        group45 = quantise("45", hidden45[:])
+        hidden6 = sums.tile([P, half], BF16, name="hidden6", offset=5 * slot_bytes + slot_bytes // 2, align_bytes=64)
+        relu_on_vector(6, hidden6[:])
+        store(second_layer(group45, ["bank4"])[0], 4)
+        summed[7] = sums.tile([P, half], BF16, name="summed7", offset=4 * slot_bytes + slot_bytes // 2, align_bytes=64)
+        nc.vector.tensor_tensor(woven(summed[7][:], WEAVE_ADD), side_by_side(banks[7][:], WEAVE_ADD), side_by_side(pos_chunk[7], WEAVE_ADD), ADD)
+        group6 = quantise("6", hidden6[:])
+        hidden7 = keep.tile([P, half], BF16, name="hidden7", align_bytes=64)
+        relu_on_vector(7, hidden7[:])
+        store(second_layer(group6, ["bank5"])[0], 6)
+        last = second_layer(quantise("7", hidden7[:]), ["bank6", "bank7"])
+        result = keep.tile([P, N // P, CHUNK], F32, name="result7", align_bytes=64)
+        nc.vector.tensor_copy(result[:, 0, :], last[0][:, 0, :])
+        nc.scalar.copy(result[:, 1, :], last[1][:, 1, :])
+        nc.sync.dma_start(out_rows[:, :, 7 * CHUNK :], result[:])

@@ -26,7 +26,7 @@ PAIR = 2 * CHUNK
 WEAVE = 4
 WEAVE_ADD = 2
 X_FIRST = 256
-ON_SCALAR = (108, 40)
+ON_SCALAR = 84
 H_BANK = (0, 1, 2, 3, 4, 2, 3, 2)
 
 
@@ -36,6 +36,7 @@ def tile_picked_phpq_relu_p_kernel(tc, x_words, x_scales, w1, w2_words, w2_scale
         keep = ctx.enter_context(tc.tile_pool(name="keep", bufs=1))
         shared = ctx.enter_context(tc.tile_pool(name="shared", bufs=1))
         sums = ctx.enter_context(tc.tile_pool(name="sums", bufs=1))
+        head = ctx.enter_context(tc.tile_pool(name="head", bufs=1))
         psum = ctx.enter_context(tc.psum_pool(name="psum", bufs=1))
 
         scale_table = shared.tile([P, T], U8, name="scale_table", offset=0, align_bytes=64)
@@ -46,15 +47,14 @@ def tile_picked_phpq_relu_p_kernel(tc, x_words, x_scales, w1, w2_words, w2_scale
         nc.sync.dma_start(offsets[:], offs)
         nc.vector.memset(scale_table[:].bitcast(I32), 0)
         nc.sync.dma_start(scale_table[0:P:8, :].bitcast(I32), x_scales[0].bitcast(I32))
-        w1_rows = w1.rearrange("(p j) c -> p j c", j=PACK)
-        w1_raw = keep.tile([P, PACK, H], F32, name="w1_raw", tag="w1_raw", align_bytes=64)
-        nc.sync.dma_start(w1_raw[:], w1_rows)
-
-        w2_rows = keep.tile([P, PACK, N // 4], I32, name="w2_rows", align_bytes=64)
-        nc.vector.memset(w2_rows[:, 0, :], 0)
-        nc.sync.dma_start(w2_rows[0:4], w2_scales[0].bitcast(I32).rearrange("(q r) n -> r q n", r=4))
-        w2_plane = w2_rows[:, 0, :].bitcast(U8)
         nc.sync.dma_start(word_table[:, X_FIRST:], x_rows[:, X_FIRST:])
+        w2_plane = keep.tile([P, N], U8, name="w2_plane", align_bytes=64)
+        nc.vector.memset(w2_plane[:].bitcast(I32), 0)
+        for q in range(4):
+            nc.gpsimd.dma_start(w2_plane[32 * q : 32 * q + 4, :].bitcast(I32), w2_scales[0, 4 * q : 4 * q + 4, :].bitcast(I32))
+        w1_rows = w1.rearrange("(p j) c -> p j c", j=PACK)
+        w1_raw = head.tile([P, PACK, H], F32, name="w1_raw", offset=0, align_bytes=64)
+        nc.sync.dma_start(w1_raw[:], w1_rows)
 
         zeros = keep.tile([P, 16], F32, name="zeros")
         zero_bias = zeros[:, 8:9]
@@ -88,19 +88,29 @@ def tile_picked_phpq_relu_p_kernel(tc, x_words, x_scales, w1, w2_words, w2_scale
         load_pos(pos_late, 3 * PAIR, 3 * PAIR, CHUNK)
         load_pos(pos_late, 3 * PAIR, 3 * PAIR + CHUNK, CHUNK)
 
+        x_chunk = {}
+
+        def gather_words(first_chunk, count, pool, **place):
+            words = pool.tile([P, count * CHUNK], U32, name="x_codes%d" % first_chunk, align_bytes=64, **place)
+            entries = offsets[:, first_chunk * CHUNK // LIST_ROWS : (first_chunk + count) * CHUNK // LIST_ROWS]
+            nc.vector.tensor_copy(words[:], word_table[:].bitcast(U32).indirect(entries))
+            for a in range(count):
+                x_chunk[first_chunk + a] = words[:, a * CHUNK : (a + 1) * CHUNK]
+
+        gather_words(0, 6, keep)
+
         w1_grouped = [
             keep.tile([P, 2, P, PACK], BF16, name="w1_grouped%d" % pair, align_bytes=64)
             for pair in range(2)
         ]
         cast_out = [grouped[:].rearrange("p t m j -> p m j t") for grouped in w1_grouped]
         cast_in = w1_raw[:].rearrange("p j (m t) -> p m j t", t=PACK)
-        for pair in range(2):
-            tiles = slice(2 * pair, 2 * pair + 2)
-            nc.scalar.activation(cast_out[pair][:, : ON_SCALAR[pair]], cast_in[:, : ON_SCALAR[pair], :, tiles], COPY)
-            nc.vector.tensor_copy(cast_out[pair][:, ON_SCALAR[pair] :], cast_in[:, ON_SCALAR[pair] :, :, tiles])
+        nc.scalar.activation(cast_out[0][:, :ON_SCALAR], cast_in[:, :ON_SCALAR, :, 0:2], COPY)
+        nc.vector.tensor_copy(cast_out[0][:, ON_SCALAR:], cast_in[:, ON_SCALAR:, :, 0:2])
+        nc.vector.tensor_copy(cast_out[1], cast_in[:, :, :, 2:4])
         w1_pairs = [
             keep.tile([P, 2, P], U32, name="w1_codes0", align_bytes=64),
-            keep.tile([P, 2, P], U32, name="w1_codes1", tag="w1_raw", align_bytes=64),
+            head.tile([P, 2, P], U32, name="w1_codes1", offset=0, align_bytes=64),
         ]
         w1_plane = keep.tile([P, PACK, P], U8, name="w1_plane", align_bytes=64)
         for pair in range(2):
@@ -109,17 +119,7 @@ def tile_picked_phpq_relu_p_kernel(tc, x_words, x_scales, w1, w2_words, w2_scale
                 scales=w1_plane[:, 2 * pair : 2 * pair + 2, :].rearrange("p t m -> p (t m)"),
                 in_=w1_grouped[pair][:].rearrange("p t m j -> p (t m j)"),
             )
-        for q in range(1, 4):
-            nc.vector.tensor_copy(w2_rows[32 * q : 32 * q + 4, 0, :], w2_rows[0:4, q, :])
-
-        x_chunk = {}
-
-        def gather_words(g, tag):
-            words = keep.tile([P, PAIR], U32, name="x_codes%d" % g, tag=tag, align_bytes=64)
-            entries = offsets[:, g * PAIR // LIST_ROWS : (g + 1) * PAIR // LIST_ROWS]
-            nc.vector.tensor_copy(words[:], word_table[:].bitcast(U32).indirect(entries))
-            x_chunk[2 * g] = words[:, :CHUNK]
-            x_chunk[2 * g + 1] = words[:, CHUNK:]
+        gather_words(6, 2, head, offset=2048)
 
         out_rows = out.rearrange("(u p) s -> p u s", p=P)
         slot_bytes = 2 * CHUNK * PACK
@@ -149,11 +149,6 @@ def tile_picked_phpq_relu_p_kernel(tc, x_words, x_scales, w1, w2_words, w2_scale
         def sum_tile(c, slot):
             summed[c] = sums.tile([P, CHUNK * PACK], BF16, name="summed%d" % c, offset=slot * slot_bytes, align_bytes=64)
             return summed[c][:]
-
-        def add_on_gpsimd(c, slot):
-            emptied = keep.tile([P, PACK, CHUNK], F32, name="emptied%d" % c, tag="emptied", align_bytes=64)
-            nc.scalar.copy(emptied[:], banks[c][:])
-            nc.gpsimd.tensor_tensor(sum_tile(c, slot).rearrange("p (t n) -> p t n", t=PACK), emptied[:], pos_chunk[c], ADD)
 
         def add_plain(c, slot):
             nc.vector.tensor_tensor(sum_tile(c, slot).rearrange("p (t n) -> p t n", t=PACK), banks[c][:], pos_chunk[c], ADD)
@@ -201,20 +196,16 @@ def tile_picked_phpq_relu_p_kernel(tc, x_words, x_scales, w1, w2_words, w2_scale
         half = CHUNK * PACK
         hidden01 = keep.tile([P, 2 * half], BF16, name="hidden01", align_bytes=64)
 
-        gather_words(0, "x_first")
-        gather_words(1, "x_second")
-        gather_words(2, "x_third")
+        hidden23 = keep.tile([P, 2 * half], BF16, name="hidden23", align_bytes=64)
         products(0)
         products(1)
-        add_on_gpsimd(0, 0)
+        add_plain(0, 0)
+        relu_on_scalar(0, hidden01[:, :half])
         add_plain(1, 1)
         relu_on_scalar(1, hidden01[:, half:])
-        relu_on_scalar(0, hidden01[:, :half])
-        gather_words(3, "x_first")
         products(2)
         products(3)
         products(4)
-        hidden23 = keep.tile([P, 2 * half], BF16, name="hidden23", tag="emptied", align_bytes=64)
         add_plain(2, 2)
         relu_on_scalar(2, hidden23[:, :half])
         add_plain(3, 3)
@@ -222,19 +213,20 @@ def tile_picked_phpq_relu_p_kernel(tc, x_words, x_scales, w1, w2_words, w2_scale
         products(5)
         store(second_layer(quantise("01", hidden01[:]), ["bank0"])[0], 0)
         hidden45 = keep.tile([P, 2 * half], BF16, name="hidden45", tag="h_codes01", align_bytes=64)
-        add_plain(4, 0)
+        add_plain(4, 1)
         relu_on_scalar(4, hidden45[:, :half])
         products(6)
-        add_plain(5, 5)
-        relu_on_scalar(5, hidden45[:, half:])
+        add_woven(5, 5)
         products(7)
-        store(second_layer(quantise("23", hidden23[:]), ["bank1"])[0], 2)
+        group23 = quantise("23", hidden23[:])
+        relu_on_vector(5, hidden45[:, half:])
+        store(second_layer(group23, ["bank1"])[0], 2)
         add_woven(6, 3)
         group45 = quantise("45", hidden45[:])
-        hidden6 = sums.tile([P, half], BF16, name="hidden6", offset=5 * slot_bytes + slot_bytes // 2, align_bytes=64)
+        hidden6 = sums.tile([P, half], BF16, name="hidden6", offset=slot_bytes + slot_bytes // 2, align_bytes=64)
         relu_on_vector(6, hidden6[:])
         store(second_layer(group45, ["bank4"])[0], 4)
-        summed[7] = sums.tile([P, half], BF16, name="summed7", offset=4 * slot_bytes + slot_bytes // 2, align_bytes=64)
+        summed[7] = sums.tile([P, half], BF16, name="summed7", offset=slot_bytes // 2, align_bytes=64)
         nc.vector.tensor_tensor(woven(summed[7][:], WEAVE_ADD), side_by_side(banks[7][:], WEAVE_ADD), side_by_side(pos_chunk[7], WEAVE_ADD), ADD)
         group6 = quantise("6", hidden6[:])
         hidden7 = keep.tile([P, half], BF16, name="hidden7", align_bytes=64)

@@ -26,7 +26,7 @@ PAIR = 2 * CHUNK
 WEAVE = 4
 WEAVE_ADD = 2
 X_FIRST = 256
-ON_SCALAR = 84
+ON_SCALAR = ((128, 56), (42, 82))
 H_BANK = (0, 1, 2, 3, 4, 2, 3, 2)
 
 
@@ -53,8 +53,12 @@ def tile_picked_phpq_relu_p_kernel(tc, x_words, x_scales, w1, w2_words, w2_scale
         for q in range(4):
             nc.gpsimd.dma_start(w2_plane[32 * q : 32 * q + 4, :].bitcast(I32), w2_scales[0, 4 * q : 4 * q + 4, :].bitcast(I32))
         w1_rows = w1.rearrange("(p j) c -> p j c", j=PACK)
-        w1_raw = head.tile([P, PACK, H], F32, name="w1_raw", offset=0, align_bytes=64)
-        nc.sync.dma_start(w1_raw[:], w1_rows)
+        w1_raw = [
+            keep.tile([P, 2, H], F32, name="w1_raw0", align_bytes=64),
+            head.tile([P, 2, H], F32, name="w1_raw1", offset=0, align_bytes=64),
+        ]
+        for rows in range(2):
+            nc.sync.dma_start(w1_raw[rows][:], w1_rows[:, 2 * rows : 2 * rows + 2, :])
 
         zeros = keep.tile([P, 16], F32, name="zeros")
         zero_bias = zeros[:, 8:9]
@@ -82,8 +86,8 @@ def tile_picked_phpq_relu_p_kernel(tc, x_words, x_scales, w1, w2_words, w2_scale
         w2_codes = shared.tile([P, 2 * N], U8, name="w2_codes", offset=0, align_bytes=64)
         load_pos(pos_early, 0, 0, PAIR)
         load_pos(pos_early, 0, PAIR, PAIR)
-        nc.sync.dma_start(w2_codes[:].bitcast(I32), w2_words[0].bitcast(I32))
         load_pos(pos_early, 0, 2 * PAIR, PAIR)
+        nc.sync.dma_start(w2_codes[:].bitcast(I32), w2_words[0].bitcast(I32))
         pos_late = shared.tile([P, PACK * PAIR], F32, name="pos_late", offset=early_bytes, align_bytes=64)
         load_pos(pos_late, 3 * PAIR, 3 * PAIR, CHUNK)
         load_pos(pos_late, 3 * PAIR, 3 * PAIR + CHUNK, CHUNK)
@@ -104,10 +108,15 @@ def tile_picked_phpq_relu_p_kernel(tc, x_words, x_scales, w1, w2_words, w2_scale
             for pair in range(2)
         ]
         cast_out = [grouped[:].rearrange("p t m j -> p m j t") for grouped in w1_grouped]
-        cast_in = w1_raw[:].rearrange("p j (m t) -> p m j t", t=PACK)
-        nc.scalar.activation(cast_out[0][:, :ON_SCALAR], cast_in[:, :ON_SCALAR, :, 0:2], COPY)
-        nc.vector.tensor_copy(cast_out[0][:, ON_SCALAR:], cast_in[:, ON_SCALAR:, :, 0:2])
-        nc.vector.tensor_copy(cast_out[1], cast_in[:, :, :, 2:4])
+        for rows in range(2):
+            cast_in = w1_raw[rows][:].rearrange("p j (m t) -> p m j t", t=PACK)
+            for pair in range(2):
+                split = ON_SCALAR[rows][pair]
+                source = cast_in[:, :, :, 2 * pair : 2 * pair + 2]
+                target = cast_out[pair][:, :, 2 * rows : 2 * rows + 2, :]
+                nc.scalar.activation(target[:, :split], source[:, :split], COPY)
+                if split < P:
+                    nc.vector.tensor_copy(target[:, split:], source[:, split:])
         w1_pairs = [
             keep.tile([P, 2, P], U32, name="w1_codes0", align_bytes=64),
             head.tile([P, 2, P], U32, name="w1_codes1", offset=0, align_bytes=64),
@@ -134,7 +143,7 @@ def tile_picked_phpq_relu_p_kernel(tc, x_words, x_scales, w1, w2_words, w2_scale
 
         def products(c):
             bank = psum.tile([P, PACK, CHUNK], F32, name="h_bank%d" % c, tag="bank%d" % H_BANK[c])
-            for t in range(PACK):
+            for t in (range(PACK) if c == 0 else (2, 3, 0, 1)):
                 nc.tensor.matmul_mx(
                     out=bank[:, t, :],
                     lhsT=w1_pairs[t // 2][:, t % 2, :].bitcast(FP8X4),
@@ -147,7 +156,7 @@ def tile_picked_phpq_relu_p_kernel(tc, x_words, x_scales, w1, w2_words, w2_scale
             banks[c] = bank
 
         def sum_tile(c, slot):
-            summed[c] = sums.tile([P, CHUNK * PACK], BF16, name="summed%d" % c, offset=slot * slot_bytes, align_bytes=64)
+            summed[c] = sums.tile([P, CHUNK * PACK], BF16, name="summed%d" % c, offset=slot * slot_bytes // 2, align_bytes=64)
             return summed[c][:]
 
         def add_plain(c, slot):
@@ -195,39 +204,37 @@ def tile_picked_phpq_relu_p_kernel(tc, x_words, x_scales, w1, w2_words, w2_scale
 
         half = CHUNK * PACK
         hidden01 = keep.tile([P, 2 * half], BF16, name="hidden01", align_bytes=64)
-
         hidden23 = keep.tile([P, 2 * half], BF16, name="hidden23", align_bytes=64)
         products(0)
         products(1)
         add_plain(0, 0)
         relu_on_scalar(0, hidden01[:, :half])
-        add_plain(1, 1)
+        add_plain(1, 6)
         relu_on_scalar(1, hidden01[:, half:])
         products(2)
         products(3)
         products(4)
         add_plain(2, 2)
         relu_on_scalar(2, hidden23[:, :half])
-        add_plain(3, 3)
+        add_plain(3, 10)
         relu_on_scalar(3, hidden23[:, half:])
         products(5)
         store(second_layer(quantise("01", hidden01[:]), ["bank0"])[0], 0)
         hidden45 = keep.tile([P, 2 * half], BF16, name="hidden45", tag="h_codes01", align_bytes=64)
-        add_plain(4, 1)
+        add_plain(4, 6)
         relu_on_scalar(4, hidden45[:, :half])
         products(6)
-        add_woven(5, 5)
+        add_woven(5, 12)
         products(7)
         group23 = quantise("23", hidden23[:])
         relu_on_vector(5, hidden45[:, half:])
         store(second_layer(group23, ["bank1"])[0], 2)
-        add_woven(6, 3)
+        add_woven(6, 10)
         group45 = quantise("45", hidden45[:])
-        hidden6 = sums.tile([P, half], BF16, name="hidden6", offset=slot_bytes + slot_bytes // 2, align_bytes=64)
+        hidden6 = sums.tile([P, half], BF16, name="hidden6", offset=7 * slot_bytes // 2, align_bytes=64)
         relu_on_vector(6, hidden6[:])
         store(second_layer(group45, ["bank4"])[0], 4)
-        summed[7] = sums.tile([P, half], BF16, name="summed7", offset=slot_bytes // 2, align_bytes=64)
-        nc.vector.tensor_tensor(woven(summed[7][:], WEAVE_ADD), side_by_side(banks[7][:], WEAVE_ADD), side_by_side(pos_chunk[7], WEAVE_ADD), ADD)
+        add_woven(7, 5)
         group6 = quantise("6", hidden6[:])
         hidden7 = keep.tile([P, half], BF16, name="hidden7", align_bytes=64)
         relu_on_vector(7, hidden7[:])

@@ -27,7 +27,7 @@ WEAVE = 4
 WEAVE_ADD = 2
 X_FIRST = 256
 ON_SCALAR = ((128, 56), (42, 82))
-H_BANK = (0, 1, 2, 3, 4, 2, 3, 2)
+H_BANK = (0, 1, 2, 3, 4, 5, 3, 5)
 
 
 def tile_picked_phpq_relu_p_kernel(tc, x_words, x_scales, w1, w2_words, w2_scales, pos, offs, out):
@@ -213,12 +213,12 @@ def tile_picked_phpq_relu_p_kernel(tc, x_words, x_scales, w1, w2_words, w2_scale
         relu_on_scalar(1, hidden01[:, half:])
         products(2)
         products(3)
+        products(5)
         products(4)
         add_plain(2, 2)
         relu_on_scalar(2, hidden23[:, :half])
         add_plain(3, 10)
         relu_on_scalar(3, hidden23[:, half:])
-        products(5)
         store(second_layer(quantise("01", hidden01[:]), ["bank0"])[0], 0)
         hidden45 = keep.tile([P, 2 * half], BF16, name="hidden45", tag="h_codes01", align_bytes=64)
         add_plain(4, 6)
@@ -233,14 +233,19 @@ def tile_picked_phpq_relu_p_kernel(tc, x_words, x_scales, w1, w2_words, w2_scale
         group45 = quantise("45", hidden45[:])
         hidden6 = sums.tile([P, half], BF16, name="hidden6", offset=7 * slot_bytes // 2, align_bytes=64)
         relu_on_vector(6, hidden6[:])
-        store(second_layer(group45, ["bank4"])[0], 4)
+        third = second_layer(group45, ["bank4", "bank0"])
+        for u in range(N // P):
+            result = keep.tile([P, PAIR], F32, name="result4_%d" % u, align_bytes=64)
+            nc.scalar.copy(result[:], third[u][:, u, :])
+            nc.sync.dma_start(out_rows[:, u, 2 * PAIR : 3 * PAIR], result[:])
         add_woven(7, 5)
         group6 = quantise("6", hidden6[:])
         hidden7 = keep.tile([P, half], BF16, name="hidden7", align_bytes=64)
         relu_on_vector(7, hidden7[:])
-        store(second_layer(group6, ["bank5"])[0], 6)
+        store(second_layer(group6, ["bank2"])[0], 6)
         last = second_layer(quantise("7", hidden7[:]), ["bank6", "bank7"])
         result = keep.tile([P, N // P, CHUNK], F32, name="result7", align_bytes=64)
         nc.vector.tensor_copy(result[:, 0, :], last[0][:, 0, :])
+        nc.sync.dma_start(out_rows[:, 0, 7 * CHUNK :], result[:, 0, :])
         nc.scalar.copy(result[:, 1, :], last[1][:, 1, :])
-        nc.sync.dma_start(out_rows[:, :, 7 * CHUNK :], result[:])
+        nc.sync.dma_start(out_rows[:, 1, 7 * CHUNK :], result[:, 1, :])

@@ -24,7 +24,7 @@ LIST_ROWS = 16
 CHUNK = 128
 PAIR = 2 * CHUNK
 WEAVE = 4
-WEAVE_ADD = 2
+WEAVE_ADD = 4
 X_FIRST = 256
 ON_SCALAR = ((128, 56), (42, 82))
 H_BANK = (0, 1, 2, 3, 4, 5, 3, 5)

from contextlib import ExitStack

import concourse.mybir as mybir

K, T, S, H, N = 512, 2048, 1024, 512, 256
FLOPS = 2 * K * H * S + 2 * H * N * S

F32 = mybir.dt.float32
BF16 = mybir.dt.bfloat16
I32 = mybir.dt.int32
U32 = mybir.dt.uint32
U16 = mybir.dt.uint16
U8 = mybir.dt.uint8
FP8X4 = mybir.dt.float8_e4m3fn_x4
FP4X4 = mybir.dt.float4_e2m1fn_x4
ADD = mybir.AluOpType.add
MAX = mybir.AluOpType.max
RELU = mybir.ActivationFunctionType.Relu
COPY = mybir.ActivationFunctionType.Copy

P = 128
PACK = 4
LIST_ROWS = 16
CHUNK = 128
PAIR = 2 * CHUNK
WEAVE = 4
WEAVE_ADD = 4
X_FIRST = 256
ON_SCALAR = ((128, 56), (42, 82))
H_BANK = (0, 1, 2, 3, 4, 5, 3, 5)


def tile_picked_phpq_relu_p_kernel(tc, x_words, x_scales, w1, w2_words, w2_scales, pos, offs, out):
    nc = tc.nc
    with ExitStack() as ctx:
        keep = ctx.enter_context(tc.tile_pool(name="keep", bufs=1))
        shared = ctx.enter_context(tc.tile_pool(name="shared", bufs=1))
        sums = ctx.enter_context(tc.tile_pool(name="sums", bufs=1))
        head = ctx.enter_context(tc.tile_pool(name="head", bufs=1))
        psum = ctx.enter_context(tc.psum_pool(name="psum", bufs=1))

        scale_table = shared.tile([P, T], U8, name="scale_table", offset=0, align_bytes=64)
        word_table = keep.tile([P, T], I32, name="word_table", align_bytes=64)
        x_rows = x_words[0].rearrange("p n t -> p (n t)").bitcast(I32)
        nc.sync.dma_start(word_table[:, :X_FIRST], x_rows[:, :X_FIRST])
        offsets = keep.tile([P, S // LIST_ROWS], U16, name="offsets")
        nc.sync.dma_start(offsets[:], offs)
        nc.vector.memset(scale_table[:].bitcast(I32), 0)
        nc.sync.dma_start(scale_table[0:P:8, :].bitcast(I32), x_scales[0].bitcast(I32))
        nc.sync.dma_start(word_table[:, X_FIRST:], x_rows[:, X_FIRST:])
        w2_plane = keep.tile([P, N], U8, name="w2_plane", align_bytes=64)
        nc.vector.memset(w2_plane[:].bitcast(I32), 0)
        for q in range(4):
            nc.gpsimd.dma_start(w2_plane[32 * q : 32 * q + 4, :].bitcast(I32), w2_scales[0, 4 * q : 4 * q + 4, :].bitcast(I32))
        w1_rows = w1.rearrange("(p j) c -> p j c", j=PACK)
        w1_raw = [
            keep.tile([P, 2, H], F32, name="w1_raw0", align_bytes=64),
            head.tile([P, 2, H], F32, name="w1_raw1", offset=0, align_bytes=64),
        ]
        for rows in range(2):
            nc.sync.dma_start(w1_raw[rows][:], w1_rows[:, 2 * rows : 2 * rows + 2, :])

        zeros = keep.tile([P, 16], F32, name="zeros")
        zero_bias = zeros[:, 8:9]
        nc.vector.memset(zeros[:, 0:1], 0.0)
        nc.scalar.activation(zero_bias, zeros[:, 0:1], RELU)

        x_plane = keep.tile([P, S], U8, name="x_plane", align_bytes=64)
        nc.vector.memset(x_plane[:].bitcast(I32), 0)
        early_bytes = 2 * N + 4 * PACK * 3 * PAIR
        picked = shared.tile([P, S], U8, name="picked", offset=early_bytes, align_bytes=64)
        nc.vector.tensor_copy(picked[:], scale_table[:].indirect(offsets[:]))
        for r in range(4):
            nc.sync.dma_start(x_plane[r:P:32, :].bitcast(I32), picked[8 * r : P : 32, :].bitcast(I32))

        pos_rows = pos.rearrange("(p t) s -> p t s", t=PACK)
        pos_chunk = {}

        def load_pos(flat, first, start, width):
            rows = flat[:, PACK * (start - first) : PACK * (start - first + width)].rearrange("p (t n) -> p t n", t=PACK)
            nc.sync.dma_start(rows, pos_rows[:, :, start : start + width])
            for c0 in range(0, width, CHUNK):
                pos_chunk[(start + c0) // CHUNK] = rows[:, :, c0 : c0 + CHUNK]

        pos_early = shared.tile([P, PACK * 3 * PAIR], F32, name="pos_early", offset=2 * N, align_bytes=64)
        w2_codes = shared.tile([P, 2 * N], U8, name="w2_codes", offset=0, align_bytes=64)
        load_pos(pos_early, 0, 0, PAIR)
        load_pos(pos_early, 0, PAIR, PAIR)
        load_pos(pos_early, 0, 2 * PAIR, PAIR)
        nc.sync.dma_start(w2_codes[:].bitcast(I32), w2_words[0].bitcast(I32))
        pos_late = shared.tile([P, PACK * PAIR], F32, name="pos_late", offset=early_bytes, align_bytes=64)
        load_pos(pos_late, 3 * PAIR, 3 * PAIR, CHUNK)
        load_pos(pos_late, 3 * PAIR, 3 * PAIR + CHUNK, CHUNK)

        x_chunk = {}

        def gather_words(first_chunk, count, pool, **place):
            words = pool.tile([P, count * CHUNK], U32, name="x_codes%d" % first_chunk, align_bytes=64, **place)
            entries = offsets[:, first_chunk * CHUNK // LIST_ROWS : (first_chunk + count) * CHUNK // LIST_ROWS]
            nc.vector.tensor_copy(words[:], word_table[:].bitcast(U32).indirect(entries))
            for a in range(count):
                x_chunk[first_chunk + a] = words[:, a * CHUNK : (a + 1) * CHUNK]

        gather_words(0, 6, keep)

        w1_grouped = [
            keep.tile([P, 2, P, PACK], BF16, name="w1_grouped%d" % pair, align_bytes=64)
            for pair in range(2)
        ]
        cast_out = [grouped[:].rearrange("p t m j -> p m j t") for grouped in w1_grouped]
        for rows in range(2):
            cast_in = w1_raw[rows][:].rearrange("p j (m t) -> p m j t", t=PACK)
            for pair in range(2):
                split = ON_SCALAR[rows][pair]
                source = cast_in[:, :, :, 2 * pair : 2 * pair + 2]
                target = cast_out[pair][:, :, 2 * rows : 2 * rows + 2, :]
                nc.scalar.activation(target[:, :split], source[:, :split], COPY)
                if split < P:
                    nc.vector.tensor_copy(target[:, split:], source[:, split:])
        w1_pairs = [
            keep.tile([P, 2, P], U32, name="w1_codes0", align_bytes=64),
            head.tile([P, 2, P], U32, name="w1_codes1", offset=0, align_bytes=64),
        ]
        w1_plane = keep.tile([P, PACK, P], U8, name="w1_plane", align_bytes=64)
        for pair in range(2):
            nc.vector.quantize_mx(
                out=w1_pairs[pair][:].rearrange("p t m -> p (t m)").bitcast(FP8X4),
                scales=w1_plane[:, 2 * pair : 2 * pair + 2, :].rearrange("p t m -> p (t m)"),
                in_=w1_grouped[pair][:].rearrange("p t m j -> p (t m j)"),
            )
        gather_words(6, 2, head, offset=2048)

        out_rows = out.rearrange("(u p) s -> p u s", p=P)
        slot_bytes = 2 * CHUNK * PACK
        banks = {}
        summed = {}

        def woven(flat, run):
            return flat.rearrange("p (c i t) -> p c t i", i=run, t=PACK)

        def side_by_side(rows, run):
            return rows.rearrange("p t (c i) -> p c t i", i=run)

        def products(c):
            bank = psum.tile([P, PACK, CHUNK], F32, name="h_bank%d" % c, tag="bank%d" % H_BANK[c])
            for t in (range(PACK) if c == 0 else (2, 3, 0, 1)):
                nc.tensor.matmul_mx(
                    out=bank[:, t, :],
                    lhsT=w1_pairs[t // 2][:, t % 2, :].bitcast(FP8X4),
                    lhsT_scale=w1_plane[:, t, :],
                    rhs=x_chunk[c].bitcast(FP8X4),
                    rhs_scale=x_plane[:, c * CHUNK : (c + 1) * CHUNK],
                    start=True,
                    stop=True,
                )
            banks[c] = bank

        def sum_tile(c, slot):
            summed[c] = sums.tile([P, CHUNK * PACK], BF16, name="summed%d" % c, offset=slot * slot_bytes // 2, align_bytes=64)
            return summed[c][:]

        def add_plain(c, slot):
            nc.vector.tensor_tensor(sum_tile(c, slot).rearrange("p (t n) -> p t n", t=PACK), banks[c][:], pos_chunk[c], ADD)

        def add_woven(c, slot):
            nc.vector.tensor_tensor(woven(sum_tile(c, slot), WEAVE_ADD), side_by_side(banks[c][:], WEAVE_ADD), side_by_side(pos_chunk[c], WEAVE_ADD), ADD)

        def relu_on_scalar(c, hidden):
            rows = summed[c][:].rearrange("p (t n) -> p t n", t=PACK)
            nc.scalar.activation(woven(hidden, WEAVE), side_by_side(rows, WEAVE), RELU, bias=zero_bias)

        def relu_on_vector(c, hidden):
            nc.vector.tensor_scalar(hidden, summed[c][:], 0.0, None, MAX)

        def quantise(name, hidden):
            width = hidden.shape[1] // PACK
            codes = keep.tile([P, width], U32, name="h_codes" + name, tag="h_codes" + name, align_bytes=64)
            plane = keep.tile([P, width], U8, name="h_plane" + name, align_bytes=64)
            nc.vector.quantize_mx(out=codes[:].bitcast(FP8X4), scales=plane[:], in_=hidden)
            return codes, plane

        def second_layer(quantised, tags):
            codes, plane = quantised
            width = codes.shape[1]
            tiles = [psum.tile([P, N // P, width], F32, name="out_" + tag, tag=tag) for tag in tags]
            halves = [tiles[u % len(tiles)][:, u, :] for u in range(N // P)]
            for u in range(N // P):
                nc.tensor.matmul_mx(
                    out=halves[u],
                    lhsT=w2_codes[:, 2 * P * u : 2 * P * (u + 1)].bitcast(FP4X4),
                    lhsT_scale=w2_plane[:, P * u : P * (u + 1)],
                    rhs=codes[:].bitcast(FP8X4),
                    rhs_scale=plane[:],
                    start=True,
                    stop=True,
                )
            return tiles

        def store(bank, first_chunk):
            width = bank.shape[2]
            result = keep.tile([P, N // P, width], F32, name="result%d" % first_chunk, align_bytes=64)
            nc.scalar.copy(result[:], bank[:])
            nc.sync.dma_start(out_rows[:, :, first_chunk * CHUNK : first_chunk * CHUNK + width], result[:])

        half = CHUNK * PACK
        hidden01 = keep.tile([P, 2 * half], BF16, name="hidden01", align_bytes=64)
        hidden23 = keep.tile([P, 2 * half], BF16, name="hidden23", align_bytes=64)
        products(0)
        products(1)
        add_plain(0, 0)
        relu_on_scalar(0, hidden01[:, :half])
        add_plain(1, 6)
        relu_on_scalar(1, hidden01[:, half:])
        products(2)
        products(3)
        products(5)
        products(4)
        add_plain(2, 2)
        relu_on_scalar(2, hidden23[:, :half])
        add_plain(3, 10)
        relu_on_scalar(3, hidden23[:, half:])
        store(second_layer(quantise("01", hidden01[:]), ["bank0"])[0], 0)
        hidden45 = keep.tile([P, 2 * half], BF16, name="hidden45", tag="h_codes01", align_bytes=64)
        add_plain(4, 6)
        relu_on_scalar(4, hidden45[:, :half])
        products(6)
        add_woven(5, 12)
        products(7)
        group23 = quantise("23", hidden23[:])
        relu_on_vector(5, hidden45[:, half:])
        store(second_layer(group23, ["bank1"])[0], 2)
        add_woven(6, 10)
        group45 = quantise("45", hidden45[:])
        hidden6 = sums.tile([P, half], BF16, name="hidden6", offset=7 * slot_bytes // 2, align_bytes=64)
        relu_on_vector(6, hidden6[:])
        third = second_layer(group45, ["bank4", "bank0"])
        for u in range(N // P):
            result = keep.tile([P, PAIR], F32, name="result4_%d" % u, align_bytes=64)
            nc.scalar.copy(result[:], third[u][:, u, :])
            nc.sync.dma_start(out_rows[:, u, 2 * PAIR : 3 * PAIR], result[:])
        add_woven(7, 5)
        group6 = quantise("6", hidden6[:])
        hidden7 = keep.tile([P, half], BF16, name="hidden7", align_bytes=64)
        relu_on_vector(7, hidden7[:])
        store(second_layer(group6, ["bank2"])[0], 6)
        last = second_layer(quantise("7", hidden7[:]), ["bank6", "bank7"])
        result = keep.tile([P, N // P, CHUNK], F32, name="result7", align_bytes=64)
        nc.vector.tensor_copy(result[:, 0, :], last[0][:, 0, :])
        nc.sync.dma_start(out_rows[:, 0, 7 * CHUNK :], result[:, 0, :])
        nc.scalar.copy(result[:, 1, :], last[1][:, 1, :])
        nc.sync.dma_start(out_rows[:, 1, 7 * CHUNK :], result[:, 1, :])
